import numpy as np
import ml_dtypes


def mxq(x, axis, fmt="e4m3"):
    dtype, down = {"e4m3": (ml_dtypes.float8_e4m3fn, 7), "e5m2": (ml_dtypes.float8_e5m2, 14)}[fmt]
    v = np.moveaxis(np.asarray(x, np.float32).astype(ml_dtypes.bfloat16).astype(np.float64), axis, -1)
    blocks = v.reshape(v.shape[:-1] + (-1, 32))
    amax = np.abs(blocks).max(-1, keepdims=True)
    byte = np.maximum(np.where(amax > 0, np.frexp(amax)[1] - 1 + 127, 0) - down, 1)
    scale = np.exp2(byte - 127.0)
    codes = (blocks / scale).astype(np.float32).astype(dtype).astype(np.float64)
    return np.moveaxis((codes * scale).reshape(v.shape), -1, axis)


WIDE = False


def mx_kscale(k):
    if not WIDE:
        return np.ones(k)
    levels = np.array([24, -24, 12, -12, 0])
    if k % 512:
        return np.exp2(np.random.permutation(np.resize(levels, k // 32))).repeat(32)
    a = np.empty((k // 512, 16))
    for p in range(k // 512):
        a[p, :8] = np.random.permutation(np.resize(levels, 8))
        for g in range(8):
            far = levels[np.abs(levels - a[p, g]) >= 10]
            a[p, g + 8] = far[np.random.randint(len(far))]
    return np.exp2(a.ravel()).repeat(32)


def f64(x):
    return np.asarray(x).astype(np.float64)


def striped(idx):
    return np.tile(idx.reshape(-1, 16).T, (8, 1)).astype(np.uint16)


def unstriped(offs):
    return offs[:16].T.reshape(-1).astype(np.int64)


E2M1 = np.array([0.0, 0.5, 1.0, 1.5, 2.0, 3.0, 4.0, 6.0, -0.0, -0.5, -1.0, -1.5, -2.0, -3.0, -4.0, -6.0])


def pack_weight(w, fmt):
    k, n = w.shape
    w = f64(np.asarray(w, np.float32).astype(ml_dtypes.bfloat16)).reshape(k // 32, 32, n)
    amax = np.abs(w).max(1)
    if fmt == "e4m3":
        byte = np.frexp(amax)[1] - 1 + 127 - 7
    else:
        mant, ex = np.frexp(amax / 6.0)
        byte = np.where(mant > 0.5, ex, ex - 1) + 127
    byte = np.clip(np.where(amax > 0, byte, 1), 1, 254)
    scaled = (w * np.exp2(127.0 - byte)[:, None, :]).reshape(k, n).astype(np.float32)
    by_word = np.ascontiguousarray(scaled.reshape(k // 512, 128, 4, n).transpose(0, 1, 3, 2))
    if fmt == "e4m3":
        words = by_word.astype(ml_dtypes.float8_e4m3fn).view(np.uint8)
    else:
        c = by_word.astype(ml_dtypes.float4_e2m1fn).view(np.uint8) & 0xF
        words = (c[..., 0::2] | (c[..., 1::2] << 4)).reshape(k // 512, 128, 2 * n)
    return np.ascontiguousarray(words), np.ascontiguousarray(byte.astype(np.uint8).reshape(k // 512, 16, n))


def unpack_weight(words, scales, fmt):
    g, _, n = scales.shape
    words = np.ascontiguousarray(words).reshape(g, 128, n, -1)
    if fmt == "e4m3":
        vals = words.view(ml_dtypes.float8_e4m3fn).astype(np.float64)
    else:
        nib = np.empty((g, 128, n, 4), np.uint8)
        nib[..., 0::2] = words & 0xF
        nib[..., 1::2] = words >> 4
        vals = E2M1[nib]
    vals = vals * np.repeat(np.exp2(scales.astype(np.float64) - 127.0), 8, axis=1)[..., None]
    return vals.transpose(0, 1, 3, 2).reshape(g * 512, n)


def pack_table4(v):
    words, scales = pack_weight(v, "e2m1")
    g, t = words.shape[0] // 2, v.shape[1]
    return np.ascontiguousarray(words.reshape(g, 2, 128, t, 2).transpose(0, 2, 3, 1, 4).reshape(g, 128, t, 4)), scales


def unpack_table4(words, scales):
    g, _, t, _ = words.shape
    return unpack_weight(words.reshape(g, 128, t, 2, 2).transpose(0, 3, 1, 2, 4).reshape(2 * g, 128, 2 * t), scales, "e2m1")


K, R, N, T, J = 1024, 1024, 512, 4096, 512


def setup_inputs():
    n = np.random.standard_normal
    s = mx_kscale(K)[:, None]
    u = mx_kscale(R)[:, None]
    wd = n((R, N)) / np.sqrt(R) / u
    p_tab = pack_table4(n((K, T)) * s)
    p_w = pack_weight(n((K, R)) / np.sqrt(K) / s * u.T, "e4m3")
    p_wd8 = pack_weight(wd[:512], "e4m3")
    p_wd4 = pack_weight(wd[512:], "e2m1")
    return {
        "tab_words": p_tab[0],
        "tab_scales": p_tab[1],
        "c": (n((K, J)) * s).astype(np.float32),
        "w_words": p_w[0],
        "w_scales": p_w[1],
        "wc": (n((K, R)) / np.sqrt(K) / s * u.T).astype(np.float32),
        "wd8_words": p_wd8[0],
        "wd8_scales": p_wd8[1],
        "wd4_words": p_wd4[0],
        "wd4_scales": p_wd4[1],
        "res": (n((N, J))).astype(np.float32),
        "offs": striped(np.concatenate([np.random.permutation(T)[:J] for _ in range(2)])),
    }


def reference(tab_words, tab_scales, c, w_words, w_scales, wc, wd8_words, wd8_scales, wd4_words, wd4_scales, res, offs):
    idx = unstriped(offs).reshape(2, J)
    tab_ = unpack_table4(tab_words, tab_scales)[:, idx]
    c_ = mxq(f64(c), 0, "e4m3")
    w_ = unpack_weight(w_words, w_scales, "e4m3")
    a0 = w_.T @ tab_[:, 0]
    a1 = w_.T @ tab_[:, 1]
    wc_ = mxq(f64(wc), 0, "e4m3")
    ac = wc_.T @ c_
    h = np.maximum(np.maximum(a0, a1) + ac, 0.0)
    h_ = mxq(h, 0, "e4m3")
    wd8_ = unpack_weight(wd8_words, wd8_scales, "e4m3")
    wd4_ = unpack_weight(wd4_words, wd4_scales, "e2m1")
    y = wd8_.T @ h_[:512] + wd4_.T @ h_[512:]
    return f64(res) + y

@@ -1,0 +1,312 @@
+from contextlib import ExitStack
+
+import concourse.mybir as mybir
+
+K, R, N, T, J = 1024, 1024, 512, 4096, 512
+FLOPS = 3758096384
+
+F32 = mybir.dt.float32
+BF16 = mybir.dt.bfloat16
+I32 = mybir.dt.int32
+U32 = mybir.dt.uint32
+U16 = mybir.dt.uint16
+U8 = mybir.dt.uint8
+FP8X4 = mybir.dt.float8_e4m3fn_x4
+FP4X4 = mybir.dt.float4_e2m1fn_x4
+ALU = mybir.AluOpType
+ACT = mybir.ActivationFunctionType
+
+P = 128
+PACK = 4
+PASS = P * PACK
+JT = 128
+NJT = J // JT
+SPLIT_M = 80
+PLAIN = 2
+W_AT = 2 * J
+WD_AT = W_AT + R
+ROW = WD_AT + N
+
+
+def tile_list_pnet_mix_res_kernel(
+    tc, tab_words, tab_scales, c, w_words, w_scales, wc, wd8_words, wd8_scales,
+    wd4_words, wd4_scales, res, offs, out,
+):
+    nc = tc.nc
+    with ExitStack() as ctx:
+        lists = ctx.enter_context(tc.tile_pool(name="lists", bufs=1))
+        keep = ctx.enter_context(tc.tile_pool(name="keep", bufs=1))
+        ring = ctx.enter_context(tc.tile_pool(name="ring", bufs=3))
+        psum = ctx.enter_context(tc.psum_pool(name="psum", bufs=2))
+
+        def held(shape, dtype, name, tag=None):
+            return keep.tile(shape, dtype, name=name, tag=tag or name, align_bytes=64)
+
+        offsets = lists.tile([P, 2 * J // 16], U16, name="offsets")
+        nc.sync.dma_start(offsets[:], offs)
+
+        tsc_win = held([P, T], U8, "tsc_win", "stage_a")
+        nc.sync.dma_start(tsc_win[0:32, :].bitcast(I32), tab_scales.rearrange("a q t -> q a t").bitcast(I32))
+        nc.vector.memset(tsc_win[32:64, :].bitcast(I32), 0)
+        nc.gpsimd.memset(tsc_win[64:128, :].bitcast(I32), 0)
+        wsc_raw = held([P, R], U8, "wsc_raw")
+        nc.sync.dma_start(wsc_raw[0:32, :].bitcast(I32), w_scales.rearrange("a q r -> q a r").bitcast(I32))
+        nc.vector.memset(wsc_raw[32:64, :].bitcast(I32), 0)
+        nc.vector.memset(wsc_raw[64:128, :].bitcast(I32), 0)
+        dense = held([P, ROW], U8, "dense", "stage_b")
+        for a, scales in enumerate((wd8_scales, wd4_scales)):
+            nc.sync.dma_start(dense[a:32:2, WD_AT:ROW].bitcast(I32), scales[0].bitcast(I32))
+        tab = held([P, T], U32, "tab", "stage_c")
+        nc.sync.dma_start(tab[:].bitcast(I32), tab_words[0].rearrange("p t b -> p (t b)").bitcast(I32))
+
+        w_flat = w_words.rearrange("a p r i -> p a (r i)")
+
+        def load_w(b, tag):
+            raw = held([P, 2, PASS], U32, "w_raw%d" % b, tag)
+            nc.sync.dma_start(raw[:].bitcast(I32), w_flat[:, :, 4 * PASS * b : 4 * PASS * (b + 1)].bitcast(I32))
+            return raw
+
+        def load_c(a, tag):
+            raw = held([P, PACK, J], F32, "c_raw%d" % a, tag)
+            nc.sync.dma_start(raw[:], c[PASS * a : PASS * (a + 1), :].rearrange("(p i) j -> p i j", i=PACK))
+            return raw
+
+        def load_wc(raw, b, a):
+            nc.sync.dma_start(
+                raw, wc[PASS * a : PASS * (a + 1), PASS * b : PASS * (b + 1)].rearrange("(p i) r -> p i r", i=PACK)
+            )
+
+        w_raw = [load_w(0, "stage_d")]
+        c_raw = [load_c(0, "stage_f")]
+
+        planes = held([P, 2 * ROW], U8, "planes")
+        nc.vector.tensor_copy(
+            dense[:, W_AT:WD_AT].rearrange("p (b t m) -> p b t m", t=PACK, m=P),
+            wsc_raw[:].rearrange("p (b m t) -> p b t m", t=PACK, m=P),
+        )
+        nc.gpsimd.memset(planes[:].bitcast(I32), 0)
+        tsc_got = held([P, 2 * J], U8, "tsc_got")
+        nc.vector.tensor_copy(tsc_got[:], tsc_win[:].indirect(offsets[:]))
+        nc.vector.tensor_copy(dense[0:32, 0:W_AT].bitcast(I32), tsc_got[0:32, :].bitcast(I32))
+        for q in range(4):
+            nc.scalar.dma_start(planes[32 * q : 32 * q + 4, :].bitcast(I32), dense[8 * q : 8 * q + 8, :].bitcast(I32))
+        w_raw.append(load_w(1, "stage_a"))
+        c_raw.append(load_c(1, "stage_b"))
+        wc_raw = {}
+
+        t_codes = []
+        w_codes = []
+
+        def gather_words(g):
+            got = held([P, J], U32, "t_got%d" % g)
+            nc.vector.tensor_copy(got[:], tab[:].indirect(offsets[:, g * (J // 16) : (g + 1) * (J // 16)]))
+            parted = held([P, 2 * 2 * J], U8, "t_codes%d" % g)
+            nc.vector.tensor_copy(
+                parted[:].bitcast(U16).rearrange("p (d m) -> p d m", d=2),
+                got[:].bitcast(U16).rearrange("p (m d) -> p d m", d=2),
+            )
+            t_codes.append(parted)
+
+        def order_w(b):
+            codes = held([P, 2 * PASS], U32, "w_codes%d" % b)
+            nc.vector.tensor_copy(
+                codes[:].rearrange("p (a t m) -> p a m t", a=2, t=PACK),
+                w_raw[b][:].rearrange("p a (m t) -> p a m t", t=PACK),
+            )
+            w_codes.append(codes)
+
+        gather_words(0)
+        order_w(0)
+        wc_raw[0, 0] = held([P, PACK, PASS], F32, "wc_raw00", "stage_d")[:]
+        load_wc(wc_raw[0, 0], 0, 0)
+        gather_words(1)
+        trio = held([P, 3, PACK, PASS], F32, "wc_raw_trio", "stage_c")
+        for n, (b, a) in enumerate(((0, 1), (1, 0), (1, 1))):
+            wc_raw[b, a] = trio[:, n]
+            load_wc(wc_raw[b, a], b, a)
+
+        pooled = {}
+
+        def by_point(view):
+            return view.rearrange("p (j t) -> p j t", t=PACK)
+
+        def bank_by_point(bank):
+            return bank[:].rearrange("p (t j) -> p j t", t=PACK)
+
+        def neighbour_sums(b, jt, close):
+            banks = []
+            for g in range(2):
+                bank = psum.tile([P, PACK * JT], F32, name="nbr%d" % g, tag="nbr%d" % g)
+                for t in range(PACK):
+                    for a in range(2):
+                        col = PASS * a + P * t
+                        pcol = ROW * a + W_AT + PASS * b + P * t
+                        tcol = ROW * a + J * g + JT * jt
+                        nc.tensor.matmul_mx(
+                            out=bank[:, JT * t : JT * (t + 1)],
+                            lhsT=w_codes[b][:, col : col + P].bitcast(FP8X4),
+                            lhsT_scale=planes[:, pcol : pcol + P],
+                            rhs=t_codes[g][:, 2 * (J * a + JT * jt) : 2 * (J * a + JT * (jt + 1))].bitcast(FP4X4),
+                            rhs_scale=planes[:, tcol : tcol + JT],
+                            start=(t == 0 and a == 0),
+                            stop=(close and t == PACK - 1 and a == 1),
+                        )
+                banks.append(bank)
+            return banks
+
+        def pool_banks(banks, func, best):
+            first = ring.tile([P, JT * PACK], F32, name="first", align_bytes=64)
+            nc.scalar.activation(by_point(first[:]), bank_by_point(banks[0]), func)
+            nc.vector.tensor_tensor(by_point(best), bank_by_point(banks[1]), by_point(first[:]), ALU.max)
+
+        def pool_unit(b, jt):
+            best = held([P, JT * PACK], F32, "pooled%d%d" % (b, jt))
+            pool_banks(neighbour_sums(b, jt, True), ACT.Copy, best[:])
+            pooled[b, jt] = best
+
+        for jt in range(PLAIN):
+            pool_unit(0, jt)
+        order_w(1)
+        wd_words = held([P, 4 * N + 2 * N], U8, "wd_words", "stage_a")
+        nc.sync.dma_start(wd_words[:, 0 : 4 * N].bitcast(I32), wd8_words[0].rearrange("p n i -> p (n i)").bitcast(I32))
+        nc.sync.dma_start(wd_words[:, 4 * N : 6 * N].bitcast(I32), wd4_words[0].bitcast(I32))
+        for jt in range(NJT):
+            pool_unit(1, jt)
+        open_banks = {}
+        for jt in range(PLAIN, NJT):
+            open_banks[jt] = neighbour_sums(0, jt, False)
+
+        def cast(engine, dst, src):
+            if engine == "v":
+                nc.vector.tensor_copy(dst, src)
+            else:
+                nc.scalar.activation(dst, src, ACT.Copy)
+
+        def quantise(grouped, name):
+            width = grouped.shape[1] // PACK
+            codes = held([P, width], U32, name + "_codes")
+            plane = held([P, width], U8, name + "_plane")
+            nc.vector.quantize_mx(out=codes[:].bitcast(FP8X4), scales=plane[:], in_=grouped)
+            return codes, plane
+
+        def prepare_c(a, shares):
+            grouped = held([P, J * PACK], BF16, "c_bf%d" % a)
+            dst = grouped[:].rearrange("p (x u i) -> p x i u", u=4, i=PACK)
+            src = c_raw[a][:].rearrange("p i (x u) -> p x i u", u=4)
+            for engine, lo, hi in shares:
+                cast(engine, dst[:, lo:hi], src[:, lo:hi])
+            return quantise(grouped[:], "c%d" % a)
+
+        def prepare_wc(b, a, shares):
+            grouped = held([P, PASS * PACK], BF16, "wc_bf%d%d" % (b, a))
+            dst = grouped[:].rearrange("p (t m i) -> p m i t", t=PACK, i=PACK)
+            src = wc_raw[b, a].rearrange("p i (m t) -> p m i t", t=PACK)
+            for engine, lo, hi in shares:
+                cast(engine, dst[:, lo:hi], src[:, lo:hi])
+            return quantise(grouped[:], "wc%d%d" % (b, a))
+
+        halves = (("s", 0, 64), ("s", 64, 128))
+        c_q = [prepare_c(0, halves)]
+        res_sb = held([P, 2, N // P, J // 2], F32, "res_sb", "stage_f")
+        res_rows = res.rearrange("(n p) j -> p n j", p=P)
+        for jh in range(2):
+            nc.sync.dma_start(res_sb[:, jh], res_rows[:, :, (J // 2) * jh : (J // 2) * (jh + 1)])
+        c_q.append(prepare_c(1, (("v", 0, 128),)))
+
+        wc_q = {}
+        own = {}
+
+        def own_pass(bank, b, jt, a, opens):
+            codes, plane = wc_q[b, a]
+            for t in range(PACK):
+                nc.tensor.matmul_mx(
+                    out=bank[:, JT * t : JT * (t + 1)],
+                    lhsT=codes[:, P * t : P * (t + 1)].bitcast(FP8X4),
+                    lhsT_scale=plane[:, P * t : P * (t + 1)],
+                    rhs=c_q[a][0][:, JT * jt : JT * (jt + 1)].bitcast(FP8X4),
+                    rhs_scale=c_q[a][1][:, JT * jt : JT * (jt + 1)],
+                    start=(opens and t == 0),
+                    stop=(a == 1 and t == PACK - 1),
+                )
+
+        def open_own(b, jt):
+            own[b, jt] = psum.tile([P, PACK * JT], F32, name="own%d" % (jt % 2), tag="own%d" % (jt % 2))
+            own_pass(own[b, jt], b, jt, 0, True)
+
+        def add_own(b, jt, summed):
+            own_pass(own[b, jt], b, jt, 1, False)
+            nc.vector.tensor_tensor(by_point(summed), bank_by_point(own[b, jt]), by_point(pooled[b, jt][:]), ALU.add)
+
+        wc_q[0, 0] = prepare_wc(0, 0, halves)
+        wc_q[0, 1] = prepare_wc(0, 1, halves)
+        wc_q[1, 0] = prepare_wc(1, 0, halves)
+        wc_q[1, 1] = prepare_wc(1, 1, (("v", 0, SPLIT_M), ("s", SPLIT_M, 128)))
+
+        tile_w = PACK * JT
+        summed0 = held([P, PLAIN * tile_w], BF16, "summed0")
+        hidden0 = held([P, NJT * tile_w], BF16, "hidden0")
+        for jt in range(PLAIN):
+            open_own(0, jt)
+        for jt in range(PLAIN, NJT):
+            for bank in open_banks[jt]:
+                own_pass(bank, 0, jt, 0, False)
+        for jt in range(PLAIN):
+            add_own(0, jt, summed0[:, tile_w * jt : tile_w * (jt + 1)])
+        nc.vector.tensor_scalar_max(hidden0[:, 0 : PLAIN * tile_w], summed0[:], 0.0)
+        for jt in range(PLAIN, NJT):
+            for bank in open_banks[jt]:
+                own_pass(bank, 0, jt, 1, False)
+            pool_banks(open_banks[jt], ACT.Relu, hidden0[:, tile_w * jt : tile_w * (jt + 1)])
+        h0_codes, h0_plane = quantise(hidden0[:], "h0")
+
+        for jt in range(NJT):
+            open_own(1, jt)
+        out_rows = out.rearrange("(n p) j -> p n j", p=P)
+        h1 = {}
+
+        def first_layer_end(jt):
+            summed = held([P, tile_w], BF16, "summed1%d" % jt)
+            add_own(1, jt, summed[:])
+            h1[jt] = held([P, tile_w], BF16, "hidden1%d" % jt)
+            nc.scalar.activation(h1[jt][:], summed[:], ACT.Relu)
+
+        def second_layer(jt):
+            h1_codes, h1_plane = quantise(h1[jt][:], "h1%d" % jt)
+            bank = psum.tile([P, (N // P) * JT], F32, name="ybank", tag="nbr%d" % (jt % 2))
+            for n in range(N // P):
+                nc.tensor.matmul_mx(
+                    out=bank[:, JT * n : JT * (n + 1)],
+                    lhsT=wd_words[:, 4 * P * n : 4 * P * (n + 1)].bitcast(FP8X4),
+                    lhsT_scale=planes[:, WD_AT + P * n : WD_AT + P * (n + 1)],
+                    rhs=h0_codes[:, JT * jt : JT * (jt + 1)].bitcast(FP8X4),
+                    rhs_scale=h0_plane[:, JT * jt : JT * (jt + 1)],
+                    start=True,
+                    stop=False,
+                )
+                nc.tensor.matmul_mx(
+                    out=bank[:, JT * n : JT * (n + 1)],
+                    lhsT=wd_words[:, 4 * N + 2 * P * n : 4 * N + 2 * P * (n + 1)].bitcast(FP4X4),
+                    lhsT_scale=planes[:, ROW + WD_AT + P * n : ROW + WD_AT + P * (n + 1)],
+                    rhs=h1_codes[:].bitcast(FP8X4),
+                    rhs_scale=h1_plane[:],
+                    start=False,
+                    stop=True,
+                )
+            return bank
+
+        def finish(jt, bank):
+            result = held([P, N // P, JT], F32, "result%d" % jt)
+            lo = JT * (jt % 2)
+            nc.vector.tensor_tensor(
+                result[:], bank[:].rearrange("p (n j) -> p n j", j=JT), res_sb[:, jt // 2, :, lo : lo + JT], ALU.add
+            )
+            nc.sync.dma_start(out_rows[:, :, JT * jt : JT * (jt + 1)], result[:])
+
+        banks = {}
+        for step in range(NJT + 2):
+            if step < NJT:
+                first_layer_end(step)
+            if 1 <= step <= NJT:
+                banks[step - 1] = second_layer(step - 1)
+            if step >= 2:
+                finish(step - 2, banks[step - 2])

@@ -21,7 +21,7 @@ PACK = 4
 PASS = P * PACK
 JT = 128
 NJT = J // JT
-SPLIT_M = 80
+SPLIT_M = 48
 PLAIN = 2
 W_AT = 2 * J
 WD_AT = W_AT + R
@@ -36,48 +36,54 @@ def tile_list_pnet_mix_res_kernel(
     with ExitStack() as ctx:
         lists = ctx.enter_context(tc.tile_pool(name="lists", bufs=1))
         keep = ctx.enter_context(tc.tile_pool(name="keep", bufs=1))
+        stage = ctx.enter_context(tc.tile_pool(name="stage", bufs=1))
         ring = ctx.enter_context(tc.tile_pool(name="ring", bufs=3))
-        psum = ctx.enter_context(tc.psum_pool(name="psum", bufs=2))
+        psum = ctx.enter_context(tc.psum_pool(name="psum", bufs=8))
 
         def held(shape, dtype, name, tag=None):
             return keep.tile(shape, dtype, name=name, tag=tag or name, align_bytes=64)
 
+        def placed(shape, dtype, name, offset):
+            return stage.tile(shape, dtype, name=name, tag=name, align_bytes=64, offset=offset)
+
+        def by_row(scales):
+            return scales.rearrange("(q r) n -> r q n", r=4).bitcast(I32)
+
         offsets = lists.tile([P, 2 * J // 16], U16, name="offsets")
         nc.sync.dma_start(offsets[:], offs)
 
-        tsc_win = held([P, T], U8, "tsc_win", "stage_a")
-        nc.sync.dma_start(tsc_win[0:32, :].bitcast(I32), tab_scales.rearrange("a q t -> q a t").bitcast(I32))
+        tsc_win = held([P, T], U8, "tsc_win")
+        for a in range(2):
+            nc.sync.dma_start(tsc_win[a:32:2, :].bitcast(I32), by_row(tab_scales[a]))
         nc.vector.memset(tsc_win[32:64, :].bitcast(I32), 0)
         nc.gpsimd.memset(tsc_win[64:128, :].bitcast(I32), 0)
         wsc_raw = held([P, R], U8, "wsc_raw")
-        nc.sync.dma_start(wsc_raw[0:32, :].bitcast(I32), w_scales.rearrange("a q r -> q a r").bitcast(I32))
+        for a in range(2):
+            nc.sync.dma_start(wsc_raw[a:32:2, :].bitcast(I32), by_row(w_scales[a]))
         nc.vector.memset(wsc_raw[32:64, :].bitcast(I32), 0)
         nc.vector.memset(wsc_raw[64:128, :].bitcast(I32), 0)
         dense = held([P, ROW], U8, "dense", "stage_b")
         for a, scales in enumerate((wd8_scales, wd4_scales)):
-            nc.sync.dma_start(dense[a:32:2, WD_AT:ROW].bitcast(I32), scales[0].bitcast(I32))
+            nc.sync.dma_start(dense[a:32:2, WD_AT:ROW].bitcast(I32), by_row(scales[0]))
         tab = held([P, T], U32, "tab", "stage_c")
         nc.sync.dma_start(tab[:].bitcast(I32), tab_words[0].rearrange("p t b -> p (t b)").bitcast(I32))
 
         w_flat = w_words.rearrange("a p r i -> p a (r i)")
 
-        def load_w(b, tag):
-            raw = held([P, 2, PASS], U32, "w_raw%d" % b, tag)
+        def load_w(b, raw):
             nc.sync.dma_start(raw[:].bitcast(I32), w_flat[:, :, 4 * PASS * b : 4 * PASS * (b + 1)].bitcast(I32))
-            return raw
+            return raw[:]
 
-        def load_c(a, tag):
-            raw = held([P, PACK, J], F32, "c_raw%d" % a, tag)
+        def load_c(a, raw):
             nc.sync.dma_start(raw[:], c[PASS * a : PASS * (a + 1), :].rearrange("(p i) j -> p i j", i=PACK))
-            return raw
+            return raw[:]
 
         def load_wc(raw, b, a):
             nc.sync.dma_start(
                 raw, wc[PASS * a : PASS * (a + 1), PASS * b : PASS * (b + 1)].rearrange("(p i) r -> p i r", i=PACK)
             )
 
-        w_raw = [load_w(0, "stage_d")]
-        c_raw = [load_c(0, "stage_f")]
+        w_raw = [load_w(0, held([P, 2, PASS], U32, "w_raw0", "stage_d"))]
 
         planes = held([P, 2 * ROW], U8, "planes")
         nc.vector.tensor_copy(
@@ -85,20 +91,21 @@ def tile_list_pnet_mix_res_kernel(
             wsc_raw[:].rearrange("p (b m t) -> p b t m", t=PACK, m=P),
         )
         nc.gpsimd.memset(planes[:].bitcast(I32), 0)
-        tsc_got = held([P, 2 * J], U8, "tsc_got")
+        tsc_got = placed([P, 2 * J], U8, "tsc_got", 4 * PACK * J - J)
         nc.vector.tensor_copy(tsc_got[:], tsc_win[:].indirect(offsets[:]))
         nc.vector.tensor_copy(dense[0:32, 0:W_AT].bitcast(I32), tsc_got[0:32, :].bitcast(I32))
-        for q in range(4):
-            nc.scalar.dma_start(planes[32 * q : 32 * q + 4, :].bitcast(I32), dense[8 * q : 8 * q + 8, :].bitcast(I32))
-        w_raw.append(load_w(1, "stage_a"))
-        c_raw.append(load_c(1, "stage_b"))
+        for r in range(4):
+            nc.sync.dma_start(planes[r:128:32, :].bitcast(I32), dense[8 * r : 8 * r + 8, :].bitcast(I32))
+        c_raw = [load_c(0, placed([P, PACK, J], F32, "c_raw0", 0))]
+        w_raw.append(load_w(1, placed([P, 2, PASS], U32, "w_raw1", 4 * PACK * J)))
+        c_raw.append(load_c(1, held([P, PACK, J], F32, "c_raw1", "stage_b")))
         wc_raw = {}
 
         t_codes = []
         w_codes = []
 
-        def gather_words(g):
-            got = held([P, J], U32, "t_got%d" % g)
+        def gather_words(g, tag):
+            got = held([P, J], U32, "t_got%d" % g, tag)
             nc.vector.tensor_copy(got[:], tab[:].indirect(offsets[:, g * (J // 16) : (g + 1) * (J // 16)]))
             parted = held([P, 2 * 2 * J], U8, "t_codes%d" % g)
             nc.vector.tensor_copy(
@@ -111,19 +118,19 @@ def tile_list_pnet_mix_res_kernel(
             codes = held([P, 2 * PASS], U32, "w_codes%d" % b)
             nc.vector.tensor_copy(
                 codes[:].rearrange("p (a t m) -> p a m t", a=2, t=PACK),
-                w_raw[b][:].rearrange("p a (m t) -> p a m t", t=PACK),
+                w_raw[b].rearrange("p a (m t) -> p a m t", t=PACK),
             )
             w_codes.append(codes)
 
-        gather_words(0)
+        gather_words(0, None)
         order_w(0)
-        wc_raw[0, 0] = held([P, PACK, PASS], F32, "wc_raw00", "stage_d")[:]
-        load_wc(wc_raw[0, 0], 0, 0)
-        gather_words(1)
+        gather_words(1, "stage_d")
         trio = held([P, 3, PACK, PASS], F32, "wc_raw_trio", "stage_c")
-        for n, (b, a) in enumerate(((0, 1), (1, 0), (1, 1))):
+        for n, (b, a) in enumerate(((0, 0), (0, 1), (1, 0))):
             wc_raw[b, a] = trio[:, n]
             load_wc(wc_raw[b, a], b, a)
+        wc_raw[1, 1] = held([P, PACK, PASS], F32, "wc_raw11", "stage_d")[:]
+        load_wc(wc_raw[1, 1], 1, 1)
 
         pooled = {}
 
@@ -133,10 +140,10 @@ def tile_list_pnet_mix_res_kernel(
         def bank_by_point(bank):
             return bank[:].rearrange("p (t j) -> p j t", t=PACK)
 
-        def neighbour_sums(b, jt, close):
+        def neighbour_sums(b, jt, close, which=(0, 1)):
             banks = []
-            for g in range(2):
-                bank = psum.tile([P, PACK * JT], F32, name="nbr%d" % g, tag="nbr%d" % g)
+            for g in which:
+                bank = psum.tile([P, PACK * JT], F32, name="nbr", tag="bank")
                 for t in range(PACK):
                     for a in range(2):
                         col = PASS * a + P * t
@@ -154,28 +161,20 @@ def tile_list_pnet_mix_res_kernel(
                 banks.append(bank)
             return banks
 
-        def pool_banks(banks, func, best):
-            first = ring.tile([P, JT * PACK], F32, name="first", align_bytes=64)
+        def pool_banks(banks, func, best, last=False):
+            if last:
+                first = held([P, JT * PACK], F32, "first_last", "wc_bf01")
+            else:
+                first = ring.tile([P, JT * PACK], F32, name="first", align_bytes=64)
             nc.scalar.activation(by_point(first[:]), bank_by_point(banks[0]), func)
             nc.vector.tensor_tensor(by_point(best), bank_by_point(banks[1]), by_point(first[:]), ALU.max)
 
-        def pool_unit(b, jt):
+        def pool_unit(b, jt, banks):
             best = held([P, JT * PACK], F32, "pooled%d%d" % (b, jt))
-            pool_banks(neighbour_sums(b, jt, True), ACT.Copy, best[:])
+            pool_banks(banks, ACT.Copy, best[:], (b, jt) == (1, NJT - 1))
             pooled[b, jt] = best
 
-        for jt in range(PLAIN):
-            pool_unit(0, jt)
         order_w(1)
-        wd_words = held([P, 4 * N + 2 * N], U8, "wd_words", "stage_a")
-        nc.sync.dma_start(wd_words[:, 0 : 4 * N].bitcast(I32), wd8_words[0].rearrange("p n i -> p (n i)").bitcast(I32))
-        nc.sync.dma_start(wd_words[:, 4 * N : 6 * N].bitcast(I32), wd4_words[0].bitcast(I32))
-        for jt in range(NJT):
-            pool_unit(1, jt)
-        open_banks = {}
-        for jt in range(PLAIN, NJT):
-            open_banks[jt] = neighbour_sums(0, jt, False)
-
         def cast(engine, dst, src):
             if engine == "v":
                 nc.vector.tensor_copy(dst, src)
@@ -192,7 +191,7 @@ def tile_list_pnet_mix_res_kernel(
         def prepare_c(a, shares):
             grouped = held([P, J * PACK], BF16, "c_bf%d" % a)
             dst = grouped[:].rearrange("p (x u i) -> p x i u", u=4, i=PACK)
-            src = c_raw[a][:].rearrange("p i (x u) -> p x i u", u=4)
+            src = c_raw[a].rearrange("p i (x u) -> p x i u", u=4)
             for engine, lo, hi in shares:
                 cast(engine, dst[:, lo:hi], src[:, lo:hi])
             return quantise(grouped[:], "c%d" % a)
@@ -207,7 +206,22 @@ def tile_list_pnet_mix_res_kernel(
 
         halves = (("s", 0, 64), ("s", 64, 128))
         c_q = [prepare_c(0, halves)]
-        res_sb = held([P, 2, N // P, J // 2], F32, "res_sb", "stage_f")
+        early = [neighbour_sums(0, jt, True, (0,)) for jt in range(2)]
+        for jt in range(PLAIN):
+            if jt < 2:
+                pool_unit(0, jt, early[jt] + neighbour_sums(0, jt, True, (1,)))
+            else:
+                pool_unit(0, jt, neighbour_sums(0, jt, True))
+        for jt in range(NJT):
+            pool_unit(1, jt, neighbour_sums(1, jt, True))
+        open_banks = {}
+        for jt in range(PLAIN, NJT):
+            open_banks[jt] = neighbour_sums(0, jt, False)
+
+        wd_words = placed([P, 6 * N], U8, "wd_words", 4 * PACK * J)
+        nc.sync.dma_start(wd_words[:, 0 : 4 * N].bitcast(I32), wd8_words[0].rearrange("p n i -> p (n i)").bitcast(I32))
+        nc.sync.dma_start(wd_words[:, 4 * N : 6 * N].bitcast(I32), wd4_words[0].bitcast(I32))
+        res_sb = placed([P, 2, N // P, J // 2], F32, "res_sb", 0)
         res_rows = res.rearrange("(n p) j -> p n j", p=P)
         for jh in range(2):
             nc.sync.dma_start(res_sb[:, jh], res_rows[:, :, (J // 2) * jh : (J // 2) * (jh + 1)])
@@ -230,7 +244,7 @@ def tile_list_pnet_mix_res_kernel(
                 )
 
         def open_own(b, jt):
-            own[b, jt] = psum.tile([P, PACK * JT], F32, name="own%d" % (jt % 2), tag="own%d" % (jt % 2))
+            own[b, jt] = psum.tile([P, PACK * JT], F32, name="own", tag="bank")
             own_pass(own[b, jt], b, jt, 0, True)
 
         def add_own(b, jt, summed):
@@ -238,7 +252,7 @@ def tile_list_pnet_mix_res_kernel(
             nc.vector.tensor_tensor(by_point(summed), bank_by_point(own[b, jt]), by_point(pooled[b, jt][:]), ALU.add)
 
         wc_q[0, 0] = prepare_wc(0, 0, halves)
-        wc_q[0, 1] = prepare_wc(0, 1, halves)
+        wc_q[0, 1] = prepare_wc(0, 1, (("v", 0, 128),))
         wc_q[1, 0] = prepare_wc(1, 0, halves)
         wc_q[1, 1] = prepare_wc(1, 1, (("v", 0, SPLIT_M), ("s", SPLIT_M, 128)))
 
@@ -270,19 +284,24 @@ def tile_list_pnet_mix_res_kernel(
             h1[jt] = held([P, tile_w], BF16, "hidden1%d" % jt)
             nc.scalar.activation(h1[jt][:], summed[:], ACT.Relu)
 
-        def second_layer(jt):
-            h1_codes, h1_plane = quantise(h1[jt][:], "h1%d" % jt)
-            bank = psum.tile([P, (N // P) * JT], F32, name="ybank", tag="nbr%d" % (jt % 2))
+        ybank = {}
+        for jt in range(NJT):
+            ybank[jt] = psum.tile([P, (N // P) * JT], F32, name="ybank", tag="bank")
             for n in range(N // P):
                 nc.tensor.matmul_mx(
-                    out=bank[:, JT * n : JT * (n + 1)],
+                    out=ybank[jt][:, JT * n : JT * (n + 1)],
                     lhsT=wd_words[:, 4 * P * n : 4 * P * (n + 1)].bitcast(FP8X4),
                     lhsT_scale=planes[:, WD_AT + P * n : WD_AT + P * (n + 1)],
                     rhs=h0_codes[:, JT * jt : JT * (jt + 1)].bitcast(FP8X4),
                     rhs_scale=h0_plane[:, JT * jt : JT * (jt + 1)],
-                    start=True,
+                    start=(n == 0),
                     stop=False,
                 )
+
+        def second_layer(jt):
+            h1_codes, h1_plane = quantise(h1[jt][:], "h1%d" % jt)
+            bank = ybank[jt]
+            for n in range(N // P):
                 nc.tensor.matmul_mx(
                     out=bank[:, JT * n : JT * (n + 1)],
                     lhsT=wd_words[:, 4 * N + 2 * P * n : 4 * N + 2 * P * (n + 1)].bitcast(FP4X4),
@@ -290,7 +309,7 @@ def tile_list_pnet_mix_res_kernel(
                     rhs=h1_codes[:].bitcast(FP8X4),
                     rhs_scale=h1_plane[:],
                     start=False,
-                    stop=True,
+                    stop=(n == N // P - 1),
                 )
             return bank
 

@@ -21,7 +21,7 @@ PACK = 4
 PASS = P * PACK
 JT = 128
 NJT = J // JT
-SPLIT_M = 48
+SPLIT_M = 96
 PLAIN = 2
 W_AT = 2 * J
 WD_AT = W_AT + R
@@ -117,8 +117,8 @@ def tile_list_pnet_mix_res_kernel(
         def order_w(b):
             codes = held([P, 2 * PASS], U32, "w_codes%d" % b)
             nc.vector.tensor_copy(
-                codes[:].rearrange("p (a t m) -> p a m t", a=2, t=PACK),
-                w_raw[b].rearrange("p a (m t) -> p a m t", t=PACK),
+                codes[:].rearrange("p (a h l m) -> p a h m l", a=2, h=2, l=2),
+                w_raw[b].rearrange("p a (m h l) -> p a h m l", h=2, l=2),
             )
             w_codes.append(codes)
 
@@ -198,12 +198,13 @@ def tile_list_pnet_mix_res_kernel(
 
         def prepare_wc(b, a, shares):
             grouped = held([P, PASS * PACK], BF16, "wc_bf%d%d" % (b, a))
-            dst = grouped[:].rearrange("p (t m i) -> p m i t", t=PACK, i=PACK)
-            src = wc_raw[b, a].rearrange("p i (m t) -> p m i t", t=PACK)
-            for engine, lo, hi in shares:
-                cast(engine, dst[:, lo:hi], src[:, lo:hi])
+            dst = grouped[:].rearrange("p (h l m i) -> p h m i l", h=2, l=2, i=PACK)
+            src = wc_raw[b, a].rearrange("p i (m h l) -> p h m i l", h=2, l=2)
+            for engine, h, lo, hi in shares:
+                cast(engine, dst[:, h, lo:hi], src[:, h, lo:hi])
             return quantise(grouped[:], "wc%d%d" % (b, a))
 
+        on_scalar = (("s", 0, 0, P), ("s", 1, 0, P))
         halves = (("s", 0, 64), ("s", 64, 128))
         c_q = [prepare_c(0, halves)]
         early = [neighbour_sums(0, jt, True, (0,)) for jt in range(2)]
@@ -251,10 +252,10 @@ def tile_list_pnet_mix_res_kernel(
             own_pass(own[b, jt], b, jt, 1, False)
             nc.vector.tensor_tensor(by_point(summed), bank_by_point(own[b, jt]), by_point(pooled[b, jt][:]), ALU.add)
 
-        wc_q[0, 0] = prepare_wc(0, 0, halves)
-        wc_q[0, 1] = prepare_wc(0, 1, (("v", 0, 128),))
-        wc_q[1, 0] = prepare_wc(1, 0, halves)
-        wc_q[1, 1] = prepare_wc(1, 1, (("v", 0, SPLIT_M), ("s", SPLIT_M, 128)))
+        wc_q[0, 0] = prepare_wc(0, 0, on_scalar)
+        wc_q[0, 1] = prepare_wc(0, 1, (("v", 0, 0, P), ("v", 1, 0, P)))
+        wc_q[1, 0] = prepare_wc(1, 0, on_scalar)
+        wc_q[1, 1] = prepare_wc(1, 1, (("v", 0, 0, SPLIT_M), ("s", 1, 0, P), ("s", 0, SPLIT_M, P)))
 
         tile_w = PACK * JT
         summed0 = held([P, PLAIN * tile_w], BF16, "summed0")

@@ -3,7 +3,7 @@ from contextlib import ExitStack
 import concourse.mybir as mybir
 
 K, R, N, T, J = 1024, 1024, 512, 4096, 512
-FLOPS = 3758096384
+FLOPS = 2 * K * R * 3 * J + 2 * R * N * J
 
 F32 = mybir.dt.float32
 BF16 = mybir.dt.bfloat16
@@ -21,11 +21,18 @@ PACK = 4
 PASS = P * PACK
 JT = 128
 NJT = J // JT
-SPLIT_M = 96
-PLAIN = 2
+TILE_W = PACK * JT
+LIST_GROUP = 16
+QUADRANT = 32
+ROWS = 4
+
+DENSE = P - 32
 W_AT = 2 * J
 WD_AT = W_AT + R
 ROW = WD_AT + N
+
+PLAIN = 2
+SPLIT_M = 96
 
 
 def tile_list_pnet_mix_res_kernel(
@@ -47,26 +54,24 @@ def tile_list_pnet_mix_res_kernel(
             return stage.tile(shape, dtype, name=name, tag=name, align_bytes=64, offset=offset)
 
         def by_row(scales):
-            return scales.rearrange("(q r) n -> r q n", r=4).bitcast(I32)
+            return scales.rearrange("(d s) e -> s d e", s=ROWS).bitcast(I32)
 
-        offsets = lists.tile([P, 2 * J // 16], U16, name="offsets")
+        offsets = lists.tile([P, 2 * J // LIST_GROUP], U16, name="offsets")
         nc.sync.dma_start(offsets[:], offs)
 
-        tsc_win = held([P, T], U8, "tsc_win")
-        for a in range(2):
-            nc.sync.dma_start(tsc_win[a:32:2, :].bitcast(I32), by_row(tab_scales[a]))
-        nc.vector.memset(tsc_win[32:64, :].bitcast(I32), 0)
-        nc.gpsimd.memset(tsc_win[64:128, :].bitcast(I32), 0)
         wsc_raw = held([P, R], U8, "wsc_raw")
         for a in range(2):
-            nc.sync.dma_start(wsc_raw[a:32:2, :].bitcast(I32), by_row(w_scales[a]))
-        nc.vector.memset(wsc_raw[32:64, :].bitcast(I32), 0)
-        nc.vector.memset(wsc_raw[64:128, :].bitcast(I32), 0)
+            nc.sync.dma_start(wsc_raw[DENSE + a : P : 2, :].bitcast(I32), by_row(w_scales[a]))
+        nc.vector.memset(wsc_raw[0:DENSE, :].bitcast(I32), 0)
+        tsc_win = held([P, T], U8, "tsc_win")
+        for a in range(2):
+            nc.sync.dma_start(tsc_win[DENSE + a : P : 2, :].bitcast(I32), by_row(tab_scales[a]))
+        nc.vector.memset(tsc_win[0:DENSE, :].bitcast(I32), 0)
         dense = held([P, ROW], U8, "dense", "stage_b")
         for a, scales in enumerate((wd8_scales, wd4_scales)):
-            nc.sync.dma_start(dense[a:32:2, WD_AT:ROW].bitcast(I32), by_row(scales[0]))
+            nc.sync.dma_start(dense[DENSE + a : P : 2, WD_AT:ROW].bitcast(I32), by_row(scales[0]))
         tab = held([P, T], U32, "tab", "stage_c")
-        nc.sync.dma_start(tab[:].bitcast(I32), tab_words[0].rearrange("p t b -> p (t b)").bitcast(I32))
+        nc.sync.dma_start(tab[:].bitcast(I32), tab_words[0].rearrange("p e f -> p (e f)").bitcast(I32))
 
         w_flat = w_words.rearrange("a p r i -> p a (r i)")
 
@@ -90,47 +95,52 @@ def tile_list_pnet_mix_res_kernel(
             dense[:, W_AT:WD_AT].rearrange("p (b t m) -> p b t m", t=PACK, m=P),
             wsc_raw[:].rearrange("p (b m t) -> p b t m", t=PACK, m=P),
         )
-        nc.gpsimd.memset(planes[:].bitcast(I32), 0)
-        tsc_got = placed([P, 2 * J], U8, "tsc_got", 4 * PACK * J - J)
+        nc.vector.memset(planes[:].bitcast(I32), 0)
+        c_bytes = 4 * PACK * J
+        tsc_got = placed([P, 2 * J], U8, "tsc_got", c_bytes - J)
         nc.vector.tensor_copy(tsc_got[:], tsc_win[:].indirect(offsets[:]))
-        nc.vector.tensor_copy(dense[0:32, 0:W_AT].bitcast(I32), tsc_got[0:32, :].bitcast(I32))
-        for r in range(4):
-            nc.sync.dma_start(planes[r:128:32, :].bitcast(I32), dense[8 * r : 8 * r + 8, :].bitcast(I32))
+        nc.vector.tensor_copy(dense[DENSE:P, 0:W_AT].bitcast(I32), tsc_got[DENSE:P, :].bitcast(I32))
+        for s in range(ROWS):
+            nc.sync.dma_start(
+                planes[s:P:QUADRANT, :].bitcast(I32), dense[DENSE + 8 * s : DENSE + 8 * (s + 1), :].bitcast(I32)
+            )
         c_raw = [load_c(0, placed([P, PACK, J], F32, "c_raw0", 0))]
-        w_raw.append(load_w(1, placed([P, 2, PASS], U32, "w_raw1", 4 * PACK * J)))
+        w_raw.append(load_w(1, placed([P, 2, PASS], U32, "w_raw1", c_bytes)))
         c_raw.append(load_c(1, held([P, PACK, J], F32, "c_raw1", "stage_b")))
-        wc_raw = {}
 
         t_codes = []
         w_codes = []
 
         def gather_words(g, tag):
             got = held([P, J], U32, "t_got%d" % g, tag)
-            nc.vector.tensor_copy(got[:], tab[:].indirect(offsets[:, g * (J // 16) : (g + 1) * (J // 16)]))
+            columns = J // LIST_GROUP
+            nc.vector.tensor_copy(got[:], tab[:].indirect(offsets[:, g * columns : (g + 1) * columns]))
             parted = held([P, 2 * 2 * J], U8, "t_codes%d" % g)
             nc.vector.tensor_copy(
-                parted[:].bitcast(U16).rearrange("p (d m) -> p d m", d=2),
-                got[:].bitcast(U16).rearrange("p (m d) -> p d m", d=2),
+                parted[:].bitcast(U16).rearrange("p (a j) -> p a j", a=2),
+                got[:].bitcast(U16).rearrange("p (j a) -> p a j", a=2),
             )
             t_codes.append(parted)
 
         def order_w(b):
             codes = held([P, 2 * PASS], U32, "w_codes%d" % b)
             nc.vector.tensor_copy(
-                codes[:].rearrange("p (a h l m) -> p a h m l", a=2, h=2, l=2),
-                w_raw[b].rearrange("p a (m h l) -> p a h m l", h=2, l=2),
+                codes[:].rearrange("p (a u l m) -> p a u m l", a=2, u=2, l=2),
+                w_raw[b].rearrange("p a (m u l) -> p a u m l", u=2, l=2),
             )
             w_codes.append(codes)
 
         gather_words(0, None)
         order_w(0)
         gather_words(1, "stage_d")
+        wc_raw = {}
         trio = held([P, 3, PACK, PASS], F32, "wc_raw_trio", "stage_c")
-        for n, (b, a) in enumerate(((0, 0), (0, 1), (1, 0))):
-            wc_raw[b, a] = trio[:, n]
+        for slot, (b, a) in enumerate(((0, 0), (0, 1), (1, 0))):
+            wc_raw[b, a] = trio[:, slot]
             load_wc(wc_raw[b, a], b, a)
         wc_raw[1, 1] = held([P, PACK, PASS], F32, "wc_raw11", "stage_d")[:]
         load_wc(wc_raw[1, 1], 1, 1)
+        order_w(1)
 
         pooled = {}
 
@@ -140,46 +150,38 @@ def tile_list_pnet_mix_res_kernel(
         def bank_by_point(bank):
             return bank[:].rearrange("p (t j) -> p j t", t=PACK)
 
-        def neighbour_sums(b, jt, close, which=(0, 1)):
-            banks = []
-            for g in which:
-                bank = psum.tile([P, PACK * JT], F32, name="nbr", tag="bank")
-                for t in range(PACK):
-                    for a in range(2):
-                        col = PASS * a + P * t
-                        pcol = ROW * a + W_AT + PASS * b + P * t
-                        tcol = ROW * a + J * g + JT * jt
-                        nc.tensor.matmul_mx(
-                            out=bank[:, JT * t : JT * (t + 1)],
-                            lhsT=w_codes[b][:, col : col + P].bitcast(FP8X4),
-                            lhsT_scale=planes[:, pcol : pcol + P],
-                            rhs=t_codes[g][:, 2 * (J * a + JT * jt) : 2 * (J * a + JT * (jt + 1))].bitcast(FP4X4),
-                            rhs_scale=planes[:, tcol : tcol + JT],
-                            start=(t == 0 and a == 0),
-                            stop=(close and t == PACK - 1 and a == 1),
-                        )
-                banks.append(bank)
-            return banks
+        def neighbour_sum(b, jt, g, close):
+            bank = psum.tile([P, TILE_W], F32, name="nbr", tag="bank")
+            for t in range(PACK):
+                for a in range(2):
+                    col = PASS * a + P * t
+                    w_col = ROW * a + W_AT + PASS * b + P * t
+                    tab_col = ROW * a + J * g + JT * jt
+                    nc.tensor.matmul_mx(
+                        out=bank[:, JT * t : JT * (t + 1)],
+                        lhsT=w_codes[b][:, col : col + P].bitcast(FP8X4),
+                        lhsT_scale=planes[:, w_col : w_col + P],
+                        rhs=t_codes[g][:, 2 * (J * a + JT * jt) : 2 * (J * a + JT * (jt + 1))].bitcast(FP4X4),
+                        rhs_scale=planes[:, tab_col : tab_col + JT],
+                        start=(t == 0 and a == 0),
+                        stop=(close and t == PACK - 1 and a == 1),
+                    )
+            return bank
 
-        def pool_banks(banks, func, best, last=False):
-            if last:
-                first = held([P, JT * PACK], F32, "first_last", "wc_bf01")
-            else:
-                first = ring.tile([P, JT * PACK], F32, name="first", align_bytes=64)
+        def pool_banks(banks, func, best):
+            first = ring.tile([P, TILE_W], F32, name="first", align_bytes=64)
             nc.scalar.activation(by_point(first[:]), bank_by_point(banks[0]), func)
             nc.vector.tensor_tensor(by_point(best), bank_by_point(banks[1]), by_point(first[:]), ALU.max)
 
-        def pool_unit(b, jt, banks):
-            best = held([P, JT * PACK], F32, "pooled%d%d" % (b, jt))
-            pool_banks(banks, ACT.Copy, best[:], (b, jt) == (1, NJT - 1))
-            pooled[b, jt] = best
+        def pool_tile(b, jt, banks):
+            pooled[b, jt] = held([P, TILE_W], F32, "pooled%d%d" % (b, jt))
+            pool_banks(banks, ACT.Copy, pooled[b, jt][:])
 
-        order_w(1)
-        def cast(engine, dst, src):
-            if engine == "v":
-                nc.vector.tensor_copy(dst, src)
-            else:
-                nc.scalar.activation(dst, src, ACT.Copy)
+        def round_on_vector(dst, src):
+            nc.vector.tensor_copy(dst, src)
+
+        def round_on_scalar(dst, src):
+            nc.scalar.activation(dst, src, ACT.Copy)
 
         def quantise(grouped, name):
             width = grouped.shape[1] // PACK
@@ -190,43 +192,39 @@ def tile_list_pnet_mix_res_kernel(
 
         def prepare_c(a, shares):
             grouped = held([P, J * PACK], BF16, "c_bf%d" % a)
-            dst = grouped[:].rearrange("p (x u i) -> p x i u", u=4, i=PACK)
-            src = c_raw[a].rearrange("p i (x u) -> p x i u", u=4)
-            for engine, lo, hi in shares:
-                cast(engine, dst[:, lo:hi], src[:, lo:hi])
+            dst = grouped[:].rearrange("p (x z i) -> p x i z", z=4, i=PACK)
+            src = c_raw[a].rearrange("p i (x z) -> p x i z", z=4)
+            for rounder, lo, hi in shares:
+                rounder(dst[:, lo:hi], src[:, lo:hi])
             return quantise(grouped[:], "c%d" % a)
 
         def prepare_wc(b, a, shares):
             grouped = held([P, PASS * PACK], BF16, "wc_bf%d%d" % (b, a))
-            dst = grouped[:].rearrange("p (h l m i) -> p h m i l", h=2, l=2, i=PACK)
-            src = wc_raw[b, a].rearrange("p i (m h l) -> p h m i l", h=2, l=2)
-            for engine, h, lo, hi in shares:
-                cast(engine, dst[:, h, lo:hi], src[:, h, lo:hi])
+            dst = grouped[:].rearrange("p (u l m i) -> p u m i l", u=2, l=2, i=PACK)
+            src = wc_raw[b, a].rearrange("p i (m u l) -> p u m i l", u=2, l=2)
+            for rounder, u, lo, hi in shares:
+                rounder(dst[:, u, lo:hi], src[:, u, lo:hi])
             return quantise(grouped[:], "wc%d%d" % (b, a))
 
-        on_scalar = (("s", 0, 0, P), ("s", 1, 0, P))
-        halves = (("s", 0, 64), ("s", 64, 128))
-        c_q = [prepare_c(0, halves)]
-        early = [neighbour_sums(0, jt, True, (0,)) for jt in range(2)]
+        groups = J // 4
+        c_q = [prepare_c(0, ((round_on_scalar, 0, groups // 2), (round_on_scalar, groups // 2, groups)))]
+        leading = [neighbour_sum(0, jt, 0, True) for jt in range(PLAIN)]
         for jt in range(PLAIN):
-            if jt < 2:
-                pool_unit(0, jt, early[jt] + neighbour_sums(0, jt, True, (1,)))
-            else:
-                pool_unit(0, jt, neighbour_sums(0, jt, True))
+            pool_tile(0, jt, (leading[jt], neighbour_sum(0, jt, 1, True)))
         for jt in range(NJT):
-            pool_unit(1, jt, neighbour_sums(1, jt, True))
+            pool_tile(1, jt, [neighbour_sum(1, jt, g, True) for g in range(2)])
         open_banks = {}
         for jt in range(PLAIN, NJT):
-            open_banks[jt] = neighbour_sums(0, jt, False)
+            open_banks[jt] = [neighbour_sum(0, jt, g, False) for g in range(2)]
 
-        wd_words = placed([P, 6 * N], U8, "wd_words", 4 * PACK * J)
+        wd_words = placed([P, 6 * N], U8, "wd_words", c_bytes)
         nc.sync.dma_start(wd_words[:, 0 : 4 * N].bitcast(I32), wd8_words[0].rearrange("p n i -> p (n i)").bitcast(I32))
         nc.sync.dma_start(wd_words[:, 4 * N : 6 * N].bitcast(I32), wd4_words[0].bitcast(I32))
         res_sb = placed([P, 2, N // P, J // 2], F32, "res_sb", 0)
         res_rows = res.rearrange("(n p) j -> p n j", p=P)
         for jh in range(2):
             nc.sync.dma_start(res_sb[:, jh], res_rows[:, :, (J // 2) * jh : (J // 2) * (jh + 1)])
-        c_q.append(prepare_c(1, (("v", 0, 128),)))
+        c_q.append(prepare_c(1, ((round_on_vector, 0, groups),)))
 
         wc_q = {}
         own = {}
@@ -245,52 +243,46 @@ def tile_list_pnet_mix_res_kernel(
                 )
 
         def open_own(b, jt):
-            own[b, jt] = psum.tile([P, PACK * JT], F32, name="own", tag="bank")
+            own[b, jt] = psum.tile([P, TILE_W], F32, name="own", tag="bank")
             own_pass(own[b, jt], b, jt, 0, True)
 
         def add_own(b, jt, summed):
             own_pass(own[b, jt], b, jt, 1, False)
             nc.vector.tensor_tensor(by_point(summed), bank_by_point(own[b, jt]), by_point(pooled[b, jt][:]), ALU.add)
 
-        wc_q[0, 0] = prepare_wc(0, 0, on_scalar)
-        wc_q[0, 1] = prepare_wc(0, 1, (("v", 0, 0, P), ("v", 1, 0, P)))
-        wc_q[1, 0] = prepare_wc(1, 0, on_scalar)
-        wc_q[1, 1] = prepare_wc(1, 1, (("v", 0, 0, SPLIT_M), ("s", 1, 0, P), ("s", 0, SPLIT_M, P)))
+        wc_q[0, 0] = prepare_wc(0, 0, [(round_on_scalar, u, 0, P) for u in range(2)])
+        wc_q[0, 1] = prepare_wc(0, 1, [(round_on_vector, u, 0, P) for u in range(2)])
+        wc_q[1, 0] = prepare_wc(1, 0, [(round_on_scalar, u, 0, P) for u in range(2)])
+        wc_q[1, 1] = prepare_wc(
+            1, 1, ((round_on_vector, 0, 0, SPLIT_M), (round_on_scalar, 1, 0, P), (round_on_scalar, 0, SPLIT_M, P))
+        )
 
-        tile_w = PACK * JT
-        summed0 = held([P, PLAIN * tile_w], BF16, "summed0")
-        hidden0 = held([P, NJT * tile_w], BF16, "hidden0")
+        summed0 = held([P, PLAIN * TILE_W], BF16, "summed0")
+        hidden0 = held([P, NJT * TILE_W], BF16, "hidden0")
         for jt in range(PLAIN):
             open_own(0, jt)
         for jt in range(PLAIN, NJT):
             for bank in open_banks[jt]:
                 own_pass(bank, 0, jt, 0, False)
         for jt in range(PLAIN):
-            add_own(0, jt, summed0[:, tile_w * jt : tile_w * (jt + 1)])
-        nc.vector.tensor_scalar_max(hidden0[:, 0 : PLAIN * tile_w], summed0[:], 0.0)
+            add_own(0, jt, summed0[:, TILE_W * jt : TILE_W * (jt + 1)])
+        nc.vector.tensor_scalar_max(hidden0[:, 0 : PLAIN * TILE_W], summed0[:], 0.0)
         for jt in range(PLAIN, NJT):
             for bank in open_banks[jt]:
                 own_pass(bank, 0, jt, 1, False)
-            pool_banks(open_banks[jt], ACT.Relu, hidden0[:, tile_w * jt : tile_w * (jt + 1)])
+            pool_banks(open_banks[jt], ACT.Relu, hidden0[:, TILE_W * jt : TILE_W * (jt + 1)])
         h0_codes, h0_plane = quantise(hidden0[:], "h0")
 
         for jt in range(NJT):
             open_own(1, jt)
         out_rows = out.rearrange("(n p) j -> p n j", p=P)
-        h1 = {}
-
-        def first_layer_end(jt):
-            summed = held([P, tile_w], BF16, "summed1%d" % jt)
-            add_own(1, jt, summed[:])
-            h1[jt] = held([P, tile_w], BF16, "hidden1%d" % jt)
-            nc.scalar.activation(h1[jt][:], summed[:], ACT.Relu)
-
-        ybank = {}
+        hidden1 = {}
+        y_bank = {}
         for jt in range(NJT):
-            ybank[jt] = psum.tile([P, (N // P) * JT], F32, name="ybank", tag="bank")
+            y_bank[jt] = psum.tile([P, (N // P) * JT], F32, name="y_bank", tag="bank")
             for n in range(N // P):
                 nc.tensor.matmul_mx(
-                    out=ybank[jt][:, JT * n : JT * (n + 1)],
+                    out=y_bank[jt][:, JT * n : JT * (n + 1)],
                     lhsT=wd_words[:, 4 * P * n : 4 * P * (n + 1)].bitcast(FP8X4),
                     lhsT_scale=planes[:, WD_AT + P * n : WD_AT + P * (n + 1)],
                     rhs=h0_codes[:, JT * jt : JT * (jt + 1)].bitcast(FP8X4),
@@ -299,12 +291,17 @@ def tile_list_pnet_mix_res_kernel(
                     stop=False,
                 )
 
-        def second_layer(jt):
-            h1_codes, h1_plane = quantise(h1[jt][:], "h1%d" % jt)
-            bank = ybank[jt]
+        def end_first_layer(jt):
+            summed = held([P, TILE_W], BF16, "summed1%d" % jt)
+            add_own(1, jt, summed[:])
+            hidden1[jt] = held([P, TILE_W], BF16, "hidden1%d" % jt)
+            nc.scalar.activation(hidden1[jt][:], summed[:], ACT.Relu)
+
+        def end_second_layer(jt):
+            h1_codes, h1_plane = quantise(hidden1[jt][:], "h1%d" % jt)
             for n in range(N // P):
                 nc.tensor.matmul_mx(
-                    out=bank[:, JT * n : JT * (n + 1)],
+                    out=y_bank[jt][:, JT * n : JT * (n + 1)],
                     lhsT=wd_words[:, 4 * N + 2 * P * n : 4 * N + 2 * P * (n + 1)].bitcast(FP4X4),
                     lhsT_scale=planes[:, ROW + WD_AT + P * n : ROW + WD_AT + P * (n + 1)],
                     rhs=h1_codes[:].bitcast(FP8X4),
@@ -312,21 +309,22 @@ def tile_list_pnet_mix_res_kernel(
                     start=False,
                     stop=(n == N // P - 1),
                 )
-            return bank
 
-        def finish(jt, bank):
+        def add_residual_and_store(jt):
             result = held([P, N // P, JT], F32, "result%d" % jt)
-            lo = JT * (jt % 2)
+            first_point = JT * (jt % 2)
             nc.vector.tensor_tensor(
-                result[:], bank[:].rearrange("p (n j) -> p n j", j=JT), res_sb[:, jt // 2, :, lo : lo + JT], ALU.add
+                result[:],
+                y_bank[jt][:].rearrange("p (n j) -> p n j", j=JT),
+                res_sb[:, jt // 2, :, first_point : first_point + JT],
+                ALU.add,
             )
             nc.sync.dma_start(out_rows[:, :, JT * jt : JT * (jt + 1)], result[:])
 
-        banks = {}
         for step in range(NJT + 2):
             if step < NJT:
-                first_layer_end(step)
+                end_first_layer(step)
             if 1 <= step <= NJT:
-                banks[step - 1] = second_layer(step - 1)
+                end_second_layer(step - 1)
             if step >= 2:
-                finish(step - 2, banks[step - 2])
+                add_residual_and_store(step - 2)

@@ -53,60 +53,72 @@ def tile_list_pnet_mix_res_kernel(
         def placed(shape, dtype, name, offset):
             return stage.tile(shape, dtype, name=name, tag=name, align_bytes=64, offset=offset)
 
-        def by_row(scales):
-            return scales.rearrange("(d s) e -> s d e", s=ROWS).bitcast(I32)
+        def by_block(scales):
+            return scales.rearrange("a q e -> q a e").bitcast(I32)
 
         offsets = lists.tile([P, 2 * J // LIST_GROUP], U16, name="offsets")
         nc.sync.dma_start(offsets[:], offs)
 
-        wsc_raw = held([P, R], U8, "wsc_raw")
-        for a in range(2):
-            nc.sync.dma_start(wsc_raw[DENSE + a : P : 2, :].bitcast(I32), by_row(w_scales[a]))
-        nc.vector.memset(wsc_raw[0:DENSE, :].bitcast(I32), 0)
         tsc_win = held([P, T], U8, "tsc_win")
-        for a in range(2):
-            nc.sync.dma_start(tsc_win[DENSE + a : P : 2, :].bitcast(I32), by_row(tab_scales[a]))
+        nc.sync.dma_start(tsc_win[DENSE:P, :].bitcast(I32), by_block(tab_scales))
         nc.vector.memset(tsc_win[0:DENSE, :].bitcast(I32), 0)
-        dense = held([P, ROW], U8, "dense", "stage_b")
+        wsc_raw = held([P, R], U8, "wsc_raw")
+        nc.sync.dma_start(wsc_raw[DENSE:P, :].bitcast(I32), by_block(w_scales))
+        nc.vector.memset(wsc_raw[0:DENSE, :].bitcast(I32), 0)
+        dense = held([P, ROW], U8, "dense")
         for a, scales in enumerate((wd8_scales, wd4_scales)):
-            nc.sync.dma_start(dense[DENSE + a : P : 2, WD_AT:ROW].bitcast(I32), by_row(scales[0]))
-        tab = held([P, T], U32, "tab", "stage_c")
+            nc.sync.dma_start(dense[DENSE + a : P : 2, WD_AT:ROW].bitcast(I32), scales[0].bitcast(I32))
+        tab = held([P, T], U32, "tab")
         nc.sync.dma_start(tab[:].bitcast(I32), tab_words[0].rearrange("p e f -> p (e f)").bitcast(I32))
 
         w_flat = w_words.rearrange("a p r i -> p a (r i)")
 
         def load_w(b, raw):
-            nc.sync.dma_start(raw[:].bitcast(I32), w_flat[:, :, 4 * PASS * b : 4 * PASS * (b + 1)].bitcast(I32))
-            return raw[:]
+            nc.sync.dma_start(raw.bitcast(I32), w_flat[:, :, 4 * PASS * b : 4 * PASS * (b + 1)].bitcast(I32))
+            return raw
 
         def load_c(a, raw):
-            nc.sync.dma_start(raw[:], c[PASS * a : PASS * (a + 1), :].rearrange("(p i) j -> p i j", i=PACK))
-            return raw[:]
+            nc.sync.dma_start(raw, c[PASS * a : PASS * (a + 1), :].rearrange("(p i) j -> p i j", i=PACK))
+            return raw
 
         def load_wc(raw, b, a):
             nc.sync.dma_start(
                 raw, wc[PASS * a : PASS * (a + 1), PASS * b : PASS * (b + 1)].rearrange("(p i) r -> p i r", i=PACK)
             )
 
-        w_raw = [load_w(0, held([P, 2, PASS], U32, "w_raw0", "stage_d"))]
+        w_raw = [load_w(0, held([P, 2, PASS], U32, "w_raw0", "stage_d")[:])]
+        c_raw = [load_c(0, held([P, PACK, J], F32, "c_raw0")[:])]
 
         planes = held([P, 2 * ROW], U8, "planes")
+        nc.gpsimd.memset(planes[:].bitcast(I32), 0)
+        piece = PACK * PASS
+        float_bytes = 4 * 6 * piece
+        tsc_got = placed([P, 2 * J], U8, "tsc_got", float_bytes - J)
+        nc.vector.tensor_copy(tsc_got[:], tsc_win[:].indirect(offsets[:]))
         nc.vector.tensor_copy(
             dense[:, W_AT:WD_AT].rearrange("p (b t m) -> p b t m", t=PACK, m=P),
             wsc_raw[:].rearrange("p (b m t) -> p b t m", t=PACK, m=P),
         )
-        nc.vector.memset(planes[:].bitcast(I32), 0)
-        c_bytes = 4 * PACK * J
-        tsc_got = placed([P, 2 * J], U8, "tsc_got", c_bytes - J)
-        nc.vector.tensor_copy(tsc_got[:], tsc_win[:].indirect(offsets[:]))
         nc.vector.tensor_copy(dense[DENSE:P, 0:W_AT].bitcast(I32), tsc_got[DENSE:P, :].bitcast(I32))
-        for s in range(ROWS):
+        for quad in range(P // QUADRANT):
             nc.sync.dma_start(
-                planes[s:P:QUADRANT, :].bitcast(I32), dense[DENSE + 8 * s : DENSE + 8 * (s + 1), :].bitcast(I32)
+                planes[QUADRANT * quad : QUADRANT * quad + ROWS, :].bitcast(I32),
+                dense[DENSE + 2 * ROWS * quad : DENSE + 2 * ROWS * (quad + 1), :].bitcast(I32),
             )
-        c_raw = [load_c(0, placed([P, PACK, J], F32, "c_raw0", 0))]
-        w_raw.append(load_w(1, placed([P, 2, PASS], U32, "w_raw1", c_bytes)))
-        c_raw.append(load_c(1, held([P, PACK, J], F32, "c_raw1", "stage_b")))
+        floats = placed([P, 6, PACK, PASS], F32, "floats", 0)
+        words = placed([P, 2 * 4 * PASS + 6 * N], U8, "words", float_bytes)
+        w_raw.append(load_w(1, words[:, 0 : 2 * 4 * PASS].bitcast(U32).rearrange("p (a r) -> p a r", a=2)))
+        c_raw.append(load_c(1, floats[:, 0]))
+        wc_raw = {}
+        for b in range(2):
+            for a in range(2):
+                wc_raw[b, a] = floats[:, 1 + 2 * b + a]
+                load_wc(wc_raw[b, a], b, a)
+        wd_words = words[:, 2 * 4 * PASS :]
+        nc.sync.dma_start(wd_words[:, 0 : 4 * N].bitcast(I32), wd8_words[0].rearrange("p n i -> p (n i)").bitcast(I32))
+        nc.sync.dma_start(wd_words[:, 4 * N : 6 * N].bitcast(I32), wd4_words[0].bitcast(I32))
+        res_sb = floats[:, 5]
+        nc.sync.dma_start(res_sb, res.rearrange("(n p) j -> p n j", p=P))
 
         t_codes = []
         w_codes = []
@@ -133,13 +145,6 @@ def tile_list_pnet_mix_res_kernel(
         gather_words(0, None)
         order_w(0)
         gather_words(1, "stage_d")
-        wc_raw = {}
-        trio = held([P, 3, PACK, PASS], F32, "wc_raw_trio", "stage_c")
-        for slot, (b, a) in enumerate(((0, 0), (0, 1), (1, 0))):
-            wc_raw[b, a] = trio[:, slot]
-            load_wc(wc_raw[b, a], b, a)
-        wc_raw[1, 1] = held([P, PACK, PASS], F32, "wc_raw11", "stage_d")[:]
-        load_wc(wc_raw[1, 1], 1, 1)
         order_w(1)
 
         pooled = {}
@@ -217,14 +222,14 @@ def tile_list_pnet_mix_res_kernel(
         for jt in range(PLAIN, NJT):
             open_banks[jt] = [neighbour_sum(0, jt, g, False) for g in range(2)]
 
-        wd_words = placed([P, 6 * N], U8, "wd_words", c_bytes)
-        nc.sync.dma_start(wd_words[:, 0 : 4 * N].bitcast(I32), wd8_words[0].rearrange("p n i -> p (n i)").bitcast(I32))
-        nc.sync.dma_start(wd_words[:, 4 * N : 6 * N].bitcast(I32), wd4_words[0].bitcast(I32))
-        res_sb = placed([P, 2, N // P, J // 2], F32, "res_sb", 0)
-        res_rows = res.rearrange("(n p) j -> p n j", p=P)
-        for jh in range(2):
-            nc.sync.dma_start(res_sb[:, jh], res_rows[:, :, (J // 2) * jh : (J // 2) * (jh + 1)])
-        c_q.append(prepare_c(1, ((round_on_vector, 0, groups),)))
+        c_bf1 = held([P, J * PACK], BF16, "c_bf1")
+        for jt in range(NJT):
+            nc.gpsimd.tensor_scalar(
+                c_bf1[:, TILE_W * jt : TILE_W * (jt + 1)].rearrange("p (j i) -> p j i", i=PACK),
+                c_raw[1][:, :, JT * jt : JT * (jt + 1)].rearrange("p i j -> p j i"),
+                1.0, 0.0, ALU.mult, ALU.add,
+            )
+        c_q.append(quantise(c_bf1[:], "c1"))
 
         wc_q = {}
         own = {}
@@ -312,11 +317,10 @@ def tile_list_pnet_mix_res_kernel(
 
         def add_residual_and_store(jt):
             result = held([P, N // P, JT], F32, "result%d" % jt)
-            first_point = JT * (jt % 2)
             nc.vector.tensor_tensor(
                 result[:],
                 y_bank[jt][:].rearrange("p (n j) -> p n j", j=JT),
-                res_sb[:, jt // 2, :, first_point : first_point + JT],
+                res_sb[:, :, JT * jt : JT * (jt + 1)],
                 ALU.add,
             )
             nc.sync.dma_start(out_rows[:, :, JT * jt : JT * (jt + 1)], result[:])

@@ -1,6 +1,7 @@
 from contextlib import ExitStack
 
 import concourse.mybir as mybir
+from concourse.masks import make_identity
 
 K, R, N, T, J = 1024, 1024, 512, 4096, 512
 FLOPS = 2 * K * R * 3 * J + 2 * R * N * J
@@ -16,23 +17,23 @@ FP4X4 = mybir.dt.float4_e2m1fn_x4
 ALU = mybir.AluOpType
 ACT = mybir.ActivationFunctionType
 
+KB = 1024
 P = 128
 PACK = 4
 PASS = P * PACK
 JT = 128
 NJT = J // JT
-TILE_W = PACK * JT
 LIST_GROUP = 16
 QUADRANT = 32
 ROWS = 4
-
 DENSE = P - 32
 W_AT = 2 * J
 WD_AT = W_AT + R
 ROW = WD_AT + N
-
 PLAIN = 2
-SPLIT_M = 96
+GROUPS = PASS // 4
+SCALAR_C = (64, 48)
+SCALAR_WC = (64, 64, 96, 64)
 
 
 def tile_list_pnet_mix_res_kernel(
@@ -44,14 +45,16 @@ def tile_list_pnet_mix_res_kernel(
         lists = ctx.enter_context(tc.tile_pool(name="lists", bufs=1))
         keep = ctx.enter_context(tc.tile_pool(name="keep", bufs=1))
         stage = ctx.enter_context(tc.tile_pool(name="stage", bufs=1))
-        ring = ctx.enter_context(tc.tile_pool(name="ring", bufs=3))
-        psum = ctx.enter_context(tc.psum_pool(name="psum", bufs=8))
+        psum = ctx.enter_context(tc.psum_pool(name="psum", bufs=1))
 
-        def held(shape, dtype, name, tag=None):
-            return keep.tile(shape, dtype, name=name, tag=tag or name, align_bytes=64)
+        def held(shape, dtype, name):
+            return keep.tile(shape, dtype, name=name, tag=name, align_bytes=64)
 
         def placed(shape, dtype, name, offset):
             return stage.tile(shape, dtype, name=name, tag=name, align_bytes=64, offset=offset)
+
+        def bank_tile(slot):
+            return psum.tile([P, PASS], F32, name="bank", tag="bank%d" % slot)
 
         def by_block(scales):
             return scales.rearrange("a q e -> q a e").bitcast(I32)
@@ -62,69 +65,43 @@ def tile_list_pnet_mix_res_kernel(
         tsc_win = held([P, T], U8, "tsc_win")
         nc.sync.dma_start(tsc_win[DENSE:P, :].bitcast(I32), by_block(tab_scales))
         nc.vector.memset(tsc_win[0:DENSE, :].bitcast(I32), 0)
-        wsc_raw = held([P, R], U8, "wsc_raw")
-        nc.sync.dma_start(wsc_raw[DENSE:P, :].bitcast(I32), by_block(w_scales))
-        nc.vector.memset(wsc_raw[0:DENSE, :].bitcast(I32), 0)
-        dense = held([P, ROW], U8, "dense")
+        dense = placed([P, ROW], U8, "dense", 52 * KB)
+        nc.sync.dma_start(dense[DENSE:P, W_AT:WD_AT].bitcast(I32), by_block(w_scales))
         for a, scales in enumerate((wd8_scales, wd4_scales)):
             nc.sync.dma_start(dense[DENSE + a : P : 2, WD_AT:ROW].bitcast(I32), scales[0].bitcast(I32))
-        tab = held([P, T], U32, "tab")
+        tab = placed([P, T], U32, "tab", 29 * KB)
         nc.sync.dma_start(tab[:].bitcast(I32), tab_words[0].rearrange("p e f -> p (e f)").bitcast(I32))
 
         w_flat = w_words.rearrange("a p r i -> p a (r i)")
 
         def load_w(b, raw):
-            nc.sync.dma_start(raw.bitcast(I32), w_flat[:, :, 4 * PASS * b : 4 * PASS * (b + 1)].bitcast(I32))
+            nc.sync.dma_start(raw[:].bitcast(I32), w_flat[:, :, 4 * PASS * b : 4 * PASS * (b + 1)].bitcast(I32))
             return raw
 
-        def load_c(a, raw):
-            nc.sync.dma_start(raw, c[PASS * a : PASS * (a + 1), :].rearrange("(p i) j -> p i j", i=PACK))
+        def load_rows(raw, rows):
+            nc.sync.dma_start(raw[:], rows.rearrange("(p i) x -> p i x", i=PACK))
             return raw
 
-        def load_wc(raw, b, a):
-            nc.sync.dma_start(
-                raw, wc[PASS * a : PASS * (a + 1), PASS * b : PASS * (b + 1)].rearrange("(p i) r -> p i r", i=PACK)
-            )
-
-        w_raw = [load_w(0, held([P, 2, PASS], U32, "w_raw0", "stage_d")[:])]
-        c_raw = [load_c(0, held([P, PACK, J], F32, "c_raw0")[:])]
+        w_codes = [load_w(0, held([P, 2, PASS], U32, "w_codes0"))]
 
         planes = held([P, 2 * ROW], U8, "planes")
-        nc.gpsimd.memset(planes[:].bitcast(I32), 0)
-        piece = PACK * PASS
-        float_bytes = 4 * 6 * piece
-        tsc_got = placed([P, 2 * J], U8, "tsc_got", float_bytes - J)
+        nc.vector.memset(planes[:].bitcast(I32), 0)
+        ident = held([P, P], F32, "ident")
+        make_identity(nc, ident[:])
+        tsc_got = placed([P, 2 * J], U8, "tsc_got", 15 * KB - J)
         nc.vector.tensor_copy(tsc_got[:], tsc_win[:].indirect(offsets[:]))
-        nc.vector.tensor_copy(
-            dense[:, W_AT:WD_AT].rearrange("p (b t m) -> p b t m", t=PACK, m=P),
-            wsc_raw[:].rearrange("p (b m t) -> p b t m", t=PACK, m=P),
-        )
         nc.vector.tensor_copy(dense[DENSE:P, 0:W_AT].bitcast(I32), tsc_got[DENSE:P, :].bitcast(I32))
         for quad in range(P // QUADRANT):
             nc.sync.dma_start(
                 planes[QUADRANT * quad : QUADRANT * quad + ROWS, :].bitcast(I32),
                 dense[DENSE + 2 * ROWS * quad : DENSE + 2 * ROWS * (quad + 1), :].bitcast(I32),
             )
-        floats = placed([P, 6, PACK, PASS], F32, "floats", 0)
-        words = placed([P, 2 * 4 * PASS + 6 * N], U8, "words", float_bytes)
-        w_raw.append(load_w(1, words[:, 0 : 2 * 4 * PASS].bitcast(U32).rearrange("p (a r) -> p a r", a=2)))
-        c_raw.append(load_c(1, floats[:, 0]))
-        wc_raw = {}
-        for b in range(2):
-            for a in range(2):
-                wc_raw[b, a] = floats[:, 1 + 2 * b + a]
-                load_wc(wc_raw[b, a], b, a)
-        wd_words = words[:, 2 * 4 * PASS :]
-        nc.sync.dma_start(wd_words[:, 0 : 4 * N].bitcast(I32), wd8_words[0].rearrange("p n i -> p (n i)").bitcast(I32))
-        nc.sync.dma_start(wd_words[:, 4 * N : 6 * N].bitcast(I32), wd4_words[0].bitcast(I32))
-        res_sb = floats[:, 5]
-        nc.sync.dma_start(res_sb, res.rearrange("(n p) j -> p n j", p=P))
+        c_raw = [load_rows(placed([P, PACK, J], F32, "c_raw0", 7 * KB), c[0:PASS, :])]
+        w_codes.append(load_w(1, placed([P, 2, PASS], U32, "w_codes1", 15 * KB)))
 
         t_codes = []
-        w_codes = []
 
-        def gather_words(g, tag):
-            got = held([P, J], U32, "t_got%d" % g, tag)
+        def gather_words(g, got):
             columns = J // LIST_GROUP
             nc.vector.tensor_copy(got[:], tab[:].indirect(offsets[:, g * columns : (g + 1) * columns]))
             parted = held([P, 2 * 2 * J], U8, "t_codes%d" % g)
@@ -134,59 +111,49 @@ def tile_list_pnet_mix_res_kernel(
             )
             t_codes.append(parted)
 
-        def order_w(b):
-            codes = held([P, 2 * PASS], U32, "w_codes%d" % b)
-            nc.vector.tensor_copy(
-                codes[:].rearrange("p (a u l m) -> p a u m l", a=2, u=2, l=2),
-                w_raw[b].rearrange("p a (m u l) -> p a u m l", u=2, l=2),
-            )
-            w_codes.append(codes)
-
-        gather_words(0, None)
-        order_w(0)
-        gather_words(1, "stage_d")
-        order_w(1)
+        gather_words(0, placed([P, J], U32, "t_got0", 20 * KB))
+        c_raw.append(load_rows(placed([P, PACK, J], F32, "c_raw1", 21 * KB), c[PASS : 2 * PASS, :]))
+        gather_words(1, placed([P, J], U32, "t_got1", 19 * KB))
+        wc_raw = {}
+        for b in range(2):
+            for a in range(2):
+                wc_raw[b, a] = load_rows(
+                    placed([P, PACK, PASS], F32, "wc_raw%d%d" % (b, a), (29 + 16 * b + 8 * a) * KB),
+                    wc[PASS * a : PASS * (a + 1), PASS * b : PASS * (b + 1)],
+                )
 
         pooled = {}
 
-        def by_point(view):
-            return view.rearrange("p (j t) -> p j t", t=PACK)
+        def by_pair(view):
+            return view.rearrange("p (u q e) -> p u q e", u=2, e=2)
 
-        def bank_by_point(bank):
-            return bank[:].rearrange("p (t j) -> p j t", t=PACK)
+        def bank_by_pair(bank):
+            return bank[:].rearrange("p (q u e) -> p u q e", u=2, e=2)
 
-        def neighbour_sum(b, jt, g, close):
-            bank = psum.tile([P, TILE_W], F32, name="nbr", tag="bank")
-            for t in range(PACK):
-                for a in range(2):
-                    col = PASS * a + P * t
-                    w_col = ROW * a + W_AT + PASS * b + P * t
-                    tab_col = ROW * a + J * g + JT * jt
-                    nc.tensor.matmul_mx(
-                        out=bank[:, JT * t : JT * (t + 1)],
-                        lhsT=w_codes[b][:, col : col + P].bitcast(FP8X4),
-                        lhsT_scale=planes[:, w_col : w_col + P],
-                        rhs=t_codes[g][:, 2 * (J * a + JT * jt) : 2 * (J * a + JT * (jt + 1))].bitcast(FP4X4),
-                        rhs_scale=planes[:, tab_col : tab_col + JT],
-                        start=(t == 0 and a == 0),
-                        stop=(close and t == PACK - 1 and a == 1),
-                    )
+        def neighbour_sum(b, jt, g, close, slot):
+            bank = bank_tile(slot)
+            for a in range(2):
+                tab_col = ROW * a + J * g + JT * jt
+                w_col = ROW * a + W_AT + PASS * b
+                nc.tensor.matmul_mx(
+                    out=bank[:],
+                    lhsT=t_codes[g][:, 2 * (J * a + JT * jt) : 2 * (J * a + JT * (jt + 1))].bitcast(FP4X4),
+                    lhsT_scale=planes[:, tab_col : tab_col + JT],
+                    rhs=w_codes[b][:, a, :].bitcast(FP8X4),
+                    rhs_scale=planes[:, w_col : w_col + PASS],
+                    start=(a == 0),
+                    stop=(close and a == 1),
+                )
             return bank
 
-        def pool_banks(banks, func, best):
-            first = ring.tile([P, TILE_W], F32, name="first", align_bytes=64)
-            nc.scalar.activation(by_point(first[:]), bank_by_point(banks[0]), func)
-            nc.vector.tensor_tensor(by_point(best), bank_by_point(banks[1]), by_point(first[:]), ALU.max)
+        def pool_banks(banks, func, best, name, offset):
+            first = placed([P, PASS], F32, name, offset)
+            nc.scalar.activation(by_pair(first[:]), bank_by_pair(banks[0]), func)
+            nc.vector.tensor_tensor(by_pair(best), bank_by_pair(banks[1]), by_pair(first[:]), ALU.max)
 
-        def pool_tile(b, jt, banks):
-            pooled[b, jt] = held([P, TILE_W], F32, "pooled%d%d" % (b, jt))
-            pool_banks(banks, ACT.Copy, pooled[b, jt][:])
-
-        def round_on_vector(dst, src):
-            nc.vector.tensor_copy(dst, src)
-
-        def round_on_scalar(dst, src):
-            nc.scalar.activation(dst, src, ACT.Copy)
+        def pool_tile(b, jt, banks, offset):
+            pooled[b, jt] = held([P, PASS], F32, "pooled%d%d" % (b, jt))
+            pool_banks(banks, ACT.Copy, pooled[b, jt][:], "first%d%d" % (b, jt), offset)
 
         def quantise(grouped, name):
             width = grouped.shape[1] // PACK
@@ -195,96 +162,105 @@ def tile_list_pnet_mix_res_kernel(
             nc.vector.quantize_mx(out=codes[:].bitcast(FP8X4), scales=plane[:], in_=grouped)
             return codes, plane
 
-        def prepare_c(a, shares):
-            grouped = held([P, J * PACK], BF16, "c_bf%d" % a)
+        def prepare(raw, name, split):
+            grouped = held([P, PASS * PACK], BF16, name + "_bf")
             dst = grouped[:].rearrange("p (x z i) -> p x i z", z=4, i=PACK)
-            src = c_raw[a].rearrange("p i (x z) -> p x i z", z=4)
-            for rounder, lo, hi in shares:
-                rounder(dst[:, lo:hi], src[:, lo:hi])
-            return quantise(grouped[:], "c%d" % a)
+            src = raw[:].rearrange("p i (x z) -> p x i z", z=4)
+            nc.scalar.activation(dst[:, 0:split], src[:, 0:split], ACT.Copy)
+            if split < GROUPS:
+                nc.vector.tensor_copy(dst[:, split:GROUPS], src[:, split:GROUPS])
+            return quantise(grouped[:], name)
 
-        def prepare_wc(b, a, shares):
-            grouped = held([P, PASS * PACK], BF16, "wc_bf%d%d" % (b, a))
-            dst = grouped[:].rearrange("p (u l m i) -> p u m i l", u=2, l=2, i=PACK)
-            src = wc_raw[b, a].rearrange("p i (m u l) -> p u m i l", u=2, l=2)
-            for rounder, u, lo, hi in shares:
-                rounder(dst[:, u, lo:hi], src[:, u, lo:hi])
-            return quantise(grouped[:], "wc%d%d" % (b, a))
-
-        groups = J // 4
-        c_q = [prepare_c(0, ((round_on_scalar, 0, groups // 2), (round_on_scalar, groups // 2, groups)))]
-        leading = [neighbour_sum(0, jt, 0, True) for jt in range(PLAIN)]
+        c_q = [prepare(c_raw[0], "c0", SCALAR_C[0])]
+        wd_words = placed([P, 6 * N], U8, "wd_words", 12 * KB)
+        nc.sync.dma_start(wd_words[:, 0 : 4 * N].bitcast(I32), wd8_words[0].rearrange("p n i -> p (n i)").bitcast(I32))
+        nc.sync.dma_start(wd_words[:, 4 * N : 6 * N].bitcast(I32), wd4_words[0].bitcast(I32))
+        res_sb = placed([P, N // P, J], F32, "res_sb", 0)
+        nc.sync.dma_start(res_sb[:], res.rearrange("(n p) j -> p n j", p=P))
+        leading = [neighbour_sum(0, jt, 0, jt < PLAIN, jt) for jt in range(NJT)]
         for jt in range(PLAIN):
-            pool_tile(0, jt, (leading[jt], neighbour_sum(0, jt, 1, True)))
-        for jt in range(NJT):
-            pool_tile(1, jt, [neighbour_sum(1, jt, g, True) for g in range(2)])
+            pool_tile(0, jt, (leading[jt], neighbour_sum(0, jt, 1, True, NJT + jt)), (8 + 2 * jt) * KB)
         open_banks = {}
         for jt in range(PLAIN, NJT):
-            open_banks[jt] = [neighbour_sum(0, jt, g, False) for g in range(2)]
-
-        c_bf1 = held([P, J * PACK], BF16, "c_bf1")
-        for jt in range(NJT):
-            nc.gpsimd.tensor_scalar(
-                c_bf1[:, TILE_W * jt : TILE_W * (jt + 1)].rearrange("p (j i) -> p j i", i=PACK),
-                c_raw[1][:, :, JT * jt : JT * (jt + 1)].rearrange("p i j -> p j i"),
-                1.0, 0.0, ALU.mult, ALU.add,
-            )
-        c_q.append(quantise(c_bf1[:], "c1"))
+            open_banks[jt] = [leading[jt], neighbour_sum(0, jt, 1, False, NJT + jt)]
+        c_q.append(prepare(c_raw[1], "c1", SCALAR_C[1]))
 
         wc_q = {}
         own = {}
 
         def own_pass(bank, b, jt, a, opens):
             codes, plane = wc_q[b, a]
-            for t in range(PACK):
-                nc.tensor.matmul_mx(
-                    out=bank[:, JT * t : JT * (t + 1)],
-                    lhsT=codes[:, P * t : P * (t + 1)].bitcast(FP8X4),
-                    lhsT_scale=plane[:, P * t : P * (t + 1)],
-                    rhs=c_q[a][0][:, JT * jt : JT * (jt + 1)].bitcast(FP8X4),
-                    rhs_scale=c_q[a][1][:, JT * jt : JT * (jt + 1)],
-                    start=(opens and t == 0),
-                    stop=(a == 1 and t == PACK - 1),
-                )
+            nc.tensor.matmul_mx(
+                out=bank[:],
+                lhsT=c_q[a][0][:, JT * jt : JT * (jt + 1)].bitcast(FP8X4),
+                lhsT_scale=c_q[a][1][:, JT * jt : JT * (jt + 1)],
+                rhs=codes[:].bitcast(FP8X4),
+                rhs_scale=plane[:],
+                start=opens,
+                stop=(a == 1),
+            )
 
-        def open_own(b, jt):
-            own[b, jt] = psum.tile([P, TILE_W], F32, name="own", tag="bank")
+        def open_own(b, jt, slot):
+            own[b, jt] = bank_tile(slot)
             own_pass(own[b, jt], b, jt, 0, True)
 
         def add_own(b, jt, summed):
             own_pass(own[b, jt], b, jt, 1, False)
-            nc.vector.tensor_tensor(by_point(summed), bank_by_point(own[b, jt]), by_point(pooled[b, jt][:]), ALU.add)
+            nc.vector.tensor_tensor(by_pair(summed), bank_by_pair(own[b, jt]), by_pair(pooled[b, jt][:]), ALU.add)
 
-        wc_q[0, 0] = prepare_wc(0, 0, [(round_on_scalar, u, 0, P) for u in range(2)])
-        wc_q[0, 1] = prepare_wc(0, 1, [(round_on_vector, u, 0, P) for u in range(2)])
-        wc_q[1, 0] = prepare_wc(1, 0, [(round_on_scalar, u, 0, P) for u in range(2)])
-        wc_q[1, 1] = prepare_wc(
-            1, 1, ((round_on_vector, 0, 0, SPLIT_M), (round_on_scalar, 1, 0, P), (round_on_scalar, 0, SPLIT_M, P))
-        )
+        def turn(tiles, slot):
+            bank = bank_tile(slot)
+            width = JT * len(tiles)
+            for x, rows in enumerate(tiles):
+                for u in range(2):
+                    at = width * u + JT * x
+                    nc.tensor.transpose(bank[:, at : at + JT], rows.bitcast(F32)[:, P * u : P * (u + 1)], ident[:])
+            return bank[:, 0 : 2 * width]
 
-        summed0 = held([P, PLAIN * TILE_W], BF16, "summed0")
-        hidden0 = held([P, NJT * TILE_W], BF16, "hidden0")
-        for jt in range(PLAIN):
-            open_own(0, jt)
+        def relu_out(turned, hidden):
+            nc.scalar.activation(
+                hidden.rearrange("p (j u e) -> p j u e", u=2, e=2),
+                turned.bitcast(BF16).rearrange("p (u j e) -> p j u e", u=2, e=2),
+                ACT.Relu,
+            )
+
+        wc_q[0, 0] = prepare(wc_raw[0, 0], "wc00", SCALAR_WC[0])
+        for jt in range(2):
+            pool_tile(1, jt, [neighbour_sum(1, jt, g, True, jt + NJT * g) for g in range(2)], (29 + 2 * jt) * KB)
+        wc_q[0, 1] = prepare(wc_raw[0, 1], "wc01", SCALAR_WC[1])
+        pool_tile(1, 2, [neighbour_sum(1, 2, g, True, NJT * g) for g in range(2)], 37 * KB)
+
+        summed0 = [held([P, PASS], BF16, "summed0%d" % jt) for jt in range(NJT)]
         for jt in range(PLAIN, NJT):
             for bank in open_banks[jt]:
                 own_pass(bank, 0, jt, 0, False)
         for jt in range(PLAIN):
-            add_own(0, jt, summed0[:, TILE_W * jt : TILE_W * (jt + 1)])
-        nc.vector.tensor_scalar_max(hidden0[:, 0 : PLAIN * TILE_W], summed0[:], 0.0)
+            open_own(0, jt, 1 + NJT * jt)
+        for jt in range(PLAIN):
+            add_own(0, jt, summed0[jt][:])
+        wc_q[1, 0] = prepare(wc_raw[1, 0], "wc10", SCALAR_WC[2])
         for jt in range(PLAIN, NJT):
             for bank in open_banks[jt]:
                 own_pass(bank, 0, jt, 1, False)
-            pool_banks(open_banks[jt], ACT.Relu, hidden0[:, TILE_W * jt : TILE_W * (jt + 1)])
+            pool_banks(open_banks[jt], ACT.Relu, summed0[jt][:], "first0%d" % jt, (41 + 2 * jt) * KB)
+        pool_tile(1, 3, [neighbour_sum(1, 3, g, True, 1 + NJT * g) for g in range(2)], 49 * KB)
+        wc_q[1, 1] = prepare(wc_raw[1, 1], "wc11", SCALAR_WC[3])
+        hidden0 = placed([P, NJT * PASS], BF16, "hidden0", 55 * KB)
+        relu_out(turn([summed0[jt][:] for jt in range(PLAIN)], 0), hidden0[:, 0 : PLAIN * PASS])
+        nc.scalar.copy(
+            hidden0[:, PLAIN * PASS :].bitcast(F32).rearrange("p (j u) -> p j u", u=2),
+            turn([summed0[jt][:] for jt in range(PLAIN, NJT)], NJT).rearrange("p (u j) -> p j u", u=2),
+        )
         h0_codes, h0_plane = quantise(hidden0[:], "h0")
 
+        own_slots = (2, 6, 3, 7)
         for jt in range(NJT):
-            open_own(1, jt)
+            open_own(1, jt, own_slots[jt])
         out_rows = out.rearrange("(n p) j -> p n j", p=P)
         hidden1 = {}
         y_bank = {}
-        for jt in range(NJT):
-            y_bank[jt] = psum.tile([P, (N // P) * JT], F32, name="y_bank", tag="bank")
+        for jt, slot in enumerate((0, 4, 1, 5)):
+            y_bank[jt] = bank_tile(slot)
             for n in range(N // P):
                 nc.tensor.matmul_mx(
                     out=y_bank[jt][:, JT * n : JT * (n + 1)],
@@ -297,10 +273,10 @@ def tile_list_pnet_mix_res_kernel(
                 )
 
         def end_first_layer(jt):
-            summed = held([P, TILE_W], BF16, "summed1%d" % jt)
+            summed = held([P, PASS], BF16, "summed1%d" % jt)
             add_own(1, jt, summed[:])
-            hidden1[jt] = held([P, TILE_W], BF16, "hidden1%d" % jt)
-            nc.scalar.activation(hidden1[jt][:], summed[:], ACT.Relu)
+            hidden1[jt] = held([P, PASS], BF16, "hidden1%d" % jt)
+            relu_out(turn([summed[:]], own_slots[jt]), hidden1[jt][:])
 
         def end_second_layer(jt):
             h1_codes, h1_plane = quantise(hidden1[jt][:], "h1%d" % jt)

@@ -28,8 +28,6 @@ QUADRANT = 32
 ROWS = 4
 DENSE = P - 32
 W_AT = 2 * J
-WD_AT = W_AT + R
-ROW = WD_AT + N
 PLAIN = 2
 GROUPS = PASS // 4
 SCALAR_C = (64, 48)
@@ -59,18 +57,32 @@ def tile_list_pnet_mix_res_kernel(
         def by_block(scales):
             return scales.rearrange("a q e -> q a e").bitcast(I32)
 
+        def move_rows(target, rows):
+            for quad in (0, 2, 1, 3):
+                nc.sync.dma_start(
+                    target[QUADRANT * quad : QUADRANT * quad + ROWS, :].bitcast(I32),
+                    rows[DENSE + 2 * ROWS * quad : DENSE + 2 * ROWS * (quad + 1), :].bitcast(I32),
+                )
+
         offsets = lists.tile([P, 2 * J // LIST_GROUP], U16, name="offsets")
         nc.sync.dma_start(offsets[:], offs)
 
-        tsc_win = held([P, T], U8, "tsc_win")
+        tsc_win = placed([P, T], U8, "tsc_win", 13 * KB)
         nc.sync.dma_start(tsc_win[DENSE:P, :].bitcast(I32), by_block(tab_scales))
         nc.vector.memset(tsc_win[0:DENSE, :].bitcast(I32), 0)
-        dense = placed([P, ROW], U8, "dense", 52 * KB)
-        nc.sync.dma_start(dense[DENSE:P, W_AT:WD_AT].bitcast(I32), by_block(w_scales))
+        wd_dense = held([P, N], U8, "wd_dense")
         for a, scales in enumerate((wd8_scales, wd4_scales)):
-            nc.sync.dma_start(dense[DENSE + a : P : 2, WD_AT:ROW].bitcast(I32), scales[0].bitcast(I32))
+            nc.sync.dma_start(wd_dense[DENSE + a : P : 2, :].bitcast(I32), scales[0].bitcast(I32))
         tab = placed([P, T], U32, "tab", 29 * KB)
         nc.sync.dma_start(tab[:].bitcast(I32), tab_words[0].rearrange("p e f -> p (e f)").bitcast(I32))
+
+        planes = held([P, 2 * W_AT + 2 * R], U8, "planes")
+        nc.vector.memset(planes[:].bitcast(I32), 0)
+        for s in range(ROWS):
+            nc.sync.dma_start(
+                planes[s:P:QUADRANT, 2 * W_AT :].bitcast(I32),
+                w_scales[:, s : 4 * ROWS : ROWS, :].rearrange("a d e -> d a e").bitcast(I32),
+            )
 
         w_flat = w_words.rearrange("a p r i -> p a (r i)")
 
@@ -84,18 +96,11 @@ def tile_list_pnet_mix_res_kernel(
 
         w_codes = [load_w(0, held([P, 2, PASS], U32, "w_codes0"))]
 
-        planes = held([P, 2 * ROW], U8, "planes")
-        nc.vector.memset(planes[:].bitcast(I32), 0)
         ident = held([P, P], F32, "ident")
         make_identity(nc, ident[:])
-        tsc_got = placed([P, 2 * J], U8, "tsc_got", 15 * KB - J)
+        tsc_got = placed([P, 2 * J], U8, "tsc_got", 53 * KB - J)
         nc.vector.tensor_copy(tsc_got[:], tsc_win[:].indirect(offsets[:]))
-        nc.vector.tensor_copy(dense[DENSE:P, 0:W_AT].bitcast(I32), tsc_got[DENSE:P, :].bitcast(I32))
-        for quad in range(P // QUADRANT):
-            nc.sync.dma_start(
-                planes[QUADRANT * quad : QUADRANT * quad + ROWS, :].bitcast(I32),
-                dense[DENSE + 2 * ROWS * quad : DENSE + 2 * ROWS * (quad + 1), :].bitcast(I32),
-            )
+        move_rows(planes[:, 0 : 2 * W_AT], tsc_got)
         c_raw = [load_rows(placed([P, PACK, J], F32, "c_raw0", 7 * KB), c[0:PASS, :])]
         w_codes.append(load_w(1, placed([P, 2, PASS], U32, "w_codes1", 15 * KB)))
 
@@ -133,8 +138,8 @@ def tile_list_pnet_mix_res_kernel(
         def neighbour_sum(b, jt, g, close, slot):
             bank = bank_tile(slot)
             for a in range(2):
-                tab_col = ROW * a + J * g + JT * jt
-                w_col = ROW * a + W_AT + PASS * b
+                tab_col = W_AT * a + J * g + JT * jt
+                w_col = 2 * W_AT + R * a + PASS * b
                 nc.tensor.matmul_mx(
                     out=bank[:],
                     lhsT=t_codes[g][:, 2 * (J * a + JT * jt) : 2 * (J * a + JT * (jt + 1))].bitcast(FP4X4),
@@ -162,8 +167,11 @@ def tile_list_pnet_mix_res_kernel(
             nc.vector.quantize_mx(out=codes[:].bitcast(FP8X4), scales=plane[:], in_=grouped)
             return codes, plane
 
+        rounded = []
+
         def prepare(raw, name, split):
-            grouped = held([P, PASS * PACK], BF16, name + "_bf")
+            grouped = placed([P, PASS * PACK], BF16, name + "_bf", (69 + 4 * len(rounded)) * KB)
+            rounded.append(grouped)
             dst = grouped[:].rearrange("p (x z i) -> p x i z", z=4, i=PACK)
             src = raw[:].rearrange("p i (x z) -> p x i z", z=4)
             nc.scalar.activation(dst[:, 0:split], src[:, 0:split], ACT.Copy)
@@ -172,10 +180,13 @@ def tile_list_pnet_mix_res_kernel(
             return quantise(grouped[:], name)
 
         c_q = [prepare(c_raw[0], "c0", SCALAR_C[0])]
+        wd_planes = placed([P, 2 * N], U8, "wd_planes", 7 * KB)
+        nc.vector.memset(wd_planes[:].bitcast(I32), 0)
+        move_rows(wd_planes[:], wd_dense)
         wd_words = placed([P, 6 * N], U8, "wd_words", 12 * KB)
         nc.sync.dma_start(wd_words[:, 0 : 4 * N].bitcast(I32), wd8_words[0].rearrange("p n i -> p (n i)").bitcast(I32))
         nc.sync.dma_start(wd_words[:, 4 * N : 6 * N].bitcast(I32), wd4_words[0].bitcast(I32))
-        res_sb = placed([P, N // P, J], F32, "res_sb", 0)
+        res_sb = placed([P, N // P, J], F32, "res_sb", 62 * KB)
         nc.sync.dma_start(res_sb[:], res.rearrange("(n p) j -> p n j", p=P))
         leading = [neighbour_sum(0, jt, 0, jt < PLAIN, jt) for jt in range(NJT)]
         for jt in range(PLAIN):
@@ -265,7 +276,7 @@ def tile_list_pnet_mix_res_kernel(
                 nc.tensor.matmul_mx(
                     out=y_bank[jt][:, JT * n : JT * (n + 1)],
                     lhsT=wd_words[:, 4 * P * n : 4 * P * (n + 1)].bitcast(FP8X4),
-                    lhsT_scale=planes[:, WD_AT + P * n : WD_AT + P * (n + 1)],
+                    lhsT_scale=wd_planes[:, P * n : P * (n + 1)],
                     rhs=h0_codes[:, JT * jt : JT * (jt + 1)].bitcast(FP8X4),
                     rhs_scale=h0_plane[:, JT * jt : JT * (jt + 1)],
                     start=(n == 0),
@@ -284,7 +295,7 @@ def tile_list_pnet_mix_res_kernel(
                 nc.tensor.matmul_mx(
                     out=y_bank[jt][:, JT * n : JT * (n + 1)],
                     lhsT=wd_words[:, 4 * N + 2 * P * n : 4 * N + 2 * P * (n + 1)].bitcast(FP4X4),
-                    lhsT_scale=planes[:, ROW + WD_AT + P * n : ROW + WD_AT + P * (n + 1)],
+                    lhsT_scale=wd_planes[:, N + P * n : N + P * (n + 1)],
                     rhs=h1_codes[:].bitcast(FP8X4),
                     rhs_scale=h1_plane[:],
                     start=False,

@@ -31,7 +31,7 @@ W_AT = 2 * J
 PLAIN = 2
 GROUPS = PASS // 4
 SCALAR_C = (64, 48)
-SCALAR_WC = (64, 64, 96, 64)
+SCALAR_WC = (64, 48, 128, 64)
 
 
 def tile_list_pnet_mix_res_kernel(
@@ -156,8 +156,9 @@ def tile_list_pnet_mix_res_kernel(
             nc.scalar.activation(by_pair(first[:]), bank_by_pair(banks[0]), func)
             nc.vector.tensor_tensor(by_pair(best), bank_by_pair(banks[1]), by_pair(first[:]), ALU.max)
 
-        def pool_tile(b, jt, banks, offset):
-            pooled[b, jt] = held([P, PASS], F32, "pooled%d%d" % (b, jt))
+        def pool_tile(b, jt, banks, offset, at=None):
+            name = "pooled%d%d" % (b, jt)
+            pooled[b, jt] = held([P, PASS], F32, name) if at is None else placed([P, PASS], F32, name, at)
             pool_banks(banks, ACT.Copy, pooled[b, jt][:], "first%d%d" % (b, jt), offset)
 
         def quantise(grouped, name):
@@ -216,7 +217,6 @@ def tile_list_pnet_mix_res_kernel(
             own_pass(own[b, jt], b, jt, 0, True)
 
         def add_own(b, jt, summed):
-            own_pass(own[b, jt], b, jt, 1, False)
             nc.vector.tensor_tensor(by_pair(summed), bank_by_pair(own[b, jt]), by_pair(pooled[b, jt][:]), ALU.add)
 
         def turn(tiles, slot):
@@ -235,50 +235,65 @@ def tile_list_pnet_mix_res_kernel(
                 ACT.Relu,
             )
 
-        wc_q[0, 0] = prepare(wc_raw[0, 0], "wc00", SCALAR_WC[0])
+        def pool_second(jt, offset, at=None):
+            pool_tile(1, jt, [neighbour_sum(1, jt, g, True, jt % 2 + NJT * g) for g in range(2)], offset, at)
+
         for jt in range(2):
-            pool_tile(1, jt, [neighbour_sum(1, jt, g, True, jt + NJT * g) for g in range(2)], (29 + 2 * jt) * KB)
+            pool_second(jt, (21 + 2 * jt) * KB)
+        wc_q[0, 0] = prepare(wc_raw[0, 0], "wc00", SCALAR_WC[0])
+        pool_second(2, 29 * KB)
         wc_q[0, 1] = prepare(wc_raw[0, 1], "wc01", SCALAR_WC[1])
-        pool_tile(1, 2, [neighbour_sum(1, 2, g, True, NJT * g) for g in range(2)], 37 * KB)
+        pool_second(3, 31 * KB, 81 * KB)
 
         summed0 = [held([P, PASS], BF16, "summed0%d" % jt) for jt in range(NJT)]
         for jt in range(PLAIN, NJT):
             for bank in open_banks[jt]:
                 own_pass(bank, 0, jt, 0, False)
         for jt in range(PLAIN):
-            open_own(0, jt, 1 + NJT * jt)
+            open_own(0, jt, NJT * jt)
         for jt in range(PLAIN):
+            own_pass(own[0, jt], 0, jt, 1, False)
             add_own(0, jt, summed0[jt][:])
-        wc_q[1, 0] = prepare(wc_raw[1, 0], "wc10", SCALAR_WC[2])
         for jt in range(PLAIN, NJT):
             for bank in open_banks[jt]:
                 own_pass(bank, 0, jt, 1, False)
-            pool_banks(open_banks[jt], ACT.Relu, summed0[jt][:], "first0%d" % jt, (41 + 2 * jt) * KB)
-        pool_tile(1, 3, [neighbour_sum(1, 3, g, True, 1 + NJT * g) for g in range(2)], 49 * KB)
-        wc_q[1, 1] = prepare(wc_raw[1, 1], "wc11", SCALAR_WC[3])
-        hidden0 = placed([P, NJT * PASS], BF16, "hidden0", 55 * KB)
-        relu_out(turn([summed0[jt][:] for jt in range(PLAIN)], 0), hidden0[:, 0 : PLAIN * PASS])
-        nc.scalar.copy(
-            hidden0[:, PLAIN * PASS :].bitcast(F32).rearrange("p (j u) -> p j u", u=2),
-            turn([summed0[jt][:] for jt in range(PLAIN, NJT)], NJT).rearrange("p (u j) -> p j u", u=2),
-        )
-        h0_codes, h0_plane = quantise(hidden0[:], "h0")
-
-        own_slots = (2, 6, 3, 7)
-        for jt in range(NJT):
+        wc_q[1, 0] = prepare(wc_raw[1, 0], "wc10", SCALAR_WC[2])
+        own_slots = (1, 5, 4, 0)
+        last = NJT - 1
+        for jt in range(last):
             open_own(1, jt, own_slots[jt])
+        turned = turn([summed0[jt][:] for jt in range(PLAIN)], 0)
+        wc_q[1, 1] = prepare(wc_raw[1, 1], "wc11", SCALAR_WC[3])
+        for jt in range(last):
+            own_pass(own[1, jt], 1, jt, 1, False)
+        hidden0 = [placed([P, 2 * PASS], BF16, "hidden00", 57 * KB), held([P, 2 * PASS], BF16, "hidden01")]
+        relu_out(turned, hidden0[0][:])
+        open_own(1, last, own_slots[last])
+        own_pass(own[1, last], 1, last, 1, False)
+        h0_q = [quantise(hidden0[0][:], "h00")]
+        for jt in range(PLAIN, NJT):
+            pool_banks(open_banks[jt], ACT.Relu, summed0[jt][:], "first0%d" % jt, (49 + 2 * jt) * KB)
+
+        def finish_doubled():
+            nc.scalar.copy(
+                hidden0[1][:].bitcast(F32).rearrange("p (j u) -> p j u", u=2),
+                turn([summed0[jt][:] for jt in range(PLAIN, NJT)], 3).rearrange("p (u j) -> p j u", u=2),
+            )
+            h0_q.append(quantise(hidden0[1][:], "h01"))
+
         out_rows = out.rearrange("(n p) j -> p n j", p=P)
         hidden1 = {}
         y_bank = {}
-        for jt, slot in enumerate((0, 4, 1, 5)):
-            y_bank[jt] = bank_tile(slot)
+
+        def open_second_layer(jt):
+            y_bank[jt] = bank_tile((6, 7, 2, 3)[jt])
             for n in range(N // P):
                 nc.tensor.matmul_mx(
                     out=y_bank[jt][:, JT * n : JT * (n + 1)],
                     lhsT=wd_words[:, 4 * P * n : 4 * P * (n + 1)].bitcast(FP8X4),
                     lhsT_scale=wd_planes[:, P * n : P * (n + 1)],
-                    rhs=h0_codes[:, JT * jt : JT * (jt + 1)].bitcast(FP8X4),
-                    rhs_scale=h0_plane[:, JT * jt : JT * (jt + 1)],
+                    rhs=h0_q[jt // 2][0][:, JT * (jt % 2) : JT * (jt % 2 + 1)].bitcast(FP8X4),
+                    rhs_scale=h0_q[jt // 2][1][:, JT * (jt % 2) : JT * (jt % 2 + 1)],
                     start=(n == 0),
                     stop=False,
                 )
@@ -290,6 +305,7 @@ def tile_list_pnet_mix_res_kernel(
             relu_out(turn([summed[:]], own_slots[jt]), hidden1[jt][:])
 
         def end_second_layer(jt):
+            open_second_layer(jt)
             h1_codes, h1_plane = quantise(hidden1[jt][:], "h1%d" % jt)
             for n in range(N // P):
                 nc.tensor.matmul_mx(
@@ -315,6 +331,8 @@ def tile_list_pnet_mix_res_kernel(
         for step in range(NJT + 2):
             if step < NJT:
                 end_first_layer(step)
+            if step == 1:
+                finish_doubled()
             if 1 <= step <= NJT:
                 end_second_layer(step - 1)
             if step >= 2:

@@ -21,17 +21,16 @@ KB = 1024
 P = 128
 PACK = 4
 PASS = P * PACK
+HALF = PASS // 2
 JT = 128
 NJT = J // JT
 LIST_GROUP = 16
 QUADRANT = 32
 ROWS = 4
 DENSE = P - 32
-W_AT = 2 * J
-PLAIN = 2
-GROUPS = PASS // 4
-SCALAR_C = (64, 48)
-SCALAR_WC = (64, 48, 128, 64)
+SHARE_C = ((0, 0), (80, 48))
+SHARE_WC = ((80, 48), (76, 52), (76, 52))
+SHARE_LAST = ((64, 0), (40, 24))
 
 
 def tile_list_pnet_mix_res_kernel(
@@ -54,9 +53,6 @@ def tile_list_pnet_mix_res_kernel(
         def bank_tile(slot):
             return psum.tile([P, PASS], F32, name="bank", tag="bank%d" % slot)
 
-        def by_block(scales):
-            return scales.rearrange("a q e -> q a e").bitcast(I32)
-
         def move_rows(target, rows):
             for quad in (0, 2, 1, 3):
                 nc.sync.dma_start(
@@ -64,45 +60,43 @@ def tile_list_pnet_mix_res_kernel(
                     rows[DENSE + 2 * ROWS * quad : DENSE + 2 * ROWS * (quad + 1), :].bitcast(I32),
                 )
 
-        offsets = lists.tile([P, 2 * J // LIST_GROUP], U16, name="offsets")
-        nc.sync.dma_start(offsets[:], offs)
-
-        tsc_win = placed([P, T], U8, "tsc_win", 13 * KB)
-        nc.sync.dma_start(tsc_win[DENSE:P, :].bitcast(I32), by_block(tab_scales))
-        nc.vector.memset(tsc_win[0:DENSE, :].bitcast(I32), 0)
-        wd_dense = held([P, N], U8, "wd_dense")
-        for a, scales in enumerate((wd8_scales, wd4_scales)):
-            nc.sync.dma_start(wd_dense[DENSE + a : P : 2, :].bitcast(I32), scales[0].bitcast(I32))
-        tab = placed([P, T], U32, "tab", 29 * KB)
-        nc.sync.dma_start(tab[:].bitcast(I32), tab_words[0].rearrange("p e f -> p (e f)").bitcast(I32))
-
-        planes = held([P, 2 * W_AT + 2 * R], U8, "planes")
-        nc.vector.memset(planes[:].bitcast(I32), 0)
-        for s in range(ROWS):
-            nc.sync.dma_start(
-                planes[s:P:QUADRANT, 2 * W_AT :].bitcast(I32),
-                w_scales[:, s : 4 * ROWS : ROWS, :].rearrange("a d e -> d a e").bitcast(I32),
-            )
-
-        w_flat = w_words.rearrange("a p r i -> p a (r i)")
-
-        def load_w(b, raw):
-            nc.sync.dma_start(raw[:].bitcast(I32), w_flat[:, :, 4 * PASS * b : 4 * PASS * (b + 1)].bitcast(I32))
-            return raw
-
         def load_rows(raw, rows):
             nc.sync.dma_start(raw[:], rows.rearrange("(p i) x -> p i x", i=PACK))
             return raw
 
-        w_codes = [load_w(0, held([P, 2, PASS], U32, "w_codes0"))]
+        offsets = lists.tile([P, 2 * J // LIST_GROUP], U16, name="offsets")
+        nc.sync.dma_start(offsets[:], offs)
+        tsc_win = placed([P, T], U8, "tsc_win", 7 * KB)
+        nc.sync.dma_start(tsc_win[DENSE:P, :].bitcast(I32), tab_scales.rearrange("a q e -> q a e").bitcast(I32))
+        nc.vector.memset(tsc_win[0:DENSE, :].bitcast(I32), 0)
+        wd_dense = held([P, N], U8, "wd_dense")
+        for a, scales in enumerate((wd8_scales, wd4_scales)):
+            nc.sync.dma_start(wd_dense[DENSE + a : P : 2, :].bitcast(I32), scales[0].bitcast(I32))
+        tab = placed([P, T], U32, "tab", 32 * KB)
+        nc.sync.dma_start(tab[:].bitcast(I32), tab_words[0].rearrange("p e f -> p (e f)").bitcast(I32))
+        w_flat = w_words.rearrange("a p r i -> p a (r i)")
+        w_first = held([P, 2, PASS], U32, "w_codes0")
+        nc.sync.dma_start(w_first[:].bitcast(I32), w_flat[:, :, 0 : 4 * PASS].bitcast(I32))
+        w_codes = {(0, a): w_first[:, a, :] for a in range(2)}
 
+        w_planes = held([P, 2 * R], U8, "w_planes")
+        nc.gpsimd.memset(w_planes[:].bitcast(I32), 0)
+        for s in range(ROWS):
+            (nc.sync if s == ROWS - 1 else nc.gpsimd).dma_start(
+                w_planes[s:P:QUADRANT, :].bitcast(I32),
+                w_scales[:, s : 4 * ROWS : ROWS, :].rearrange("a d e -> d a e").bitcast(I32),
+            )
         ident = held([P, P], F32, "ident")
         make_identity(nc, ident[:])
-        tsc_got = placed([P, 2 * J], U8, "tsc_got", 53 * KB - J)
+
+        t_planes = held([P, 4 * J], U8, "t_planes")
+        nc.vector.memset(t_planes[:].bitcast(I32), 0)
+        tsc_got = placed([P, 2 * J], U8, "tsc_got", 24 * KB)
         nc.vector.tensor_copy(tsc_got[:], tsc_win[:].indirect(offsets[:]))
-        move_rows(planes[:, 0 : 2 * W_AT], tsc_got)
-        c_raw = [load_rows(placed([P, PACK, J], F32, "c_raw0", 7 * KB), c[0:PASS, :])]
-        w_codes.append(load_w(1, placed([P, 2, PASS], U32, "w_codes1", 15 * KB)))
+        move_rows(t_planes[:], tsc_got)
+
+        c_raw = [load_rows(placed([P, PACK, J], F32, "c_raw0", 0), c[0:PASS, :])]
+        c_raw.append(load_rows(placed([P, PACK, J], F32, "c_raw1", 8 * KB), c[PASS : 2 * PASS, :]))
 
         t_codes = []
 
@@ -116,18 +110,18 @@ def tile_list_pnet_mix_res_kernel(
             )
             t_codes.append(parted)
 
-        gather_words(0, placed([P, J], U32, "t_got0", 20 * KB))
-        c_raw.append(load_rows(placed([P, PACK, J], F32, "c_raw1", 21 * KB), c[PASS : 2 * PASS, :]))
-        gather_words(1, placed([P, J], U32, "t_got1", 19 * KB))
+        gather_words(0, placed([P, J], U32, "t_got0", 17 * KB + 512))
+        w_second = placed([P, 2, PASS], U32, "w_codes1", 19 * KB)
+        nc.sync.dma_start(w_second[:].bitcast(I32), w_flat[:, :, 4 * PASS : 8 * PASS].bitcast(I32))
+        for a in range(2):
+            w_codes[1, a] = w_second[:, a, :]
+        gather_words(1, placed([P, J], U32, "t_got1", 16 * KB))
         wc_raw = {}
-        for b in range(2):
-            for a in range(2):
-                wc_raw[b, a] = load_rows(
-                    placed([P, PACK, PASS], F32, "wc_raw%d%d" % (b, a), (29 + 16 * b + 8 * a) * KB),
-                    wc[PASS * a : PASS * (a + 1), PASS * b : PASS * (b + 1)],
-                )
-
-        pooled = {}
+        for b, a in ((0, 0), (0, 1), (1, 0)):
+            wc_raw[b, a] = load_rows(
+                placed([P, PACK, PASS], F32, "wc_raw%d%d" % (b, a), (28 + 16 * b + 8 * a) * KB),
+                wc[PASS * a : PASS * (a + 1), PASS * b : PASS * (b + 1)],
+            )
 
         def by_pair(view):
             return view.rearrange("p (u q e) -> p u q e", u=2, e=2)
@@ -135,98 +129,112 @@ def tile_list_pnet_mix_res_kernel(
         def bank_by_pair(bank):
             return bank[:].rearrange("p (q u e) -> p u q e", u=2, e=2)
 
-        def neighbour_sum(b, jt, g, close, slot):
+        def neighbour_sum(b, jt, g, slot):
             bank = bank_tile(slot)
             for a in range(2):
-                tab_col = W_AT * a + J * g + JT * jt
-                w_col = 2 * W_AT + R * a + PASS * b
+                tab_col = 2 * J * a + J * g + JT * jt
+                w_col = R * a + PASS * b
                 nc.tensor.matmul_mx(
                     out=bank[:],
                     lhsT=t_codes[g][:, 2 * (J * a + JT * jt) : 2 * (J * a + JT * (jt + 1))].bitcast(FP4X4),
-                    lhsT_scale=planes[:, tab_col : tab_col + JT],
-                    rhs=w_codes[b][:, a, :].bitcast(FP8X4),
-                    rhs_scale=planes[:, w_col : w_col + PASS],
+                    lhsT_scale=t_planes[:, tab_col : tab_col + JT],
+                    rhs=w_codes[b, a].bitcast(FP8X4),
+                    rhs_scale=w_planes[:, w_col : w_col + PASS],
                     start=(a == 0),
-                    stop=(close and a == 1),
+                    stop=(a == 1),
                 )
             return bank
 
-        def pool_banks(banks, func, best, name, offset):
-            first = placed([P, PASS], F32, name, offset)
-            nc.scalar.activation(by_pair(first[:]), bank_by_pair(banks[0]), func)
-            nc.vector.tensor_tensor(by_pair(best), bank_by_pair(banks[1]), by_pair(first[:]), ALU.max)
+        first = {}
 
-        def pool_tile(b, jt, banks, offset, at=None):
-            name = "pooled%d%d" % (b, jt)
-            pooled[b, jt] = held([P, PASS], F32, name) if at is None else placed([P, PASS], F32, name, at)
-            pool_banks(banks, ACT.Copy, pooled[b, jt][:], "first%d%d" % (b, jt), offset)
+        first_at = {(0, 0): 84, (0, 1): 86, (0, 2): 88, (0, 3): 90, (1, 0): 64, (1, 1): 92, (1, 2): 32, (1, 3): 36}
 
-        def quantise(grouped, name):
+        def copy_first(b, jt, bank):
+            first[b, jt] = placed([P, PASS], F32, "first%d%d" % (b, jt), first_at[b, jt] * KB)
+            nc.scalar.activation(by_pair(first[b, jt][:]), bank_by_pair(bank), ACT.Copy)
+
+        def second_sum(b, jt, slot, best):
+            nc.vector.tensor_tensor(best, bank_by_pair(neighbour_sum(b, jt, 1, slot)), by_pair(first[b, jt][:]), ALU.max)
+
+        def quantise(grouped, name, at=None):
             width = grouped.shape[1] // PACK
-            codes = held([P, width], U32, name + "_codes")
+            if at is None:
+                codes = held([P, width], U32, name + "_codes")
+            else:
+                codes = placed([P, width], U32, name + "_codes", at)
             plane = held([P, width], U8, name + "_plane")
             nc.vector.quantize_mx(out=codes[:].bitcast(FP8X4), scales=plane[:], in_=grouped)
             return codes, plane
 
-        rounded = []
-
-        def prepare(raw, name, split):
-            grouped = placed([P, PASS * PACK], BF16, name + "_bf", (69 + 4 * len(rounded)) * KB)
-            rounded.append(grouped)
+        def prepare(raw, name, share, at=None):
+            width = raw.shape[2]
+            shape = [P, width * PACK]
+            grouped = held(shape, BF16, name + "_bf") if at is None else placed(shape, BF16, name + "_bf", at)
             dst = grouped[:].rearrange("p (x z i) -> p x i z", z=4, i=PACK)
             src = raw[:].rearrange("p i (x z) -> p x i z", z=4)
-            nc.scalar.activation(dst[:, 0:split], src[:, 0:split], ACT.Copy)
-            if split < GROUPS:
-                nc.vector.tensor_copy(dst[:, split:GROUPS], src[:, split:GROUPS])
+            split, rest = share[0], share[0] + share[1]
+            if split > 0:
+                nc.scalar.activation(dst[:, 0:split], src[:, 0:split], ACT.Copy)
+            if rest > split:
+                nc.gpsimd.tensor_scalar(
+                    grouped[:].rearrange("p (x i) -> p x i", i=PACK)[:, 4 * split : 4 * rest],
+                    raw[:].rearrange("p i x -> p x i")[:, 4 * split : 4 * rest],
+                    1.0, 0.0, ALU.mult, ALU.add,
+                )
+            if rest < width // 4:
+                nc.vector.tensor_copy(dst[:, rest : width // 4], src[:, rest : width // 4])
             return quantise(grouped[:], name)
 
-        c_q = [prepare(c_raw[0], "c0", SCALAR_C[0])]
-        wd_planes = placed([P, 2 * N], U8, "wd_planes", 7 * KB)
+        pooled1 = [placed([P, 2 * PASS], F32, "pooled1%d" % pair, (76 + 4 * pair) * KB) for pair in range(2)]
+
+        def pool_second_half(jt):
+            copy_first(1, jt, neighbour_sum(1, jt, 0, 2 * jt))
+            best = pooled1[jt // 2][:].rearrange("p (h u j x) -> p j u h x", h=2, u=2, j=2)[:, jt % 2]
+            second_sum(1, jt, 2 * jt + 1, best)
+
+        leading = [neighbour_sum(0, jt, 0, jt) for jt in range(NJT)]
+        copy_first(0, 0, leading[0])
+        c_q = [prepare(c_raw[0], "c0", SHARE_C[0], 52 * KB)]
+        for jt in range(1, NJT):
+            copy_first(0, jt, leading[jt])
+        pooled0 = []
+        for jt in range(NJT):
+            pooled0.append(placed([P, PASS], F32, "pooled0%d" % jt, (52, 54, 84, 86)[jt] * KB))
+            second_sum(0, jt, NJT + jt, by_pair(pooled0[jt][:]))
+        last_raw = [
+            load_rows(
+                placed([P, PACK, HALF], F32, "wc_raw11%d" % h, 4 * h * KB),
+                wc[PASS : 2 * PASS, PASS + HALF * h : PASS + HALF * (h + 1)],
+            )
+            for h in range(2)
+        ]
+        c_q.append(prepare(c_raw[1], "c1", SHARE_C[1]))
+        pool_second_half(0)
+        pool_second_half(1)
+        wd_planes = placed([P, 2 * N], U8, "wd_planes", 8 * KB)
         nc.vector.memset(wd_planes[:].bitcast(I32), 0)
         move_rows(wd_planes[:], wd_dense)
-        wd_words = placed([P, 6 * N], U8, "wd_words", 12 * KB)
+        wd_words = placed([P, 6 * N], U8, "wd_words", 65 * KB + 512)
         nc.sync.dma_start(wd_words[:, 0 : 4 * N].bitcast(I32), wd8_words[0].rearrange("p n i -> p (n i)").bitcast(I32))
         nc.sync.dma_start(wd_words[:, 4 * N : 6 * N].bitcast(I32), wd4_words[0].bitcast(I32))
-        res_sb = placed([P, N // P, J], F32, "res_sb", 62 * KB)
-        nc.sync.dma_start(res_sb[:], res.rearrange("(n p) j -> p n j", p=P))
-        leading = [neighbour_sum(0, jt, 0, jt < PLAIN, jt) for jt in range(NJT)]
-        for jt in range(PLAIN):
-            pool_tile(0, jt, (leading[jt], neighbour_sum(0, jt, 1, True, NJT + jt)), (8 + 2 * jt) * KB)
-        open_banks = {}
-        for jt in range(PLAIN, NJT):
-            open_banks[jt] = [leading[jt], neighbour_sum(0, jt, 1, False, NJT + jt)]
-        c_q.append(prepare(c_raw[1], "c1", SCALAR_C[1]))
+        res_rows = res.rearrange("(n p) j -> p n j", p=P)
+        res_sb = [placed([P, N // P, 2 * JT], F32, "res_sb%d" % pair, (60 - 32 * pair) * KB + 512 * (1 - pair)) for pair in range(2)]
+        nc.sync.dma_start(res_sb[0][:], res_rows[:, :, 0 : 2 * JT])
+        wc_q = {(0, 0): prepare(wc_raw[0, 0], "wc00", SHARE_WC[0])}
+        nc.sync.dma_start(res_sb[1][:], res_rows[:, :, 2 * JT : 4 * JT])
+        pool_second_half(2)
 
-        wc_q = {}
-        own = {}
-
-        def own_pass(bank, b, jt, a, opens):
-            codes, plane = wc_q[b, a]
+        def own_pass(target, jt, a, quantised, columns, opens, closes):
+            codes, plane = quantised
             nc.tensor.matmul_mx(
-                out=bank[:],
+                out=target,
                 lhsT=c_q[a][0][:, JT * jt : JT * (jt + 1)].bitcast(FP8X4),
                 lhsT_scale=c_q[a][1][:, JT * jt : JT * (jt + 1)],
-                rhs=codes[:].bitcast(FP8X4),
-                rhs_scale=plane[:],
+                rhs=codes[:, columns].bitcast(FP8X4),
+                rhs_scale=plane[:, columns],
                 start=opens,
-                stop=(a == 1),
+                stop=closes,
             )
-
-        def open_own(b, jt, slot):
-            own[b, jt] = bank_tile(slot)
-            own_pass(own[b, jt], b, jt, 0, True)
-
-        def add_own(b, jt, summed):
-            nc.vector.tensor_tensor(by_pair(summed), bank_by_pair(own[b, jt]), by_pair(pooled[b, jt][:]), ALU.add)
-
-        def turn(tiles, slot):
-            bank = bank_tile(slot)
-            width = JT * len(tiles)
-            for x, rows in enumerate(tiles):
-                for u in range(2):
-                    at = width * u + JT * x
-                    nc.tensor.transpose(bank[:, at : at + JT], rows.bitcast(F32)[:, P * u : P * (u + 1)], ident[:])
-            return bank[:, 0 : 2 * width]
 
         def relu_out(turned, hidden):
             nc.scalar.activation(
@@ -235,58 +243,84 @@ def tile_list_pnet_mix_res_kernel(
                 ACT.Relu,
             )
 
-        def pool_second(jt, offset, at=None):
-            pool_tile(1, jt, [neighbour_sum(1, jt, g, True, jt % 2 + NJT * g) for g in range(2)], offset, at)
+        own0 = [bank_tile(jt) for jt in range(2)]
+        for jt in range(2):
+            own_pass(own0[jt][:], jt, 0, wc_q[0, 0], slice(0, PASS), True, False)
+        wc_q[0, 1] = prepare(wc_raw[0, 1], "wc01", SHARE_WC[1])
+        pool_second_half(3)
+        summed0 = [held([P, PASS], BF16, "summed0%d" % jt) for jt in range(2)]
+
+        def add_first_half(jt):
+            if jt >= 2:
+                own0.append(bank_tile(NJT + jt))
+                own_pass(own0[jt][:], jt, 0, wc_q[0, 0], slice(0, PASS), True, False)
+            own_pass(own0[jt][:], jt, 1, wc_q[0, 1], slice(0, PASS), False, True)
+            nc.vector.tensor_tensor(by_pair(summed0[jt][:]), bank_by_pair(own0[jt]), by_pair(pooled0[jt][:]), ALU.add)
+
+        turned0 = []
+
+        def turn_first_half(pair):
+            bank = bank_tile(6 * pair)
+            for x in range(2):
+                for u in range(2):
+                    at = 2 * JT * u + JT * x
+                    words = summed0[2 * pair + x][:].bitcast(F32)[:, P * u : P * (u + 1)]
+                    nc.tensor.transpose(bank[:, at : at + JT], words, ident[:])
+            turned0.append(bank)
 
         for jt in range(2):
-            pool_second(jt, (21 + 2 * jt) * KB)
-        wc_q[0, 0] = prepare(wc_raw[0, 0], "wc00", SCALAR_WC[0])
-        pool_second(2, 29 * KB)
-        wc_q[0, 1] = prepare(wc_raw[0, 1], "wc01", SCALAR_WC[1])
-        pool_second(3, 31 * KB, 81 * KB)
+            add_first_half(jt)
+        wc_q[1, 0] = prepare(wc_raw[1, 0], "wc10", SHARE_WC[2], 72 * KB)
+        summed0.append(placed([P, PASS], BF16, "summed02", 72 * KB))
+        add_first_half(2)
+        last_q = [prepare(last_raw[0], "wc110", SHARE_LAST[0], 100 * KB)]
+        summed0.append(placed([P, PASS], BF16, "summed03", 100 * KB))
+        add_first_half(3)
+        last_q.append(prepare(last_raw[1], "wc111", SHARE_LAST[1], 96 * KB))
+        turn_first_half(0)
 
-        summed0 = [held([P, PASS], BF16, "summed0%d" % jt) for jt in range(NJT)]
-        for jt in range(PLAIN, NJT):
-            for bank in open_banks[jt]:
-                own_pass(bank, 0, jt, 0, False)
-        for jt in range(PLAIN):
-            open_own(0, jt, NJT * jt)
-        for jt in range(PLAIN):
-            own_pass(own[0, jt], 0, jt, 1, False)
-            add_own(0, jt, summed0[jt][:])
-        for jt in range(PLAIN, NJT):
-            for bank in open_banks[jt]:
-                own_pass(bank, 0, jt, 1, False)
-        wc_q[1, 0] = prepare(wc_raw[1, 0], "wc10", SCALAR_WC[2])
-        own_slots = (1, 5, 4, 0)
-        last = NJT - 1
-        for jt in range(last):
-            open_own(1, jt, own_slots[jt])
-        turned = turn([summed0[jt][:] for jt in range(PLAIN)], 0)
-        wc_q[1, 1] = prepare(wc_raw[1, 1], "wc11", SCALAR_WC[3])
-        for jt in range(last):
-            own_pass(own[1, jt], 1, jt, 1, False)
-        hidden0 = [placed([P, 2 * PASS], BF16, "hidden00", 57 * KB), held([P, 2 * PASS], BF16, "hidden01")]
-        relu_out(turned, hidden0[0][:])
-        open_own(1, last, own_slots[last])
-        own_pass(own[1, last], 1, last, 1, False)
+        own1 = {(h, pair): bank_tile(2 + 2 * h + pair) for h in range(2) for pair in range(2)}
+        for h in range(2):
+            for jt in range(NJT):
+                target = own1[h, jt // 2][:, HALF * (jt % 2) : HALF * (jt % 2 + 1)]
+                own_pass(target, jt, 0, wc_q[1, 0], slice(HALF * h, HALF * (h + 1)), jt % 2 == 0, False)
+        summed1 = [placed([P, 2 * PASS], BF16, "summed1%d" % pair, (95 + 2 * pair) * KB) for pair in range(2)]
+
+        def close_second_half(h, quantised):
+            for pair in range(2):
+                for x in range(2):
+                    target = own1[h, pair][:, HALF * x : HALF * (x + 1)]
+                    own_pass(target, 2 * pair + x, 1, quantised, slice(0, HALF), False, x == 1)
+                nc.vector.tensor_tensor(
+                    summed1[pair][:].rearrange("p (j u h x) -> p h u j x", j=2, u=2, h=2)[:, h],
+                    bank_by_pair(own1[h, pair]),
+                    pooled1[pair][:, PASS * h : PASS * (h + 1)].rearrange("p (u j x) -> p u j x", u=2, j=2),
+                    ALU.add,
+                )
+
+        hidden0 = [placed([P, 2 * PASS], BF16, "hidden0%d" % pair, (4 + 2 * pair) * KB) for pair in range(2)]
+        relu_out(turned0[0][:], hidden0[0][:])
+        close_second_half(0, last_q[0])
+        turn_first_half(1)
+        relu_out(turned0[1][:], hidden0[1][:])
         h0_q = [quantise(hidden0[0][:], "h00")]
-        for jt in range(PLAIN, NJT):
-            pool_banks(open_banks[jt], ACT.Relu, summed0[jt][:], "first0%d" % jt, (49 + 2 * jt) * KB)
-
-        def finish_doubled():
-            nc.scalar.copy(
-                hidden0[1][:].bitcast(F32).rearrange("p (j u) -> p j u", u=2),
-                turn([summed0[jt][:] for jt in range(PLAIN, NJT)], 3).rearrange("p (u j) -> p j u", u=2),
-            )
-            h0_q.append(quantise(hidden0[1][:], "h01"))
+        close_second_half(1, last_q[1])
 
         out_rows = out.rearrange("(n p) j -> p n j", p=P)
         hidden1 = {}
+        turned1 = {}
         y_bank = {}
 
+        def turn_pair(pair):
+            for jt in range(2 * pair, 2 * pair + 2):
+                turned1[jt] = bank_tile((4, 0, 5, 6)[jt])
+                for u in range(2):
+                    at = P * (2 * (jt % 2) + u)
+                    words = summed1[pair][:].bitcast(F32)[:, at : at + P]
+                    nc.tensor.transpose(turned1[jt][:, P * u : P * (u + 1)], words, ident[:])
+
         def open_second_layer(jt):
-            y_bank[jt] = bank_tile((6, 7, 2, 3)[jt])
+            y_bank[jt] = bank_tile((1, 7, 2, 3)[jt])
             for n in range(N // P):
                 nc.tensor.matmul_mx(
                     out=y_bank[jt][:, JT * n : JT * (n + 1)],
@@ -299,13 +333,17 @@ def tile_list_pnet_mix_res_kernel(
                 )
 
         def end_first_layer(jt):
-            summed = held([P, PASS], BF16, "summed1%d" % jt)
-            add_own(1, jt, summed[:])
-            hidden1[jt] = held([P, PASS], BF16, "hidden1%d" % jt)
-            relu_out(turn([summed[:]], own_slots[jt]), hidden1[jt][:])
+            hidden1[jt] = placed([P, PASS], BF16, "hidden1%d" % jt, (104 + 4 * jt) * KB)
+            if jt == 1:
+                nc.vector.tensor_scalar_max(
+                    hidden1[jt][:].rearrange("p (j u e) -> p j u e", u=2, e=2),
+                    turned1[jt][:, 0:HALF].bitcast(BF16).rearrange("p (u j e) -> p j u e", u=2, e=2),
+                    0.0,
+                )
+            else:
+                relu_out(turned1[jt][:, 0:HALF], hidden1[jt][:])
 
         def end_second_layer(jt):
-            open_second_layer(jt)
             h1_codes, h1_plane = quantise(hidden1[jt][:], "h1%d" % jt)
             for n in range(N // P):
                 nc.tensor.matmul_mx(
@@ -319,21 +357,27 @@ def tile_list_pnet_mix_res_kernel(
                 )
 
         def add_residual_and_store(jt):
-            result = held([P, N // P, JT], F32, "result%d" % jt)
+            result = placed([P, N // P, JT], F32, "result%d" % jt, (120, 116, 122, 124)[jt] * KB)
             nc.vector.tensor_tensor(
                 result[:],
                 y_bank[jt][:].rearrange("p (n j) -> p n j", j=JT),
-                res_sb[:, :, JT * jt : JT * (jt + 1)],
+                res_sb[jt // 2][:, :, JT * (jt % 2) : JT * (jt % 2 + 1)],
                 ALU.add,
             )
             nc.sync.dma_start(out_rows[:, :, JT * jt : JT * (jt + 1)], result[:])
 
-        for step in range(NJT + 2):
-            if step < NJT:
-                end_first_layer(step)
-            if step == 1:
-                finish_doubled()
-            if 1 <= step <= NJT:
-                end_second_layer(step - 1)
-            if step >= 2:
-                add_residual_and_store(step - 2)
+        for jt in range(2):
+            open_second_layer(jt)
+        for pair in range(2):
+            turn_pair(pair)
+        h0_q.append(quantise(hidden0[1][:], "h01", 80 * KB))
+        for jt in range(NJT):
+            end_first_layer(jt)
+        for jt in range(2, NJT):
+            open_second_layer(jt)
+        for jt in range(NJT - 1):
+            end_second_layer(jt)
+        add_residual_and_store(0)
+        end_second_layer(NJT - 1)
+        for jt in range(1, NJT):
+            add_residual_and_store(jt)

@@ -28,9 +28,9 @@ LIST_GROUP = 16
 QUADRANT = 32
 ROWS = 4
 DENSE = P - 32
-SHARE_C = ((0, 0), (80, 48))
-SHARE_WC = ((80, 48), (76, 52), (76, 52))
-SHARE_LAST = ((64, 0), (40, 24))
+SHARE_C = (0, 128)
+SHARE_WC = (72, 48)
+SHARE_LAST = ((64, 64), (0, 64))
 
 
 def tile_list_pnet_mix_res_kernel(
@@ -74,18 +74,17 @@ def tile_list_pnet_mix_res_kernel(
             nc.sync.dma_start(wd_dense[DENSE + a : P : 2, :].bitcast(I32), scales[0].bitcast(I32))
         tab = placed([P, T], U32, "tab", 32 * KB)
         nc.sync.dma_start(tab[:].bitcast(I32), tab_words[0].rearrange("p e f -> p (e f)").bitcast(I32))
+        w_planes = held([P, 2 * R], U8, "w_planes")
+        nc.vector.memset(w_planes[:].bitcast(I32), 0)
+        for s in range(ROWS):
+            nc.sync.dma_start(
+                w_planes[s:P:QUADRANT, :].bitcast(I32),
+                w_scales[:, s : 4 * ROWS : ROWS, :].rearrange("a d e -> d a e").bitcast(I32),
+            )
         w_flat = w_words.rearrange("a p r i -> p a (r i)")
         w_first = held([P, 2, PASS], U32, "w_codes0")
         nc.sync.dma_start(w_first[:].bitcast(I32), w_flat[:, :, 0 : 4 * PASS].bitcast(I32))
         w_codes = {(0, a): w_first[:, a, :] for a in range(2)}
-
-        w_planes = held([P, 2 * R], U8, "w_planes")
-        nc.gpsimd.memset(w_planes[:].bitcast(I32), 0)
-        for s in range(ROWS):
-            (nc.sync if s == ROWS - 1 else nc.gpsimd).dma_start(
-                w_planes[s:P:QUADRANT, :].bitcast(I32),
-                w_scales[:, s : 4 * ROWS : ROWS, :].rearrange("a d e -> d a e").bitcast(I32),
-            )
         ident = held([P, P], F32, "ident")
         make_identity(nc, ident[:])
 
@@ -149,12 +148,15 @@ def tile_list_pnet_mix_res_kernel(
 
         first_at = {(0, 0): 84, (0, 1): 86, (0, 2): 88, (0, 3): 90, (1, 0): 64, (1, 1): 92, (1, 2): 32, (1, 3): 36}
 
-        def copy_first(b, jt, bank):
-            first[b, jt] = placed([P, PASS], F32, "first%d%d" % (b, jt), first_at[b, jt] * KB)
-            nc.scalar.activation(by_pair(first[b, jt][:]), bank_by_pair(bank), ACT.Copy)
+        def bank_by_slot(bank):
+            return bank[:].rearrange("p (q i) -> p i q", i=PACK)
 
-        def second_sum(b, jt, slot, best):
-            nc.vector.tensor_tensor(best, bank_by_pair(neighbour_sum(b, jt, 1, slot)), by_pair(first[b, jt][:]), ALU.max)
+        def copy_first(b, jt, bank, view=bank_by_pair):
+            first[b, jt] = placed([P, PASS], F32, "first%d%d" % (b, jt), first_at[b, jt] * KB)
+            nc.scalar.activation(first[b, jt][:], view(bank), ACT.Copy)
+
+        def second_sum(b, jt, slot, best, view=bank_by_pair):
+            nc.vector.tensor_tensor(best, view(neighbour_sum(b, jt, 1, slot)), first[b, jt][:], ALU.max)
 
         def quantise(grouped, name, at=None):
             width = grouped.shape[1] // PACK
@@ -166,41 +168,39 @@ def tile_list_pnet_mix_res_kernel(
             nc.vector.quantize_mx(out=codes[:].bitcast(FP8X4), scales=plane[:], in_=grouped)
             return codes, plane
 
-        def prepare(raw, name, share, at=None):
+        def prepare(raw, name, split, at=None):
             width = raw.shape[2]
             shape = [P, width * PACK]
             grouped = held(shape, BF16, name + "_bf") if at is None else placed(shape, BF16, name + "_bf", at)
             dst = grouped[:].rearrange("p (x z i) -> p x i z", z=4, i=PACK)
-            src = raw[:].rearrange("p i (x z) -> p x i z", z=4)
-            split, rest = share[0], share[0] + share[1]
+            src = raw.rearrange("p i (x z) -> p x i z", z=4)
             if split > 0:
                 nc.scalar.activation(dst[:, 0:split], src[:, 0:split], ACT.Copy)
-            if rest > split:
-                nc.gpsimd.tensor_scalar(
-                    grouped[:].rearrange("p (x i) -> p x i", i=PACK)[:, 4 * split : 4 * rest],
-                    raw[:].rearrange("p i x -> p x i")[:, 4 * split : 4 * rest],
-                    1.0, 0.0, ALU.mult, ALU.add,
-                )
-            if rest < width // 4:
-                nc.vector.tensor_copy(dst[:, rest : width // 4], src[:, rest : width // 4])
+            if split < width // 4:
+                nc.vector.tensor_copy(dst[:, split : width // 4], src[:, split : width // 4])
             return quantise(grouped[:], name)
 
-        pooled1 = [placed([P, 2 * PASS], F32, "pooled1%d" % pair, (76 + 4 * pair) * KB) for pair in range(2)]
+        pooled1 = {}
 
         def pool_second_half(jt):
             copy_first(1, jt, neighbour_sum(1, jt, 0, 2 * jt))
+            maximum_second_half(jt)
+
+        def maximum_second_half(jt):
+            if jt % 2 == 0:
+                pooled1[jt // 2] = placed([P, 2 * PASS], F32, "pooled1%d" % (jt // 2), (76, 40)[jt // 2] * KB)
             best = pooled1[jt // 2][:].rearrange("p (h u j x) -> p j u h x", h=2, u=2, j=2)[:, jt % 2]
             second_sum(1, jt, 2 * jt + 1, best)
 
         leading = [neighbour_sum(0, jt, 0, jt) for jt in range(NJT)]
         copy_first(0, 0, leading[0])
-        c_q = [prepare(c_raw[0], "c0", SHARE_C[0], 52 * KB)]
+        c_q = [prepare(c_raw[0][:], "c0", SHARE_C[0], 52 * KB)]
         for jt in range(1, NJT):
-            copy_first(0, jt, leading[jt])
+            copy_first(0, jt, leading[jt], bank_by_pair if jt < 3 else bank_by_slot)
         pooled0 = []
         for jt in range(NJT):
             pooled0.append(placed([P, PASS], F32, "pooled0%d" % jt, (52, 54, 84, 86)[jt] * KB))
-            second_sum(0, jt, NJT + jt, by_pair(pooled0[jt][:]))
+            second_sum(0, jt, NJT + jt, pooled0[jt][:], bank_by_pair if jt < 3 else bank_by_slot)
         last_raw = [
             load_rows(
                 placed([P, PACK, HALF], F32, "wc_raw11%d" % h, 4 * h * KB),
@@ -208,11 +208,11 @@ def tile_list_pnet_mix_res_kernel(
             )
             for h in range(2)
         ]
-        c_q.append(prepare(c_raw[1], "c1", SHARE_C[1]))
+        c_q.append(prepare(c_raw[1][:], "c1", SHARE_C[1]))
         pool_second_half(0)
         pool_second_half(1)
-        wd_planes = placed([P, 2 * N], U8, "wd_planes", 8 * KB)
-        nc.vector.memset(wd_planes[:].bitcast(I32), 0)
+        wd_planes = placed([P, 2 * N], U8, "wd_planes", 9 * KB)
+        nc.gpsimd.memset(wd_planes[:].bitcast(I32), 0)
         move_rows(wd_planes[:], wd_dense)
         wd_words = placed([P, 6 * N], U8, "wd_words", 65 * KB + 512)
         nc.sync.dma_start(wd_words[:, 0 : 4 * N].bitcast(I32), wd8_words[0].rearrange("p n i -> p (n i)").bitcast(I32))
@@ -220,9 +220,9 @@ def tile_list_pnet_mix_res_kernel(
         res_rows = res.rearrange("(n p) j -> p n j", p=P)
         res_sb = [placed([P, N // P, 2 * JT], F32, "res_sb%d" % pair, (60 - 32 * pair) * KB + 512 * (1 - pair)) for pair in range(2)]
         nc.sync.dma_start(res_sb[0][:], res_rows[:, :, 0 : 2 * JT])
-        wc_q = {(0, 0): prepare(wc_raw[0, 0], "wc00", SHARE_WC[0])}
+        wc_q = {(0, 0): prepare(wc_raw[0, 0][:], "wc00", SHARE_WC[0])}
         nc.sync.dma_start(res_sb[1][:], res_rows[:, :, 2 * JT : 4 * JT])
-        pool_second_half(2)
+        copy_first(1, 2, neighbour_sum(1, 2, 0, 4))
 
         def own_pass(target, jt, a, quantised, columns, opens, closes):
             codes, plane = quantised
@@ -246,65 +246,103 @@ def tile_list_pnet_mix_res_kernel(
         own0 = [bank_tile(jt) for jt in range(2)]
         for jt in range(2):
             own_pass(own0[jt][:], jt, 0, wc_q[0, 0], slice(0, PASS), True, False)
-        wc_q[0, 1] = prepare(wc_raw[0, 1], "wc01", SHARE_WC[1])
+        wc_q[0, 1] = prepare(wc_raw[0, 1][:], "wc01", SHARE_WC[1])
+        maximum_second_half(2)
         pool_second_half(3)
-        summed0 = [held([P, PASS], BF16, "summed0%d" % jt) for jt in range(2)]
+        summed0 = {}
 
-        def add_first_half(jt):
-            if jt >= 2:
-                own0.append(bank_tile(NJT + jt))
-                own_pass(own0[jt][:], jt, 0, wc_q[0, 0], slice(0, PASS), True, False)
-            own_pass(own0[jt][:], jt, 1, wc_q[0, 1], slice(0, PASS), False, True)
-            nc.vector.tensor_tensor(by_pair(summed0[jt][:]), bank_by_pair(own0[jt]), by_pair(pooled0[jt][:]), ALU.add)
+        def add_first_half(jt, at):
+            summed0[jt] = placed([P, PASS], BF16, "summed0%d" % jt, at * KB)
+            nc.vector.tensor_tensor(summed0[jt][:], bank_by_pair(own0[jt]), pooled0[jt][:], ALU.add)
 
-        turned0 = []
-
-        def turn_first_half(pair):
-            bank = bank_tile(6 * pair)
-            for x in range(2):
+        def turn_first_half(tiles, slot):
+            bank = bank_tile(slot)
+            width = JT * len(tiles)
+            for x, jt in enumerate(tiles):
                 for u in range(2):
-                    at = 2 * JT * u + JT * x
-                    words = summed0[2 * pair + x][:].bitcast(F32)[:, P * u : P * (u + 1)]
+                    at = width * u + JT * x
+                    words = summed0[jt][:].bitcast(F32)[:, P * u : P * (u + 1)]
                     nc.tensor.transpose(bank[:, at : at + JT], words, ident[:])
-            turned0.append(bank)
+            return bank[:, 0 : 2 * width]
+
+        kept = {}
+
+        def keep_own(jt, at):
+            kept[jt] = placed([P, PASS], F32, "kept%d" % jt, at)
+            nc.scalar.activation(kept[jt][:], bank_by_slot(own0[jt]), ACT.Copy)
+
+        def turn_and_add(jt, slot):
+            bank = bank_tile(slot)
+            for x, rows in enumerate((pooled0[jt], kept[jt])):
+                for i in range(PACK):
+                    nc.tensor.matmul(
+                        bank[:, JT * i : JT * (i + 1)], rows[:, P * i : P * (i + 1)], ident[:],
+                        start=(x == 0 and i == 0), stop=(x == 1 and i == PACK - 1), is_transpose=True,
+                    )
+            return bank
+
+        own1 = {}
+        late_q = {}
+        summed1 = {}
+
+        def prepare_late(h, a, at):
+            raw = wc_raw[1, 0][:, :, HALF * h : HALF * (h + 1)] if a == 0 else last_raw[h][:]
+            late_q[h, a] = prepare(raw, "wc1%d%d" % (a, h), SHARE_LAST[h][a], at * KB)
+
+        def late_passes(h, a, pair):
+            if a == 0:
+                own1[h, pair] = bank_tile(2 + 2 * h + pair)
+            for x in range(2):
+                target = own1[h, pair][:, HALF * x : HALF * (x + 1)]
+                own_pass(target, 2 * pair + x, a, late_q[h, a], slice(0, HALF), a == 0 and x == 0, a == 1 and x == 1)
+
+        def add_second_half(h, pair, at):
+            if h == 0:
+                summed1[pair] = placed([P, 2 * PASS], BF16, "summed1%d" % pair, at * KB)
+            nc.vector.tensor_tensor(
+                summed1[pair][:].rearrange("p (j u h x) -> p h u j x", j=2, u=2, h=2)[:, h],
+                bank_by_pair(own1[h, pair]),
+                pooled1[pair][:, PASS * h : PASS * (h + 1)].rearrange("p (u j x) -> p u j x", u=2, j=2),
+                ALU.add,
+            )
 
         for jt in range(2):
-            add_first_half(jt)
-        wc_q[1, 0] = prepare(wc_raw[1, 0], "wc10", SHARE_WC[2], 72 * KB)
-        summed0.append(placed([P, PASS], BF16, "summed02", 72 * KB))
-        add_first_half(2)
-        last_q = [prepare(last_raw[0], "wc110", SHARE_LAST[0], 100 * KB)]
-        summed0.append(placed([P, PASS], BF16, "summed03", 100 * KB))
-        add_first_half(3)
-        last_q.append(prepare(last_raw[1], "wc111", SHARE_LAST[1], 96 * KB))
-        turn_first_half(0)
-
-        own1 = {(h, pair): bank_tile(2 + 2 * h + pair) for h in range(2) for pair in range(2)}
+            own_pass(own0[jt][:], jt, 1, wc_q[0, 1], slice(0, PASS), False, True)
+        for jt in range(2, NJT):
+            own0.append(bank_tile(NJT + jt))
+            for a in range(2):
+                own_pass(own0[jt][:], jt, a, wc_q[0, a], slice(0, PASS), a == 0, a == 1)
+        add_first_half(0, 70)
+        prepare_late(1, 0, 74)
+        prepare_late(0, 0, 72)
+        add_first_half(1, 72)
         for h in range(2):
-            for jt in range(NJT):
-                target = own1[h, jt // 2][:, HALF * (jt % 2) : HALF * (jt % 2 + 1)]
-                own_pass(target, jt, 0, wc_q[1, 0], slice(HALF * h, HALF * (h + 1)), jt % 2 == 0, False)
-        summed1 = [placed([P, 2 * PASS], BF16, "summed1%d" % pair, (95 + 2 * pair) * KB) for pair in range(2)]
-
-        def close_second_half(h, quantised):
             for pair in range(2):
-                for x in range(2):
-                    target = own1[h, pair][:, HALF * x : HALF * (x + 1)]
-                    own_pass(target, 2 * pair + x, 1, quantised, slice(0, HALF), False, x == 1)
-                nc.vector.tensor_tensor(
-                    summed1[pair][:].rearrange("p (j u h x) -> p h u j x", j=2, u=2, h=2)[:, h],
-                    bank_by_pair(own1[h, pair]),
-                    pooled1[pair][:, PASS * h : PASS * (h + 1)].rearrange("p (u j x) -> p u j x", u=2, j=2),
-                    ALU.add,
-                )
-
-        hidden0 = [placed([P, 2 * PASS], BF16, "hidden0%d" % pair, (4 + 2 * pair) * KB) for pair in range(2)]
-        relu_out(turned0[0][:], hidden0[0][:])
-        close_second_half(0, last_q[0])
-        turn_first_half(1)
-        relu_out(turned0[1][:], hidden0[1][:])
+                late_passes(h, 0, pair)
+        prepare_late(0, 1, 100)
+        add_first_half(2, 100)
+        for pair in range(2):
+            late_passes(0, 1, pair)
+        prepare_late(1, 1, 96)
+        keep_own(3, 9 * KB // 2)
+        turned0 = turn_first_half((0, 1), 0)
+        late_passes(1, 1, 0)
+        hidden0 = [placed([P, 2 * PASS], BF16, "hidden0%d" % pair, (13 * KB // 2, 5 * KB // 2)[pair]) for pair in range(2)]
+        relu_out(turned0, hidden0[0][:])
+        added = turn_and_add(3, 7)
+        turned2 = turn_first_half((2,), 6)
+        late_passes(1, 1, 1)
+        relu_out(turned2, hidden0[1][:, 0:PASS])
+        nc.scalar.activation(
+            hidden0[1][:, PASS : 2 * PASS].rearrange("p (j i) -> p j i", i=PACK),
+            added[:].rearrange("p (i j) -> p j i", i=PACK),
+            ACT.Relu,
+        )
+        add_second_half(0, 0, 96)
+        add_second_half(1, 0, 0)
         h0_q = [quantise(hidden0[0][:], "h00")]
-        close_second_half(1, last_q[1])
+        add_second_half(0, 1, 76)
+        add_second_half(1, 1, 0)
 
         out_rows = out.rearrange("(n p) j -> p n j", p=P)
         hidden1 = {}
@@ -319,22 +357,24 @@ def tile_list_pnet_mix_res_kernel(
                     words = summed1[pair][:].bitcast(F32)[:, at : at + P]
                     nc.tensor.transpose(turned1[jt][:, P * u : P * (u + 1)], words, ident[:])
 
-        def open_second_layer(jt):
-            y_bank[jt] = bank_tile((1, 7, 2, 3)[jt])
-            for n in range(N // P):
-                nc.tensor.matmul_mx(
-                    out=y_bank[jt][:, JT * n : JT * (n + 1)],
-                    lhsT=wd_words[:, 4 * P * n : 4 * P * (n + 1)].bitcast(FP8X4),
-                    lhsT_scale=wd_planes[:, P * n : P * (n + 1)],
-                    rhs=h0_q[jt // 2][0][:, JT * (jt % 2) : JT * (jt % 2 + 1)].bitcast(FP8X4),
-                    rhs_scale=h0_q[jt // 2][1][:, JT * (jt % 2) : JT * (jt % 2 + 1)],
-                    start=(n == 0),
-                    stop=False,
-                )
+        def open_second_layer(pair):
+            for nh in range(2):
+                y_bank[pair, nh] = bank_tile((1, 2, 3, 7)[2 * pair + nh])
+                for x in range(2):
+                    n = 2 * nh + x
+                    nc.tensor.matmul_mx(
+                        out=y_bank[pair, nh][:, HALF * x : HALF * (x + 1)],
+                        lhsT=wd_words[:, 4 * P * n : 4 * P * (n + 1)].bitcast(FP8X4),
+                        lhsT_scale=wd_planes[:, P * n : P * (n + 1)],
+                        rhs=h0_q[pair][0][:].bitcast(FP8X4),
+                        rhs_scale=h0_q[pair][1][:],
+                        start=(x == 0),
+                        stop=False,
+                    )
 
         def end_first_layer(jt):
             hidden1[jt] = placed([P, PASS], BF16, "hidden1%d" % jt, (104 + 4 * jt) * KB)
-            if jt == 1:
+            if jt % 2 == 1:
                 nc.vector.tensor_scalar_max(
                     hidden1[jt][:].rearrange("p (j u e) -> p j u e", u=2, e=2),
                     turned1[jt][:, 0:HALF].bitcast(BF16).rearrange("p (u j e) -> p j u e", u=2, e=2),
@@ -347,37 +387,40 @@ def tile_list_pnet_mix_res_kernel(
             h1_codes, h1_plane = quantise(hidden1[jt][:], "h1%d" % jt)
             for n in range(N // P):
                 nc.tensor.matmul_mx(
-                    out=y_bank[jt][:, JT * n : JT * (n + 1)],
+                    out=y_bank[jt // 2, n // 2][:, HALF * (n % 2) + JT * (jt % 2) : HALF * (n % 2) + JT * (jt % 2 + 1)],
                     lhsT=wd_words[:, 4 * N + 2 * P * n : 4 * N + 2 * P * (n + 1)].bitcast(FP4X4),
                     lhsT_scale=wd_planes[:, N + P * n : N + P * (n + 1)],
                     rhs=h1_codes[:].bitcast(FP8X4),
                     rhs_scale=h1_plane[:],
                     start=False,
-                    stop=(n == N // P - 1),
+                    stop=(jt % 2 == 1 and n % 2 == 1),
                 )
 
-        def add_residual_and_store(jt):
-            result = placed([P, N // P, JT], F32, "result%d" % jt, (120, 116, 122, 124)[jt] * KB)
+        def add_residual_and_store(pair, nh):
+            at = (120, 116, 122, 124)[2 * pair + nh] * KB
+            result = placed([P, 2, 2 * JT], F32, "result%d%d" % (pair, nh), at)
             nc.vector.tensor_tensor(
                 result[:],
-                y_bank[jt][:].rearrange("p (n j) -> p n j", j=JT),
-                res_sb[jt // 2][:, :, JT * (jt % 2) : JT * (jt % 2 + 1)],
+                y_bank[pair, nh][:].rearrange("p (n j) -> p n j", n=2),
+                res_sb[pair][:, 2 * nh : 2 * nh + 2, :],
                 ALU.add,
             )
-            nc.sync.dma_start(out_rows[:, :, JT * jt : JT * (jt + 1)], result[:])
+            nc.sync.dma_start(out_rows[:, 2 * nh : 2 * nh + 2, 2 * JT * pair : 2 * JT * (pair + 1)], result[:])
 
+        turn_pair(0)
+        open_second_layer(0)
+        turn_pair(1)
         for jt in range(2):
-            open_second_layer(jt)
-        for pair in range(2):
-            turn_pair(pair)
-        h0_q.append(quantise(hidden0[1][:], "h01", 80 * KB))
-        for jt in range(NJT):
             end_first_layer(jt)
-        for jt in range(2, NJT):
-            open_second_layer(jt)
-        for jt in range(NJT - 1):
+        h0_q.append(quantise(hidden0[1][:], "h01", 40 * KB))
+        for jt in range(2):
             end_second_layer(jt)
-        add_residual_and_store(0)
-        end_second_layer(NJT - 1)
-        for jt in range(1, NJT):
-            add_residual_and_store(jt)
+        open_second_layer(1)
+        for jt in range(2, NJT):
+            end_first_layer(jt)
+        add_residual_and_store(0, 0)
+        for jt in range(2, NJT):
+            end_second_layer(jt)
+        add_residual_and_store(0, 1)
+        for nh in range(2):
+            add_residual_and_store(1, nh)

@@ -68,14 +68,11 @@ def tile_list_pnet_mix_res_kernel(
         nc.sync.dma_start(offsets[:], offs)
         tsc_win = placed([P, T], U8, "tsc_win", 7 * KB)
         nc.sync.dma_start(tsc_win[DENSE:P, :].bitcast(I32), tab_scales.rearrange("a q e -> q a e").bitcast(I32))
-        nc.vector.memset(tsc_win[0:DENSE, :].bitcast(I32), 0)
-        wd_dense = held([P, N], U8, "wd_dense")
-        for a, scales in enumerate((wd8_scales, wd4_scales)):
-            nc.sync.dma_start(wd_dense[DENSE + a : P : 2, :].bitcast(I32), scales[0].bitcast(I32))
         tab = placed([P, T], U32, "tab", 32 * KB)
         nc.sync.dma_start(tab[:].bitcast(I32), tab_words[0].rearrange("p e f -> p (e f)").bitcast(I32))
         w_planes = held([P, 2 * R], U8, "w_planes")
         nc.vector.memset(w_planes[:].bitcast(I32), 0)
+        nc.vector.memset(tsc_win[0:DENSE, :].bitcast(I32), 0)
         for s in range(ROWS):
             nc.sync.dma_start(
                 w_planes[s:P:QUADRANT, :].bitcast(I32),
@@ -114,6 +111,11 @@ def tile_list_pnet_mix_res_kernel(
         nc.sync.dma_start(w_second[:].bitcast(I32), w_flat[:, :, 4 * PASS : 8 * PASS].bitcast(I32))
         for a in range(2):
             w_codes[1, a] = w_second[:, a, :]
+        wd_planes = held([P, 2 * N], U8, "wd_planes")
+        nc.vector.memset(wd_planes[:].bitcast(I32), 0)
+        wd_dense = placed([P, N], U8, "wd_dense", 18 * KB)
+        for a, scales in enumerate((wd8_scales, wd4_scales)):
+            nc.sync.dma_start(wd_dense[DENSE + a : P : 2, :].bitcast(I32), scales[0].bitcast(I32))
         gather_words(1, placed([P, J], U32, "t_got1", 16 * KB))
         wc_raw = {}
         for b, a in ((0, 0), (0, 1), (1, 0)):
@@ -211,8 +213,6 @@ def tile_list_pnet_mix_res_kernel(
         c_q.append(prepare(c_raw[1][:], "c1", SHARE_C[1]))
         pool_second_half(0)
         pool_second_half(1)
-        wd_planes = placed([P, 2 * N], U8, "wd_planes", 9 * KB)
-        nc.gpsimd.memset(wd_planes[:].bitcast(I32), 0)
         move_rows(wd_planes[:], wd_dense)
         wd_words = placed([P, 6 * N], U8, "wd_words", 65 * KB + 512)
         nc.sync.dma_start(wd_words[:, 0 : 4 * N].bitcast(I32), wd8_words[0].rearrange("p n i -> p (n i)").bitcast(I32))
@@ -329,8 +329,9 @@ def tile_list_pnet_mix_res_kernel(
         late_passes(1, 1, 0)
         hidden0 = [placed([P, 2 * PASS], BF16, "hidden0%d" % pair, (13 * KB // 2, 5 * KB // 2)[pair]) for pair in range(2)]
         relu_out(turned0, hidden0[0][:])
+        add_second_half(0, 0, 96)
         added = turn_and_add(3, 7)
-        turned2 = turn_first_half((2,), 6)
+        turned2 = turn_first_half((2,), 2)
         late_passes(1, 1, 1)
         relu_out(turned2, hidden0[1][:, 0:PASS])
         nc.scalar.activation(
@@ -338,7 +339,6 @@ def tile_list_pnet_mix_res_kernel(
             added[:].rearrange("p (i j) -> p j i", i=PACK),
             ACT.Relu,
         )
-        add_second_half(0, 0, 96)
         add_second_half(1, 0, 0)
         h0_q = [quantise(hidden0[0][:], "h00")]
         add_second_half(0, 1, 76)
@@ -351,7 +351,7 @@ def tile_list_pnet_mix_res_kernel(
 
         def turn_pair(pair):
             for jt in range(2 * pair, 2 * pair + 2):
-                turned1[jt] = bank_tile((4, 0, 5, 6)[jt])
+                turned1[jt] = bank_tile((4, 0, 5, 2)[jt])
                 for u in range(2):
                     at = P * (2 * (jt % 2) + u)
                     words = summed1[pair][:].bitcast(F32)[:, at : at + P]
@@ -359,7 +359,7 @@ def tile_list_pnet_mix_res_kernel(
 
         def open_second_layer(pair):
             for nh in range(2):
-                y_bank[pair, nh] = bank_tile((1, 2, 3, 7)[2 * pair + nh])
+                y_bank[pair, nh] = bank_tile((1, 6, 3, 7)[2 * pair + nh])
                 for x in range(2):
                     n = 2 * nh + x
                     nc.tensor.matmul_mx(
@@ -383,18 +383,20 @@ def tile_list_pnet_mix_res_kernel(
             else:
                 relu_out(turned1[jt][:, 0:HALF], hidden1[jt][:])
 
-        def end_second_layer(jt):
-            h1_codes, h1_plane = quantise(hidden1[jt][:], "h1%d" % jt)
+        def end_second_layer(pair):
+            h1_q = [quantise(hidden1[jt][:], "h1%d" % jt) for jt in range(2 * pair, 2 * pair + 2)]
             for n in range(N // P):
-                nc.tensor.matmul_mx(
-                    out=y_bank[jt // 2, n // 2][:, HALF * (n % 2) + JT * (jt % 2) : HALF * (n % 2) + JT * (jt % 2 + 1)],
-                    lhsT=wd_words[:, 4 * N + 2 * P * n : 4 * N + 2 * P * (n + 1)].bitcast(FP4X4),
-                    lhsT_scale=wd_planes[:, N + P * n : N + P * (n + 1)],
-                    rhs=h1_codes[:].bitcast(FP8X4),
-                    rhs_scale=h1_plane[:],
-                    start=False,
-                    stop=(jt % 2 == 1 and n % 2 == 1),
-                )
+                for x in range(2):
+                    at = HALF * (n % 2) + JT * x
+                    nc.tensor.matmul_mx(
+                        out=y_bank[pair, n // 2][:, at : at + JT],
+                        lhsT=wd_words[:, 4 * N + 2 * P * n : 4 * N + 2 * P * (n + 1)].bitcast(FP4X4),
+                        lhsT_scale=wd_planes[:, N + P * n : N + P * (n + 1)],
+                        rhs=h1_q[x][0][:].bitcast(FP8X4),
+                        rhs_scale=h1_q[x][1][:],
+                        start=False,
+                        stop=(n % 2 == 1 and x == 1),
+                    )
 
         def add_residual_and_store(pair, nh):
             at = (120, 116, 122, 124)[2 * pair + nh] * KB
@@ -413,14 +415,12 @@ def tile_list_pnet_mix_res_kernel(
         for jt in range(2):
             end_first_layer(jt)
         h0_q.append(quantise(hidden0[1][:], "h01", 40 * KB))
-        for jt in range(2):
-            end_second_layer(jt)
+        end_second_layer(0)
         open_second_layer(1)
         for jt in range(2, NJT):
             end_first_layer(jt)
         add_residual_and_store(0, 0)
-        for jt in range(2, NJT):
-            end_second_layer(jt)
+        end_second_layer(1)
         add_residual_and_store(0, 1)
         for nh in range(2):
             add_residual_and_store(1, nh)

@@ -30,7 +30,7 @@ ROWS = 4
 DENSE = P - 32
 SHARE_C = (0, 128)
 SHARE_WC = (72, 48)
-SHARE_LAST = ((64, 64), (0, 64))
+SHARE_LAST = ((64, 64), (0, 32))
 
 
 def tile_list_pnet_mix_res_kernel(
@@ -320,16 +320,16 @@ def tile_list_pnet_mix_res_kernel(
             for pair in range(2):
                 late_passes(h, 0, pair)
         prepare_late(0, 1, 100)
-        add_first_half(2, 100)
         for pair in range(2):
             late_passes(0, 1, pair)
         prepare_late(1, 1, 96)
+        add_first_half(2, 96)
         keep_own(3, 9 * KB // 2)
         turned0 = turn_first_half((0, 1), 0)
         late_passes(1, 1, 0)
         hidden0 = [placed([P, 2 * PASS], BF16, "hidden0%d" % pair, (13 * KB // 2, 5 * KB // 2)[pair]) for pair in range(2)]
         relu_out(turned0, hidden0[0][:])
-        add_second_half(0, 0, 96)
+        add_second_half(0, 0, 97)
         added = turn_and_add(3, 7)
         turned2 = turn_first_half((2,), 2)
         late_passes(1, 1, 1)

@@ -148,7 +148,7 @@ def tile_list_pnet_mix_res_kernel(
 
         first = {}
 
-        first_at = {(0, 0): 84, (0, 1): 86, (0, 2): 88, (0, 3): 90, (1, 0): 64, (1, 1): 92, (1, 2): 32, (1, 3): 36}
+        first_at = {(0, 0): 84, (0, 1): 138, (0, 2): 88, (0, 3): 90, (1, 0): 64, (1, 1): 92, (1, 2): 32, (1, 3): 36}
 
         def bank_by_slot(bank):
             return bank[:].rearrange("p (q i) -> p i q", i=PACK)
@@ -170,7 +170,7 @@ def tile_list_pnet_mix_res_kernel(
             nc.vector.quantize_mx(out=codes[:].bitcast(FP8X4), scales=plane[:], in_=grouped)
             return codes, plane
 
-        def prepare(raw, name, split, at=None):
+        def prepare(raw, name, split, at=None, codes_at=None):
             width = raw.shape[2]
             shape = [P, width * PACK]
             grouped = held(shape, BF16, name + "_bf") if at is None else placed(shape, BF16, name + "_bf", at)
@@ -180,7 +180,7 @@ def tile_list_pnet_mix_res_kernel(
                 nc.scalar.activation(dst[:, 0:split], src[:, 0:split], ACT.Copy)
             if split < width // 4:
                 nc.vector.tensor_copy(dst[:, split : width // 4], src[:, split : width // 4])
-            return quantise(grouped[:], name)
+            return quantise(grouped[:], name, codes_at)
 
         pooled1 = {}
 
@@ -201,7 +201,7 @@ def tile_list_pnet_mix_res_kernel(
             copy_first(0, jt, leading[jt], bank_by_pair if jt < 3 else bank_by_slot)
         pooled0 = []
         for jt in range(NJT):
-            pooled0.append(placed([P, PASS], F32, "pooled0%d" % jt, (52, 54, 84, 86)[jt] * KB))
+            pooled0.append(placed([P, PASS], F32, "pooled0%d" % jt, (52, 54, 84, 138)[jt] * KB))
             second_sum(0, jt, NJT + jt, pooled0[jt][:], bank_by_pair if jt < 3 else bank_by_slot)
         last_raw = [
             load_rows(
@@ -285,9 +285,9 @@ def tile_list_pnet_mix_res_kernel(
         late_q = {}
         summed1 = {}
 
-        def prepare_late(h, a, at):
+        def prepare_late(h, a, at, codes_at=None):
             raw = wc_raw[1, 0][:, :, HALF * h : HALF * (h + 1)] if a == 0 else last_raw[h][:]
-            late_q[h, a] = prepare(raw, "wc1%d%d" % (a, h), SHARE_LAST[h][a], at * KB)
+            late_q[h, a] = prepare(raw, "wc1%d%d" % (a, h), SHARE_LAST[h][a], int(at * KB), codes_at)
 
         def late_passes(h, a, pair):
             if a == 0:
@@ -298,7 +298,7 @@ def tile_list_pnet_mix_res_kernel(
 
         def add_second_half(h, pair, at):
             if h == 0:
-                summed1[pair] = placed([P, 2 * PASS], BF16, "summed1%d" % pair, at * KB)
+                summed1[pair] = placed([P, 2 * PASS], BF16, "summed1%d" % pair, int(at * KB))
             nc.vector.tensor_tensor(
                 summed1[pair][:].rearrange("p (j u h x) -> p h u j x", j=2, u=2, h=2)[:, h],
                 bank_by_pair(own1[h, pair]),
@@ -313,26 +313,27 @@ def tile_list_pnet_mix_res_kernel(
             for a in range(2):
                 own_pass(own0[jt][:], jt, a, wc_q[0, a], slice(0, PASS), a == 0, a == 1)
         add_first_half(0, 70)
-        prepare_late(1, 0, 74)
+        prepare_late(1, 0, 134)
         prepare_late(0, 0, 72)
-        add_first_half(1, 72)
+        for jt in range(1, 3):
+            add_first_half(jt, 133 + jt)
         for h in range(2):
             for pair in range(2):
                 late_passes(h, 0, pair)
-        prepare_late(0, 1, 100)
+        prepare_late(0, 1, 100, 71 * KB + 512)
         for pair in range(2):
             late_passes(0, 1, pair)
-        prepare_late(1, 1, 96)
-        add_first_half(2, 96)
+        prepare_late(1, 1, 72.5)
         keep_own(3, 9 * KB // 2)
-        turned0 = turn_first_half((0, 1), 0)
-        late_passes(1, 1, 0)
+        turned0 = turn_first_half((0, 1), 1)
+        turned2 = turn_first_half((2,), 6)
+        for pair in range(2):
+            late_passes(1, 1, pair)
         hidden0 = [placed([P, 2 * PASS], BF16, "hidden0%d" % pair, (13 * KB // 2, 5 * KB // 2)[pair]) for pair in range(2)]
         relu_out(turned0, hidden0[0][:])
-        add_second_half(0, 0, 97)
-        added = turn_and_add(3, 7)
-        turned2 = turn_first_half((2,), 2)
-        late_passes(1, 1, 1)
+        for pair in range(2):
+            add_second_half(0, pair, 99 + 2 * pair)
+        added = turn_and_add(3, 2)
         relu_out(turned2, hidden0[1][:, 0:PASS])
         nc.scalar.activation(
             hidden0[1][:, PASS : 2 * PASS].rearrange("p (j i) -> p j i", i=PACK),
@@ -341,7 +342,6 @@ def tile_list_pnet_mix_res_kernel(
         )
         add_second_half(1, 0, 0)
         h0_q = [quantise(hidden0[0][:], "h00")]
-        add_second_half(0, 1, 76)
         add_second_half(1, 1, 0)
 
         out_rows = out.rearrange("(n p) j -> p n j", p=P)
@@ -351,7 +351,7 @@ def tile_list_pnet_mix_res_kernel(
 
         def turn_pair(pair):
             for jt in range(2 * pair, 2 * pair + 2):
-                turned1[jt] = bank_tile((4, 0, 5, 2)[jt])
+                turned1[jt] = bank_tile((4, 1, 5, 6)[jt])
                 for u in range(2):
                     at = P * (2 * (jt % 2) + u)
                     words = summed1[pair][:].bitcast(F32)[:, at : at + P]
@@ -359,7 +359,7 @@ def tile_list_pnet_mix_res_kernel(
 
         def open_second_layer(pair):
             for nh in range(2):
-                y_bank[pair, nh] = bank_tile((1, 6, 3, 7)[2 * pair + nh])
+                y_bank[pair, nh] = bank_tile((0, 7, 3, 2)[2 * pair + nh])
                 for x in range(2):
                     n = 2 * nh + x
                     nc.tensor.matmul_mx(

@@ -1,7 +1,6 @@
 from contextlib import ExitStack
 
 import concourse.mybir as mybir
-from concourse.masks import make_identity
 
 K, R, N, T, J = 1024, 1024, 512, 4096, 512
 FLOPS = 2 * K * R * 3 * J + 2 * R * N * J
@@ -23,14 +22,10 @@ PACK = 4
 PASS = P * PACK
 HALF = PASS // 2
 JT = 128
-NJT = J // JT
 LIST_GROUP = 16
 QUADRANT = 32
 ROWS = 4
 DENSE = P - 32
-SHARE_C = (0, 128)
-SHARE_WC = (72, 48)
-SHARE_LAST = ((64, 64), (0, 32))
 
 
 def tile_list_pnet_mix_res_kernel(
@@ -47,56 +42,74 @@ def tile_list_pnet_mix_res_kernel(
         def held(shape, dtype, name):
             return keep.tile(shape, dtype, name=name, tag=name, align_bytes=64)
 
-        def placed(shape, dtype, name, offset):
-            return stage.tile(shape, dtype, name=name, tag=name, align_bytes=64, offset=offset)
+        def placed(shape, dtype, name, kib):
+            if kib is None:
+                return held(shape, dtype, name)
+            return stage.tile(shape, dtype, name=name, tag=name, align_bytes=64, offset=int(kib * KB))
 
         def bank_tile(slot):
             return psum.tile([P, PASS], F32, name="bank", tag="bank%d" % slot)
 
-        def move_rows(target, rows):
+        def move_rows(planes, rows):
             for quad in (0, 2, 1, 3):
                 nc.sync.dma_start(
-                    target[QUADRANT * quad : QUADRANT * quad + ROWS, :].bitcast(I32),
+                    planes[QUADRANT * quad : QUADRANT * quad + ROWS, :].bitcast(I32),
                     rows[DENSE + 2 * ROWS * quad : DENSE + 2 * ROWS * (quad + 1), :].bitcast(I32),
                 )
 
-        def load_rows(raw, rows):
+        def load_rows(name, rows, kib):
+            raw = placed([P, PACK, rows.shape[1]], F32, name, kib)
             nc.sync.dma_start(raw[:], rows.rearrange("(p i) x -> p i x", i=PACK))
             return raw
 
+        def load_dense(target, scales):
+            nc.sync.dma_start(target[DENSE:P, :].bitcast(I32), scales.rearrange("a q e -> q a e").bitcast(I32))
+
         offsets = lists.tile([P, 2 * J // LIST_GROUP], U16, name="offsets")
         nc.sync.dma_start(offsets[:], offs)
-        tsc_win = placed([P, T], U8, "tsc_win", 7 * KB)
-        nc.sync.dma_start(tsc_win[DENSE:P, :].bitcast(I32), tab_scales.rearrange("a q e -> q a e").bitcast(I32))
-        tab = placed([P, T], U32, "tab", 32 * KB)
+        tsc_win = placed([P, T], U8, "tsc_win", 68)
+        load_dense(tsc_win, tab_scales)
+        wsc_raw = placed([P, R], U8, "wsc_raw", 72)
+        load_dense(wsc_raw, w_scales)
+        width = (2 * PASS, 2 * PASS, PASS)
+        rows = [held([P, width[s]], U8, "rows%d" % s) for s in range(2)]
+        tab = placed([P, T], U32, "tab", 48)
         nc.sync.dma_start(tab[:].bitcast(I32), tab_words[0].rearrange("p e f -> p (e f)").bitcast(I32))
-        w_planes = held([P, 2 * R], U8, "w_planes")
-        nc.vector.memset(w_planes[:].bitcast(I32), 0)
-        nc.vector.memset(tsc_win[0:DENSE, :].bitcast(I32), 0)
-        for s in range(ROWS):
-            nc.sync.dma_start(
-                w_planes[s:P:QUADRANT, :].bitcast(I32),
-                w_scales[:, s : 4 * ROWS : ROWS, :].rearrange("a d e -> d a e").bitcast(I32),
-            )
         w_flat = w_words.rearrange("a p r i -> p a (r i)")
-        w_first = held([P, 2, PASS], U32, "w_codes0")
-        nc.sync.dma_start(w_first[:].bitcast(I32), w_flat[:, :, 0 : 4 * PASS].bitcast(I32))
-        w_codes = {(0, a): w_first[:, a, :] for a in range(2)}
-        ident = held([P, P], F32, "ident")
-        make_identity(nc, ident[:])
+        w_raw = {}
 
-        t_planes = held([P, 4 * J], U8, "t_planes")
-        nc.vector.memset(t_planes[:].bitcast(I32), 0)
-        tsc_got = placed([P, 2 * J], U8, "tsc_got", 24 * KB)
+        def load_w(b, kib):
+            w_raw[b] = placed([P, 2, PASS], U32, "w_raw%d" % b, kib)
+            nc.sync.dma_start(w_raw[b][:].bitcast(I32), w_flat[:, :, 4 * PASS * b : 4 * PASS * (b + 1)].bitcast(I32))
+
+        load_w(0, None)
+        nc.vector.memset(tsc_win[0:DENSE, :].bitcast(I32), 0)
+        nc.vector.memset(wsc_raw[0:DENSE, :].bitcast(I32), 0)
+        planes = [held([P, 2 * width[s]], U8, "planes%d" % s) for s in range(2)]
+        for s in range(2):
+            nc.vector.memset(planes[s][:].bitcast(I32), 0)
+        tsc_got = placed([P, 2 * J], U8, "tsc_got", 20)
         nc.vector.tensor_copy(tsc_got[:], tsc_win[:].indirect(offsets[:]))
-        move_rows(t_planes[:], tsc_got)
+        for b in range(2):
+            nc.vector.tensor_copy(
+                rows[b][:, PASS : 2 * PASS].rearrange("p (t m) -> p t m", t=PACK),
+                wsc_raw[:, PASS * b : PASS * (b + 1)].rearrange("p (m t) -> p t m", t=PACK),
+            )
+        for g in range(2):
+            nc.vector.tensor_copy(rows[g][:, 0:J].bitcast(I32), tsc_got[:, J * g : J * (g + 1)].bitcast(I32))
+        move_rows(planes[0], rows[0])
+        c_raw = [load_rows("c_raw0", c[0:PASS, :], 12.5)]
+        move_rows(planes[1], rows[1])
+        load_w(1, 20.5)
 
-        c_raw = [load_rows(placed([P, PACK, J], F32, "c_raw0", 0), c[0:PASS, :])]
-        c_raw.append(load_rows(placed([P, PACK, J], F32, "c_raw1", 8 * KB), c[PASS : 2 * PASS, :]))
+        def scale_of(s, a, first, count):
+            at = width[s] * a + first
+            return planes[s][:, at : at + count]
 
         t_codes = []
 
-        def gather_words(g, got):
+        def gather_words(g, kib):
+            got = placed([P, J], U32, "t_got%d" % g, kib)
             columns = J // LIST_GROUP
             nc.vector.tensor_copy(got[:], tab[:].indirect(offsets[:, g * columns : (g + 1) * columns]))
             parted = held([P, 2 * 2 * J], U8, "t_codes%d" % g)
@@ -106,321 +119,274 @@ def tile_list_pnet_mix_res_kernel(
             )
             t_codes.append(parted)
 
-        gather_words(0, placed([P, J], U32, "t_got0", 17 * KB + 512))
-        w_second = placed([P, 2, PASS], U32, "w_codes1", 19 * KB)
-        nc.sync.dma_start(w_second[:].bitcast(I32), w_flat[:, :, 4 * PASS : 8 * PASS].bitcast(I32))
-        for a in range(2):
-            w_codes[1, a] = w_second[:, a, :]
-        wd_planes = held([P, 2 * N], U8, "wd_planes")
-        nc.vector.memset(wd_planes[:].bitcast(I32), 0)
-        wd_dense = placed([P, N], U8, "wd_dense", 18 * KB)
-        for a, scales in enumerate((wd8_scales, wd4_scales)):
-            nc.sync.dma_start(wd_dense[DENSE + a : P : 2, :].bitcast(I32), scales[0].bitcast(I32))
-        gather_words(1, placed([P, J], U32, "t_got1", 16 * KB))
-        wc_raw = {}
-        for b, a in ((0, 0), (0, 1), (1, 0)):
-            wc_raw[b, a] = load_rows(
-                placed([P, PACK, PASS], F32, "wc_raw%d%d" % (b, a), (28 + 16 * b + 8 * a) * KB),
-                wc[PASS * a : PASS * (a + 1), PASS * b : PASS * (b + 1)],
+        w_codes = {}
+
+        def order_w(b, u):
+            w_codes[b, u] = held([P, 2, HALF], U32, "w_codes%d%d" % (b, u))
+            nc.scalar.copy(
+                w_codes[b, u][:].rearrange("p a (e m) -> p a m e", e=2),
+                w_raw[b][:].rearrange("p a (m u e) -> p u a m e", u=2, e=2)[:, u],
             )
 
-        def by_pair(view):
-            return view.rearrange("p (u q e) -> p u q e", u=2, e=2)
+        banks = {}
 
-        def bank_by_pair(bank):
-            return bank[:].rearrange("p (q u e) -> p u q e", u=2, e=2)
+        def columns_of(key, t):
+            return banks[key][:, JT * t : JT * (t + 1)]
 
-        def neighbour_sum(b, jt, g, slot):
-            bank = bank_tile(slot)
-            for a in range(2):
-                tab_col = 2 * J * a + J * g + JT * jt
-                w_col = R * a + PASS * b
-                nc.tensor.matmul_mx(
-                    out=bank[:],
-                    lhsT=t_codes[g][:, 2 * (J * a + JT * jt) : 2 * (J * a + JT * (jt + 1))].bitcast(FP4X4),
-                    lhsT_scale=t_planes[:, tab_col : tab_col + JT],
-                    rhs=w_codes[b, a].bitcast(FP8X4),
-                    rhs_scale=w_planes[:, w_col : w_col + PASS],
-                    start=(a == 0),
-                    stop=(a == 1),
-                )
-            return bank
+        def by_point(key):
+            return banks[key][:].rearrange("p (t j) -> p j t", t=PACK)
+
+        def table_passes(b, jt, g, u, slot, alone=True):
+            if u == 0:
+                banks[b, jt, g] = bank_tile(slot)
+            for t in range(2 * u, 2 * u + 2):
+                for a in range(2):
+                    at = J * a + JT * jt
+                    nc.tensor.matmul_mx(
+                        out=columns_of((b, jt, g), t),
+                        lhsT=w_codes[b, u][:, a, P * (t % 2) : P * (t % 2 + 1)].bitcast(FP8X4),
+                        lhsT_scale=scale_of(b, a, PASS + P * t, P),
+                        rhs=t_codes[g][:, 2 * at : 2 * (at + JT)].bitcast(FP4X4),
+                        rhs_scale=scale_of(g, a, JT * jt, JT),
+                        start=(a == 0 if alone else t == 0 and a == 0),
+                        stop=(alone and a == 1),
+                    )
+
+        def neighbour_sum(b, jt, g, slot, alone=True):
+            for u in range(2):
+                table_passes(b, jt, g, u, slot, alone)
 
         first = {}
+        pooled = {}
 
-        first_at = {(0, 0): 84, (0, 1): 138, (0, 2): 88, (0, 3): 90, (1, 0): 64, (1, 1): 92, (1, 2): 32, (1, 3): 36}
+        def copy_first(b, jt, func=ACT.Copy, kib=None):
+            first[b, jt] = placed([P, PASS], F32, "first%d%d" % (b, jt), kib)
+            nc.scalar.activation(first[b, jt][:], by_point((b, jt, 0)), func)
 
-        def bank_by_slot(bank):
-            return bank[:].rearrange("p (q i) -> p i q", i=PACK)
+        def pool(b, jt, kib=None):
+            pooled[b, jt] = placed([P, PASS], F32, "pooled%d%d" % (b, jt), kib)
+            nc.vector.tensor_tensor(pooled[b, jt][:], by_point((b, jt, 1)), first[b, jt][:], ALU.max)
 
-        def copy_first(b, jt, bank, view=bank_by_pair):
-            first[b, jt] = placed([P, PASS], F32, "first%d%d" % (b, jt), first_at[b, jt] * KB)
-            nc.scalar.activation(first[b, jt][:], view(bank), ACT.Copy)
+        rounded = {}
+        quantised = {}
 
-        def second_sum(b, jt, slot, best, view=bank_by_pair):
-            nc.vector.tensor_tensor(best, view(neighbour_sum(b, jt, 1, slot)), first[b, jt][:], ALU.max)
-
-        def quantise(grouped, name, at=None):
-            width = grouped.shape[1] // PACK
-            if at is None:
-                codes = held([P, width], U32, name + "_codes")
+        def round_to(engine, dst, src):
+            if engine == "scalar":
+                nc.scalar.activation(dst, src, ACT.Copy)
             else:
-                codes = placed([P, width], U32, name + "_codes", at)
-            plane = held([P, width], U8, name + "_plane")
-            nc.vector.quantize_mx(out=codes[:].bitcast(FP8X4), scales=plane[:], in_=grouped)
-            return codes, plane
+                nc.vector.tensor_copy(dst, src)
 
-        def prepare(raw, name, split, at=None, codes_at=None):
-            width = raw.shape[2]
-            shape = [P, width * PACK]
-            grouped = held(shape, BF16, name + "_bf") if at is None else placed(shape, BF16, name + "_bf", at)
-            dst = grouped[:].rearrange("p (x z i) -> p x i z", z=4, i=PACK)
-            src = raw.rearrange("p i (x z) -> p x i z", z=4)
-            if split > 0:
-                nc.scalar.activation(dst[:, 0:split], src[:, 0:split], ACT.Copy)
-            if split < width // 4:
-                nc.vector.tensor_copy(dst[:, split : width // 4], src[:, split : width // 4])
-            return quantise(grouped[:], name, codes_at)
+        def round_c(a, first_point, points, engine, kib=None):
+            if first_point == 0:
+                rounded["c%d" % a] = placed([P, PACK * J], BF16, "c%d_bf" % a, kib)
+            dst = rounded["c%d" % a][:, PACK * first_point : PACK * (first_point + points)]
+            src = c_raw[a][:, :, first_point : first_point + points]
+            round_to(engine, dst.rearrange("p (x z i) -> p x i z", z=4, i=PACK), src.rearrange("p i (x z) -> p x i z", z=4))
 
-        pooled1 = {}
+        def round_wc(b, a, u, engine, kib=None):
+            name = "wc%d%d%d" % (b, a, u)
+            rounded[name] = placed([P, 2 * PASS], BF16, name + "_bf", kib)
+            src = wc_raw[b, a].rearrange("p i (m u e) -> p u m i e", u=2, e=2)[:, u]
+            round_to(engine, rounded[name][:].rearrange("p (e m i) -> p m i e", e=2, i=PACK), src)
 
-        def pool_second_half(jt):
-            copy_first(1, jt, neighbour_sum(1, jt, 0, 2 * jt))
-            maximum_second_half(jt)
+        def quantise(name, kib=None):
+            words = rounded[name].shape[1] // PACK
+            codes = placed([P, words], U32, name + "_codes", kib)
+            plane = held([P, words], U8, name + "_plane")
+            nc.vector.quantize_mx(out=codes[:].bitcast(FP8X4), scales=plane[:], in_=rounded[name][:])
+            quantised[name] = (codes, plane)
 
-        def maximum_second_half(jt):
-            if jt % 2 == 0:
-                pooled1[jt // 2] = placed([P, 2 * PASS], F32, "pooled1%d" % (jt // 2), (76, 40)[jt // 2] * KB)
-            best = pooled1[jt // 2][:].rearrange("p (h u j x) -> p j u h x", h=2, u=2, j=2)[:, jt % 2]
-            second_sum(1, jt, 2 * jt + 1, best)
+        def own_passes(b, jt, a, u, g=2, slot=None):
+            opens = g == 2 and a == 0 and u == 0
+            if opens:
+                banks[b, jt, g] = bank_tile(slot)
+            w_code, w_plane = quantised["wc%d%d%d" % (b, a, u)]
+            c_code, c_plane = quantised["c%d" % a]
+            points = slice(JT * jt, JT * (jt + 1))
+            for e in range(2):
+                nc.tensor.matmul_mx(
+                    out=columns_of((b, jt, g), 2 * u + e),
+                    lhsT=w_code[:, P * e : P * (e + 1)].bitcast(FP8X4),
+                    lhsT_scale=w_plane[:, P * e : P * (e + 1)],
+                    rhs=c_code[:, points].bitcast(FP8X4),
+                    rhs_scale=c_plane[:, points],
+                    start=(opens and e == 0),
+                    stop=(a == 1 and u == 1 and e == 1),
+                )
 
-        leading = [neighbour_sum(0, jt, 0, jt) for jt in range(NJT)]
-        copy_first(0, 0, leading[0])
-        c_q = [prepare(c_raw[0][:], "c0", SHARE_C[0], 52 * KB)]
-        for jt in range(1, NJT):
-            copy_first(0, jt, leading[jt], bank_by_pair if jt < 3 else bank_by_slot)
-        pooled0 = []
-        for jt in range(NJT):
-            pooled0.append(placed([P, PASS], F32, "pooled0%d" % jt, (52, 54, 84, 138)[jt] * KB))
-            second_sum(0, jt, NJT + jt, pooled0[jt][:], bank_by_pair if jt < 3 else bank_by_slot)
-        last_raw = [
-            load_rows(
-                placed([P, PACK, HALF], F32, "wc_raw11%d" % h, 4 * h * KB),
-                wc[PASS : 2 * PASS, PASS + HALF * h : PASS + HALF * (h + 1)],
-            )
-            for h in range(2)
-        ]
-        c_q.append(prepare(c_raw[1][:], "c1", SHARE_C[1]))
-        pool_second_half(0)
-        pool_second_half(1)
-        move_rows(wd_planes[:], wd_dense)
-        wd_words = placed([P, 6 * N], U8, "wd_words", 65 * KB + 512)
-        nc.sync.dma_start(wd_words[:, 0 : 4 * N].bitcast(I32), wd8_words[0].rearrange("p n i -> p (n i)").bitcast(I32))
-        nc.sync.dma_start(wd_words[:, 4 * N : 6 * N].bitcast(I32), wd4_words[0].bitcast(I32))
-        res_rows = res.rearrange("(n p) j -> p n j", p=P)
-        res_sb = [placed([P, N // P, 2 * JT], F32, "res_sb%d" % pair, (60 - 32 * pair) * KB + 512 * (1 - pair)) for pair in range(2)]
-        nc.sync.dma_start(res_sb[0][:], res_rows[:, :, 0 : 2 * JT])
-        wc_q = {(0, 0): prepare(wc_raw[0, 0][:], "wc00", SHARE_WC[0])}
-        nc.sync.dma_start(res_sb[1][:], res_rows[:, :, 2 * JT : 4 * JT])
-        copy_first(1, 2, neighbour_sum(1, 2, 0, 4))
+        def add_own(b, jt, target):
+            nc.vector.tensor_tensor(target, by_point((b, jt, 2)), pooled[b, jt][:], ALU.add)
 
-        def own_pass(target, jt, a, quantised, columns, opens, closes):
-            codes, plane = quantised
-            nc.tensor.matmul_mx(
-                out=target,
-                lhsT=c_q[a][0][:, JT * jt : JT * (jt + 1)].bitcast(FP8X4),
-                lhsT_scale=c_q[a][1][:, JT * jt : JT * (jt + 1)],
-                rhs=codes[:, columns].bitcast(FP8X4),
-                rhs_scale=plane[:, columns],
-                start=opens,
-                stop=closes,
-            )
+        def relu(name, src, engine, kib=None):
+            rounded[name] = placed([P, src.shape[1]], BF16, name + "_bf", kib)
+            if engine == "scalar":
+                nc.scalar.activation(rounded[name][:], src, ACT.Relu)
+            else:
+                nc.vector.tensor_scalar_max(rounded[name][:], src, 0.0)
 
-        def relu_out(turned, hidden):
-            nc.scalar.activation(
-                hidden.rearrange("p (j u e) -> p j u e", u=2, e=2),
-                turned.bitcast(BF16).rearrange("p (u j e) -> p j u e", u=2, e=2),
-                ACT.Relu,
-            )
+        def larger_of_both(jt, kib=None):
+            rounded["h1%d" % jt] = placed([P, PASS], BF16, "h1%d_bf" % jt, kib)
+            nc.vector.tensor_tensor(rounded["h1%d" % jt][:], by_point((1, jt, 1)), first[1, jt][:], ALU.max)
 
-        own0 = [bank_tile(jt) for jt in range(2)]
-        for jt in range(2):
-            own_pass(own0[jt][:], jt, 0, wc_q[0, 0], slice(0, PASS), True, False)
-        wc_q[0, 1] = prepare(wc_raw[0, 1][:], "wc01", SHARE_WC[1])
-        maximum_second_half(2)
-        pool_second_half(3)
-        summed0 = {}
-
-        def add_first_half(jt, at):
-            summed0[jt] = placed([P, PASS], BF16, "summed0%d" % jt, at * KB)
-            nc.vector.tensor_tensor(summed0[jt][:], bank_by_pair(own0[jt]), pooled0[jt][:], ALU.add)
-
-        def turn_first_half(tiles, slot):
-            bank = bank_tile(slot)
-            width = JT * len(tiles)
-            for x, jt in enumerate(tiles):
-                for u in range(2):
-                    at = width * u + JT * x
-                    words = summed0[jt][:].bitcast(F32)[:, P * u : P * (u + 1)]
-                    nc.tensor.transpose(bank[:, at : at + JT], words, ident[:])
-            return bank[:, 0 : 2 * width]
-
-        kept = {}
-
-        def keep_own(jt, at):
-            kept[jt] = placed([P, PASS], F32, "kept%d" % jt, at)
-            nc.scalar.activation(kept[jt][:], bank_by_slot(own0[jt]), ACT.Copy)
-
-        def turn_and_add(jt, slot):
-            bank = bank_tile(slot)
-            for x, rows in enumerate((pooled0[jt], kept[jt])):
-                for i in range(PACK):
-                    nc.tensor.matmul(
-                        bank[:, JT * i : JT * (i + 1)], rows[:, P * i : P * (i + 1)], ident[:],
-                        start=(x == 0 and i == 0), stop=(x == 1 and i == PACK - 1), is_transpose=True,
-                    )
-            return bank
-
-        own1 = {}
-        late_q = {}
-        summed1 = {}
-
-        def prepare_late(h, a, at, codes_at=None):
-            raw = wc_raw[1, 0][:, :, HALF * h : HALF * (h + 1)] if a == 0 else last_raw[h][:]
-            late_q[h, a] = prepare(raw, "wc1%d%d" % (a, h), SHARE_LAST[h][a], int(at * KB), codes_at)
-
-        def late_passes(h, a, pair):
-            if a == 0:
-                own1[h, pair] = bank_tile(2 + 2 * h + pair)
-            for x in range(2):
-                target = own1[h, pair][:, HALF * x : HALF * (x + 1)]
-                own_pass(target, 2 * pair + x, a, late_q[h, a], slice(0, HALF), a == 0 and x == 0, a == 1 and x == 1)
-
-        def add_second_half(h, pair, at):
-            if h == 0:
-                summed1[pair] = placed([P, 2 * PASS], BF16, "summed1%d" % pair, int(at * KB))
-            nc.vector.tensor_tensor(
-                summed1[pair][:].rearrange("p (j u h x) -> p h u j x", j=2, u=2, h=2)[:, h],
-                bank_by_pair(own1[h, pair]),
-                pooled1[pair][:, PASS * h : PASS * (h + 1)].rearrange("p (u j x) -> p u j x", u=2, j=2),
-                ALU.add,
-            )
-
-        for jt in range(2):
-            own_pass(own0[jt][:], jt, 1, wc_q[0, 1], slice(0, PASS), False, True)
-        for jt in range(2, NJT):
-            own0.append(bank_tile(NJT + jt))
-            for a in range(2):
-                own_pass(own0[jt][:], jt, a, wc_q[0, a], slice(0, PASS), a == 0, a == 1)
-        add_first_half(0, 70)
-        prepare_late(1, 0, 134)
-        prepare_late(0, 0, 72)
-        for jt in range(1, 3):
-            add_first_half(jt, 133 + jt)
-        for h in range(2):
-            for pair in range(2):
-                late_passes(h, 0, pair)
-        prepare_late(0, 1, 100, 71 * KB + 512)
-        for pair in range(2):
-            late_passes(0, 1, pair)
-        prepare_late(1, 1, 72.5)
-        keep_own(3, 9 * KB // 2)
-        turned0 = turn_first_half((0, 1), 1)
-        turned2 = turn_first_half((2,), 6)
-        for pair in range(2):
-            late_passes(1, 1, pair)
-        hidden0 = [placed([P, 2 * PASS], BF16, "hidden0%d" % pair, (13 * KB // 2, 5 * KB // 2)[pair]) for pair in range(2)]
-        relu_out(turned0, hidden0[0][:])
-        for pair in range(2):
-            add_second_half(0, pair, 99 + 2 * pair)
-        added = turn_and_add(3, 2)
-        relu_out(turned2, hidden0[1][:, 0:PASS])
-        nc.scalar.activation(
-            hidden0[1][:, PASS : 2 * PASS].rearrange("p (j i) -> p j i", i=PACK),
-            added[:].rearrange("p (i j) -> p j i", i=PACK),
-            ACT.Relu,
-        )
-        add_second_half(1, 0, 0)
-        h0_q = [quantise(hidden0[0][:], "h00")]
-        add_second_half(1, 1, 0)
-
-        out_rows = out.rearrange("(n p) j -> p n j", p=P)
-        hidden1 = {}
-        turned1 = {}
         y_bank = {}
 
-        def turn_pair(pair):
-            for jt in range(2 * pair, 2 * pair + 2):
-                turned1[jt] = bank_tile((4, 1, 5, 6)[jt])
-                for u in range(2):
-                    at = P * (2 * (jt % 2) + u)
-                    words = summed1[pair][:].bitcast(F32)[:, at : at + P]
-                    nc.tensor.transpose(turned1[jt][:, P * u : P * (u + 1)], words, ident[:])
-
-        def open_second_layer(pair):
+        def open_second_layer(pair, slots):
+            codes, plane = quantised["h0%d" % pair]
             for nh in range(2):
-                y_bank[pair, nh] = bank_tile((0, 7, 3, 2)[2 * pair + nh])
+                y_bank[pair, nh] = bank_tile(slots[nh])
                 for x in range(2):
                     n = 2 * nh + x
                     nc.tensor.matmul_mx(
                         out=y_bank[pair, nh][:, HALF * x : HALF * (x + 1)],
                         lhsT=wd_words[:, 4 * P * n : 4 * P * (n + 1)].bitcast(FP8X4),
-                        lhsT_scale=wd_planes[:, P * n : P * (n + 1)],
-                        rhs=h0_q[pair][0][:].bitcast(FP8X4),
-                        rhs_scale=h0_q[pair][1][:],
+                        lhsT_scale=scale_of(2, 0, P * n, P),
+                        rhs=codes[:].bitcast(FP8X4),
+                        rhs_scale=plane[:],
                         start=(x == 0),
                         stop=False,
                     )
 
-        def end_first_layer(jt):
-            hidden1[jt] = placed([P, PASS], BF16, "hidden1%d" % jt, (104 + 4 * jt) * KB)
-            if jt % 2 == 1:
-                nc.vector.tensor_scalar_max(
-                    hidden1[jt][:].rearrange("p (j u e) -> p j u e", u=2, e=2),
-                    turned1[jt][:, 0:HALF].bitcast(BF16).rearrange("p (u j e) -> p j u e", u=2, e=2),
-                    0.0,
-                )
-            else:
-                relu_out(turned1[jt][:, 0:HALF], hidden1[jt][:])
-
-        def end_second_layer(pair):
-            h1_q = [quantise(hidden1[jt][:], "h1%d" % jt) for jt in range(2 * pair, 2 * pair + 2)]
+        def close_second_layer(jt):
+            codes, plane = quantised["h1%d" % jt]
             for n in range(N // P):
-                for x in range(2):
-                    at = HALF * (n % 2) + JT * x
-                    nc.tensor.matmul_mx(
-                        out=y_bank[pair, n // 2][:, at : at + JT],
-                        lhsT=wd_words[:, 4 * N + 2 * P * n : 4 * N + 2 * P * (n + 1)].bitcast(FP4X4),
-                        lhsT_scale=wd_planes[:, N + P * n : N + P * (n + 1)],
-                        rhs=h1_q[x][0][:].bitcast(FP8X4),
-                        rhs_scale=h1_q[x][1][:],
-                        start=False,
-                        stop=(n % 2 == 1 and x == 1),
-                    )
+                at = HALF * (n % 2) + JT * (jt % 2)
+                nc.tensor.matmul_mx(
+                    out=y_bank[jt // 2, n // 2][:, at : at + JT],
+                    lhsT=wd_words[:, 4 * N + 2 * P * n : 4 * N + 2 * P * (n + 1)].bitcast(FP4X4),
+                    lhsT_scale=scale_of(2, 1, P * n, P),
+                    rhs=codes[:].bitcast(FP8X4),
+                    rhs_scale=plane[:],
+                    start=False,
+                    stop=(n % 2 == 1 and jt % 2 == 1),
+                )
 
-        def add_residual_and_store(pair, nh):
-            at = (120, 116, 122, 124)[2 * pair + nh] * KB
-            result = placed([P, 2, 2 * JT], F32, "result%d%d" % (pair, nh), at)
+        out_rows = out.rearrange("(n p) j -> p n j", p=P)
+
+        def add_residual_and_store(pair, nh, kib=None):
+            result = placed([P, 2, HALF], F32, "result%d%d" % (pair, nh), kib)
             nc.vector.tensor_tensor(
                 result[:],
                 y_bank[pair, nh][:].rearrange("p (n j) -> p n j", n=2),
                 res_sb[pair][:, 2 * nh : 2 * nh + 2, :],
                 ALU.add,
             )
-            nc.sync.dma_start(out_rows[:, 2 * nh : 2 * nh + 2, 2 * JT * pair : 2 * JT * (pair + 1)], result[:])
+            nc.sync.dma_start(out_rows[:, 2 * nh : 2 * nh + 2, HALF * pair : HALF * (pair + 1)], result[:])
 
-        turn_pair(0)
-        open_second_layer(0)
-        turn_pair(1)
+        gather_words(0, 84)
+        gather_words(1, 85.5)
+        wd_rows = placed([P, N], U8, "wd_rows", 85)
+        for a, scales in enumerate((wd8_scales, wd4_scales)):
+            nc.sync.dma_start(wd_rows[DENSE + a : P : 2, :].bitcast(I32), scales[0].bitcast(I32))
+        c_raw.append(load_rows("c_raw1", c[PASS : 2 * PASS, :], 76.5))
+        wc_raw = {}
+        for b, a, kib in ((0, 0, 42), (0, 1, 50), (1, 0, 58), (1, 1, 24)):
+            wc_raw[b, a] = load_rows("wc_raw%d%d" % (b, a), wc[PASS * a : PASS * (a + 1), PASS * b : PASS * (b + 1)], kib)[:]
+        for u in range(2):
+            order_w(0, u)
+        for jt in range(4):
+            neighbour_sum(0, jt, 0, jt)
+            copy_first(0, jt, kib=96 + 2 * jt)
+        for jt in range(4):
+            neighbour_sum(0, jt, 1, 4 + jt)
+        round_c(0, 0, J, "vector", 86)
+        quantise("c0")
+        for u in range(2):
+            order_w(1, u)
+        for jt in range(4):
+            pool(0, jt, 106 + 2 * jt)
+        planes.append(placed([P, 2 * N], U8, "planes2", 22))
+        nc.vector.memset(planes[2][:].bitcast(I32), 0)
+        move_rows(planes[2], wd_rows)
+        wd_words = placed([P, 6 * N], U8, "wd_words", 73.75)
+        nc.sync.dma_start(wd_words[:, 0 : 4 * N].bitcast(I32), wd8_words[0].rearrange("p n i -> p (n i)").bitcast(I32))
+        nc.sync.dma_start(wd_words[:, 4 * N : 6 * N].bitcast(I32), wd4_words[0].bitcast(I32))
+        res_rows = res.rearrange("(n p) j -> p n j", p=P)
+        res_sb = []
+        for pair in range(2):
+            res_sb.append(placed([P, N // P, HALF], F32, "res_sb%d" % pair, (77, 39)[pair]))
+        for pair in range(2):
+            nc.sync.dma_start(res_sb[pair][:], res_rows[:, :, HALF * pair : HALF * (pair + 1)])
+        for g in range(2):
+            for jt in (0, 2):
+                neighbour_sum(1, jt, g, 2 * g + jt // 2)
+        round_c(1, 0, HALF, "vector", 97)
+        round_c(1, HALF, HALF, "scalar")
+        copy_first(1, 0, kib=81)
+        copy_first(1, 2, kib=83)
+        quantise("c1")
+        pool(1, 0)
+        for g in range(2):
+            neighbour_sum(1, 1, g, (4, 2)[g], False)
+        round_wc(0, 0, 0, "vector", 98)
+        round_wc(0, 0, 1, "scalar", 81)
+        pool(1, 2)
+        for u in range(2):
+            quantise("wc00%d" % u, (None, 44)[u])
+            for jt in range(4):
+                own_passes(0, jt, 0, u, slot=(0, 1, 6, 7)[jt])
+        round_wc(0, 1, 0, "vector", 81)
+        round_wc(0, 1, 1, "scalar", 46)
+        for u in range(2):
+            quantise("wc01%d" % u, (None, 52)[u])
+            for jt in range(4):
+                own_passes(0, jt, 1, u)
+        round_wc(1, 0, 0, "scalar", 116)
+        round_wc(1, 0, 1, "scalar", 92)
+        summed = held([P, 3 * PASS], BF16, "summed0")
+        for jt in range(3):
+            add_own(0, jt, summed[:, PASS * jt : PASS * (jt + 1)])
+        for g in range(2):
+            neighbour_sum(1, 3, g, g, False)
+
+        def plain_passes(a, u):
+            for jt in (0, 2):
+                own_passes(1, jt, a, u, slot=(5, 3)[jt // 2])
+
+        def doubled_passes(a, u):
+            for jt in (1, 3):
+                for g in range(2):
+                    own_passes(1, jt, a, u, g)
+
+        quantise("wc100", 108)
+        plain_passes(0, 0)
+        doubled_passes(0, 0)
+        last = placed([P, PASS], BF16, "summed03", 116)
+        add_own(0, 3, last[:])
+        quantise("wc101", 110)
+        plain_passes(0, 1)
+        doubled_passes(0, 1)
+        relu("h00", summed[:, 0 : 2 * PASS], "vector", 90.5)
+        round_wc(1, 1, 0, "vector", 93)
+        round_wc(1, 1, 1, "scalar")
+        rounded["h01"] = placed([P, 2 * PASS], BF16, "h01_bf", 26)
+        nc.scalar.activation(rounded["h01"][:, 0:PASS], summed[:, 2 * PASS : 3 * PASS], ACT.Relu)
+        nc.scalar.activation(rounded["h01"][:, PASS : 2 * PASS], last[:], ACT.Relu)
+        for u in range(2):
+            quantise("wc11%d" % u, (None, 28)[u])
+            plain_passes(1, u)
+        for jt in (1, 3):
+            for g in range(2):
+                for u in range(2):
+                    own_passes(1, jt, 1, u, g)
+        quantise("h00", 30)
+        open_second_layer(0, (6, 7))
+        late = {jt: held([P, PASS], BF16, "summed1%d" % jt) for jt in (0, 2)}
+        add_own(1, 0, late[0][:])
+        quantise("h01")
+        add_own(1, 2, late[2][:])
+        open_second_layer(1, (5, 3))
+        for pair in range(2):
+            copy_first(1, 2 * pair + 1, ACT.Relu)
+            relu("h1%d" % (2 * pair), late[2 * pair][:], "scalar")
+        larger_of_both(1)
         for jt in range(2):
-            end_first_layer(jt)
-        h0_q.append(quantise(hidden0[1][:], "h01", 40 * KB))
-        end_second_layer(0)
-        open_second_layer(1)
-        for jt in range(2, NJT):
-            end_first_layer(jt)
+            quantise("h1%d" % jt)
+            close_second_layer(jt)
+        larger_of_both(3)
         add_residual_and_store(0, 0)
-        end_second_layer(1)
+        for jt in range(2, 4):
+            quantise("h1%d" % jt)
+            close_second_layer(jt)
         add_residual_and_store(0, 1)
         for nh in range(2):
             add_residual_and_store(1, nh)

@@ -26,6 +26,8 @@ LIST_GROUP = 16
 QUADRANT = 32
 ROWS = 4
 DENSE = P - 32
+WIDTH = {F32: 4, U32: 4, BF16: 2, U8: 1}
+FIXED = 92
 
 
 def tile_list_pnet_mix_res_kernel(
@@ -35,17 +37,24 @@ def tile_list_pnet_mix_res_kernel(
     nc = tc.nc
     with ExitStack() as ctx:
         lists = ctx.enter_context(tc.tile_pool(name="lists", bufs=1))
-        keep = ctx.enter_context(tc.tile_pool(name="keep", bufs=1))
         stage = ctx.enter_context(tc.tile_pool(name="stage", bufs=1))
         psum = ctx.enter_context(tc.psum_pool(name="psum", bufs=1))
 
-        def held(shape, dtype, name):
-            return keep.tile(shape, dtype, name=name, tag=name, align_bytes=64)
+        where = {}
+        free = [FIXED * KB]
 
-        def placed(shape, dtype, name, kib):
-            if kib is None:
-                return held(shape, dtype, name)
-            return stage.tile(shape, dtype, name=name, tag=name, align_bytes=64, offset=int(kib * KB))
+        def placed(shape, dtype, name, on=None):
+            size = WIDTH[dtype]
+            for n in shape[1:]:
+                size *= n
+            if on is None:
+                where[name] = free[0]
+                free[0] += -(-size // 64) * 64
+            elif isinstance(on, tuple):
+                where[name] = where[on[0]] + int(on[1] * KB)
+            else:
+                where[name] = int(on * KB)
+            return stage.tile(shape, dtype, name=name, tag=name, align_bytes=64, offset=where[name])
 
         def bank_tile(slot):
             return psum.tile([P, PASS], F32, name="bank", tag="bank%d" % slot)
@@ -72,7 +81,7 @@ def tile_list_pnet_mix_res_kernel(
         wsc_raw = placed([P, R], U8, "wsc_raw", 72)
         load_dense(wsc_raw, w_scales)
         width = (2 * PASS, 2 * PASS, PASS)
-        rows = [held([P, width[s]], U8, "rows%d" % s) for s in range(2)]
+        rows = [placed([P, width[s]], U8, "rows%d" % s) for s in range(2)]
         tab = placed([P, T], U32, "tab", 48)
         nc.sync.dma_start(tab[:].bitcast(I32), tab_words[0].rearrange("p e f -> p (e f)").bitcast(I32))
         w_flat = w_words.rearrange("a p r i -> p a (r i)")
@@ -85,7 +94,7 @@ def tile_list_pnet_mix_res_kernel(
         load_w(0, None)
         nc.vector.memset(tsc_win[0:DENSE, :].bitcast(I32), 0)
         nc.vector.memset(wsc_raw[0:DENSE, :].bitcast(I32), 0)
-        planes = [held([P, 2 * width[s]], U8, "planes%d" % s) for s in range(2)]
+        planes = [placed([P, 2 * width[s]], U8, "planes%d" % s) for s in range(2)]
         for s in range(2):
             nc.vector.memset(planes[s][:].bitcast(I32), 0)
         tsc_got = placed([P, 2 * J], U8, "tsc_got", 20)
@@ -112,7 +121,7 @@ def tile_list_pnet_mix_res_kernel(
             got = placed([P, J], U32, "t_got%d" % g, kib)
             columns = J // LIST_GROUP
             nc.vector.tensor_copy(got[:], tab[:].indirect(offsets[:, g * columns : (g + 1) * columns]))
-            parted = held([P, 2 * 2 * J], U8, "t_codes%d" % g)
+            parted = placed([P, 2 * 2 * J], U8, "t_codes%d" % g)
             nc.vector.tensor_copy(
                 parted[:].bitcast(U16).rearrange("p (a j) -> p a j", a=2),
                 got[:].bitcast(U16).rearrange("p (j a) -> p a j", a=2),
@@ -121,8 +130,8 @@ def tile_list_pnet_mix_res_kernel(
 
         w_codes = {}
 
-        def order_w(b, u):
-            w_codes[b, u] = held([P, 2, HALF], U32, "w_codes%d%d" % (b, u))
+        def order_w(b, u, kib=None):
+            w_codes[b, u] = placed([P, 2, HALF], U32, "w_codes%d%d" % (b, u), kib)
             nc.scalar.copy(
                 w_codes[b, u][:].rearrange("p a (e m) -> p a m e", e=2),
                 w_raw[b][:].rearrange("p a (m u e) -> p u a m e", u=2, e=2)[:, u],
@@ -133,8 +142,11 @@ def tile_list_pnet_mix_res_kernel(
         def columns_of(key, t):
             return banks[key][:, JT * t : JT * (t + 1)]
 
-        def by_point(key):
-            return banks[key][:].rearrange("p (t j) -> p j t", t=PACK)
+        def in_pairs(view):
+            return view.rearrange("p (t x z) -> p x t z", t=PACK, z=2)
+
+        def woven(view):
+            return view.rearrange("p (x z t) -> p x t z", t=PACK, z=2)
 
         def table_passes(b, jt, g, u, slot, alone=True):
             if u == 0:
@@ -156,16 +168,27 @@ def tile_list_pnet_mix_res_kernel(
             for u in range(2):
                 table_passes(b, jt, g, u, slot, alone)
 
+        def wide_sum(t, g, slot):
+            banks[0, t, g] = bank_tile(slot)
+            for a in range(2):
+                nc.tensor.matmul_mx(
+                    out=banks[0, t, g][:],
+                    lhsT=w_codes[0, t // 2][:, a, P * (t % 2) : P * (t % 2 + 1)].bitcast(FP8X4),
+                    lhsT_scale=scale_of(0, a, PASS + P * t, P),
+                    rhs=t_codes[g][:, 2 * J * a : 2 * J * (a + 1)].bitcast(FP4X4),
+                    rhs_scale=scale_of(g, a, 0, J),
+                    start=(a == 0),
+                    stop=(a == 1),
+                )
+
         first = {}
-        pooled = {}
 
-        def copy_first(b, jt, func=ACT.Copy, kib=None):
-            first[b, jt] = placed([P, PASS], F32, "first%d%d" % (b, jt), kib)
-            nc.scalar.activation(first[b, jt][:], by_point((b, jt, 0)), func)
+        def copy_first(b, k, func=ACT.Copy, kib=None):
+            first[b, k] = placed([P, PASS], F32, "first%d%d" % (b, k), kib)
+            nc.scalar.activation(first[b, k][:], banks[b, k, 0][:], func)
 
-        def pool(b, jt, kib=None):
-            pooled[b, jt] = placed([P, PASS], F32, "pooled%d%d" % (b, jt), kib)
-            nc.vector.tensor_tensor(pooled[b, jt][:], by_point((b, jt, 1)), first[b, jt][:], ALU.max)
+        def pool(b, k, target):
+            nc.vector.tensor_tensor(target, banks[b, k, 1][:], first[b, k][:], ALU.max)
 
         rounded = {}
         quantised = {}
@@ -192,7 +215,7 @@ def tile_list_pnet_mix_res_kernel(
         def quantise(name, kib=None):
             words = rounded[name].shape[1] // PACK
             codes = placed([P, words], U32, name + "_codes", kib)
-            plane = held([P, words], U8, name + "_plane")
+            plane = placed([P, words], U8, name + "_plane")
             nc.vector.quantize_mx(out=codes[:].bitcast(FP8X4), scales=plane[:], in_=rounded[name][:])
             quantised[name] = (codes, plane)
 
@@ -214,8 +237,9 @@ def tile_list_pnet_mix_res_kernel(
                     stop=(a == 1 and u == 1 and e == 1),
                 )
 
-        def add_own(b, jt, target):
-            nc.vector.tensor_tensor(target, by_point((b, jt, 2)), pooled[b, jt][:], ALU.add)
+        def add_own(b, jt, pooled, target):
+            by_pairs = pooled.rearrange("p t (x z) -> p x t z", z=2)
+            nc.vector.tensor_tensor(woven(target), in_pairs(banks[b, jt, 2][:]), by_pairs, ALU.add)
 
         def relu(name, src, engine, kib=None):
             rounded[name] = placed([P, src.shape[1]], BF16, name + "_bf", kib)
@@ -226,7 +250,7 @@ def tile_list_pnet_mix_res_kernel(
 
         def larger_of_both(jt, kib=None):
             rounded["h1%d" % jt] = placed([P, PASS], BF16, "h1%d_bf" % jt, kib)
-            nc.vector.tensor_tensor(rounded["h1%d" % jt][:], by_point((1, jt, 1)), first[1, jt][:], ALU.max)
+            nc.vector.tensor_tensor(woven(rounded["h1%d" % jt][:]), in_pairs(banks[1, jt, 1][:]), in_pairs(first[1, jt][:]), ALU.max)
 
         y_bank = {}
 
@@ -283,19 +307,20 @@ def tile_list_pnet_mix_res_kernel(
             wc_raw[b, a] = load_rows("wc_raw%d%d" % (b, a), wc[PASS * a : PASS * (a + 1), PASS * b : PASS * (b + 1)], kib)[:]
         for u in range(2):
             order_w(0, u)
-        for jt in range(4):
-            neighbour_sum(0, jt, 0, jt)
-            copy_first(0, jt, kib=96 + 2 * jt)
-        for jt in range(4):
-            neighbour_sum(0, jt, 1, 4 + jt)
+        for t in range(PACK):
+            wide_sum(t, 0, t)
+            copy_first(0, t)
+        for t in range(PACK):
+            wide_sum(t, 1, PACK + t)
         round_c(0, 0, J, "vector", 86)
         quantise("c0")
         for u in range(2):
-            order_w(1, u)
-        for jt in range(4):
-            pool(0, jt, 106 + 2 * jt)
-        planes.append(placed([P, 2 * N], U8, "planes2", 22))
-        nc.vector.memset(planes[2][:].bitcast(I32), 0)
+            order_w(1, u, ("c_raw0", 2 * u))
+        pooled0 = placed([P, PACK, J], F32, "pooled0")
+        for t in range(PACK):
+            pool(0, t, pooled0[:, t, :])
+        planes.append(placed([P, 2 * N], U8, "planes2", ("w_raw1", 1)))
+        nc.gpsimd.memset(planes[2][:].bitcast(I32), 0)
         move_rows(planes[2], wd_rows)
         wd_words = placed([P, 6 * N], U8, "wd_words", 73.75)
         nc.sync.dma_start(wd_words[:, 0 : 4 * N].bitcast(I32), wd8_words[0].rearrange("p n i -> p (n i)").bitcast(I32))
@@ -304,37 +329,37 @@ def tile_list_pnet_mix_res_kernel(
         res_sb = []
         for pair in range(2):
             res_sb.append(placed([P, N // P, HALF], F32, "res_sb%d" % pair, (77, 39)[pair]))
-        for pair in range(2):
             nc.sync.dma_start(res_sb[pair][:], res_rows[:, :, HALF * pair : HALF * (pair + 1)])
         for g in range(2):
             for jt in (0, 2):
                 neighbour_sum(1, jt, g, 2 * g + jt // 2)
-        round_c(1, 0, HALF, "vector", 97)
+        round_c(1, 0, HALF, "vector", ("first01", 0))
         round_c(1, HALF, HALF, "scalar")
-        copy_first(1, 0, kib=81)
-        copy_first(1, 2, kib=83)
+        copy_first(1, 0, kib=("c_raw1", 4.5))
+        copy_first(1, 2, kib=("c_raw1", 6.5))
+        pooled1 = {jt: placed([P, PACK, JT], F32, "pooled1%d" % jt) for jt in (0, 2)}
         quantise("c1")
-        pool(1, 0)
+        pool(1, 0, pooled1[0][:])
+        round_wc(0, 0, 0, "vector", ("c1_bf", 0))
         for g in range(2):
             neighbour_sum(1, 1, g, (4, 2)[g], False)
-        round_wc(0, 0, 0, "vector", 98)
-        round_wc(0, 0, 1, "scalar", 81)
-        pool(1, 2)
+        round_wc(0, 0, 1, "scalar", ("first10", 0))
+        pool(1, 2, pooled1[2][:])
         for u in range(2):
-            quantise("wc00%d" % u, (None, 44)[u])
+            quantise("wc00%d" % u, (None, ("wc_raw00", 2))[u])
             for jt in range(4):
                 own_passes(0, jt, 0, u, slot=(0, 1, 6, 7)[jt])
-        round_wc(0, 1, 0, "vector", 81)
-        round_wc(0, 1, 1, "scalar", 46)
+        round_wc(0, 1, 0, "vector", ("wc001_bf", 0))
+        round_wc(0, 1, 1, "scalar", ("wc_raw00", 4))
         for u in range(2):
-            quantise("wc01%d" % u, (None, 52)[u])
+            quantise("wc01%d" % u, (None, ("wc_raw01", 2))[u])
             for jt in range(4):
                 own_passes(0, jt, 1, u)
-        round_wc(1, 0, 0, "scalar", 116)
-        round_wc(1, 0, 1, "scalar", 92)
-        summed = held([P, 3 * PASS], BF16, "summed0")
-        for jt in range(3):
-            add_own(0, jt, summed[:, PASS * jt : PASS * (jt + 1)])
+        round_wc(1, 0, 0, "scalar", ("wc_raw01", 4))
+        round_wc(1, 0, 1, "scalar", ("wc_raw01", 6))
+        summed = [placed([P, 2 * PASS], BF16, "summed0%d" % pair) for pair in range(2)]
+        for jt in range(4):
+            add_own(0, jt, pooled0[:, :, JT * jt : JT * (jt + 1)], summed[jt // 2][:, PASS * (jt % 2) : PASS * (jt % 2 + 1)])
         for g in range(2):
             neighbour_sum(1, 3, g, g, False)
 
@@ -342,38 +367,29 @@ def tile_list_pnet_mix_res_kernel(
             for jt in (0, 2):
                 own_passes(1, jt, a, u, slot=(5, 3)[jt // 2])
 
-        def doubled_passes(a, u):
+        for u in range(2):
+            quantise("wc10%d" % u, (("wc011_codes", 0), ("pooled0", 0))[u])
+            plain_passes(0, u)
             for jt in (1, 3):
                 for g in range(2):
-                    own_passes(1, jt, a, u, g)
-
-        quantise("wc100", 108)
-        plain_passes(0, 0)
-        doubled_passes(0, 0)
-        last = placed([P, PASS], BF16, "summed03", 116)
-        add_own(0, 3, last[:])
-        quantise("wc101", 110)
-        plain_passes(0, 1)
-        doubled_passes(0, 1)
-        relu("h00", summed[:, 0 : 2 * PASS], "vector", 90.5)
-        round_wc(1, 1, 0, "vector", 93)
-        round_wc(1, 1, 1, "scalar")
-        rounded["h01"] = placed([P, 2 * PASS], BF16, "h01_bf", 26)
-        nc.scalar.activation(rounded["h01"][:, 0:PASS], summed[:, 2 * PASS : 3 * PASS], ACT.Relu)
-        nc.scalar.activation(rounded["h01"][:, PASS : 2 * PASS], last[:], ACT.Relu)
+                    own_passes(1, jt, 0, u, g)
+        round_wc(1, 1, 0, "vector", ("wc101_bf", 0))
+        round_wc(1, 1, 1, "scalar", ("wc_raw10", 2))
+        relu("h00", summed[0][:], "vector", ("wc100_bf", 0))
+        relu("h01", summed[1][:], "scalar", ("wc_raw11", 2))
         for u in range(2):
-            quantise("wc11%d" % u, (None, 28)[u])
+            quantise("wc11%d" % u, (None, ("wc_raw11", 4))[u])
             plain_passes(1, u)
         for jt in (1, 3):
             for g in range(2):
                 for u in range(2):
                     own_passes(1, jt, 1, u, g)
-        quantise("h00", 30)
+        quantise("h00", ("wc_raw11", 6))
         open_second_layer(0, (6, 7))
-        late = {jt: held([P, PASS], BF16, "summed1%d" % jt) for jt in (0, 2)}
-        add_own(1, 0, late[0][:])
+        late = {jt: placed([P, PASS], BF16, "summed1%d" % jt) for jt in (0, 2)}
+        add_own(1, 0, pooled1[0][:], late[0][:])
         quantise("h01")
-        add_own(1, 2, late[2][:])
+        add_own(1, 2, pooled1[2][:], late[2][:])
         open_second_layer(1, (5, 3))
         for pair in range(2):
             copy_first(1, 2 * pair + 1, ACT.Relu)

@@ -286,15 +286,20 @@ def tile_list_pnet_mix_res_kernel(
 
         out_rows = out.rearrange("(n p) j -> p n j", p=P)
 
-        def add_residual_and_store(pair, nh, kib=None):
-            result = placed([P, 2, HALF], F32, "result%d%d" % (pair, nh), kib)
+        def store(pair, first_block, blocks, result):
+            rows_out = out_rows[:, first_block : first_block + blocks, HALF * pair : HALF * (pair + 1)]
+            nc.sync.dma_start(rows_out, result)
+
+        def add_residual_and_store(pair, first_block, blocks):
+            result = placed([P, blocks, HALF], F32, "result%d%d" % (pair, first_block))
+            at = HALF * (first_block % 2)
             nc.vector.tensor_tensor(
                 result[:],
-                y_bank[pair, nh][:].rearrange("p (n j) -> p n j", n=2),
-                res_sb[pair][:, 2 * nh : 2 * nh + 2, :],
+                y_bank[pair, first_block // 2][:, at : at + HALF * blocks].rearrange("p (n j) -> p n j", n=blocks),
+                res_sb[pair][:, first_block : first_block + blocks, :],
                 ALU.add,
             )
-            nc.sync.dma_start(out_rows[:, 2 * nh : 2 * nh + 2, HALF * pair : HALF * (pair + 1)], result[:])
+            store(pair, first_block, blocks, result[:])
 
         gather_words(0, 84)
         gather_words(1, 85.5)
@@ -353,7 +358,8 @@ def tile_list_pnet_mix_res_kernel(
         round_wc(0, 1, 1, "scalar", ("wc_raw00", 4))
         for u in range(2):
             quantise("wc01%d" % u, (None, ("wc_raw01", 2))[u])
-            for jt in range(4):
+        for jt in range(4):
+            for u in range(2):
                 own_passes(0, jt, 1, u)
         round_wc(1, 0, 0, "scalar", ("wc_raw01", 4))
         round_wc(1, 0, 1, "scalar", ("wc_raw01", 6))
@@ -373,22 +379,24 @@ def tile_list_pnet_mix_res_kernel(
             for jt in (1, 3):
                 for g in range(2):
                     own_passes(1, jt, 0, u, g)
-        round_wc(1, 1, 0, "vector", ("wc101_bf", 0))
+        round_wc(1, 1, 0, "vector", ("wc100_bf", 0))
         round_wc(1, 1, 1, "scalar", ("wc_raw10", 2))
-        relu("h00", summed[0][:], "vector", ("wc100_bf", 0))
-        relu("h01", summed[1][:], "scalar", ("wc_raw11", 2))
+        relu("h00", summed[0][:], "vector", ("wc101_bf", 0))
         for u in range(2):
             quantise("wc11%d" % u, (None, ("wc_raw11", 4))[u])
-            plain_passes(1, u)
+        for jt in (0, 2):
+            for u in range(2):
+                own_passes(1, jt, 1, u)
         for jt in (1, 3):
             for g in range(2):
                 for u in range(2):
                     own_passes(1, jt, 1, u, g)
+        relu("h01", summed[1][:], "scalar", ("wc_raw11", 2))
         quantise("h00", ("wc_raw11", 6))
         open_second_layer(0, (6, 7))
         late = {jt: placed([P, PASS], BF16, "summed1%d" % jt) for jt in (0, 2)}
         add_own(1, 0, pooled1[0][:], late[0][:])
-        quantise("h01")
+        quantise("h01", ("pooled10", 0))
         add_own(1, 2, pooled1[2][:], late[2][:])
         open_second_layer(1, (5, 3))
         for pair in range(2):
@@ -398,11 +406,13 @@ def tile_list_pnet_mix_res_kernel(
         for jt in range(2):
             quantise("h1%d" % jt)
             close_second_layer(jt)
-        larger_of_both(3)
-        add_residual_and_store(0, 0)
+        larger_of_both(3, ("h10_bf", 0))
+        for n in range(2):
+            add_residual_and_store(0, n, 1)
         for jt in range(2, 4):
             quantise("h1%d" % jt)
             close_second_layer(jt)
-        add_residual_and_store(0, 1)
-        for nh in range(2):
-            add_residual_and_store(1, nh)
+        add_residual_and_store(0, 2, 2)
+        add_residual_and_store(1, 0, 2)
+        for n in range(2, 4):
+            add_residual_and_store(1, n, 1)

@@ -148,25 +148,20 @@ def tile_list_pnet_mix_res_kernel(
         def woven(view):
             return view.rearrange("p (x z t) -> p x t z", t=PACK, z=2)
 
-        def table_passes(b, jt, g, u, slot, alone=True):
-            if u == 0:
-                banks[b, jt, g] = bank_tile(slot)
-            for t in range(2 * u, 2 * u + 2):
+        def tile_sum(jt, g, slot, closed=True):
+            banks[1, jt, g] = bank_tile(slot)
+            for t in range(PACK):
                 for a in range(2):
                     at = J * a + JT * jt
                     nc.tensor.matmul_mx(
-                        out=columns_of((b, jt, g), t),
-                        lhsT=w_codes[b, u][:, a, P * (t % 2) : P * (t % 2 + 1)].bitcast(FP8X4),
-                        lhsT_scale=scale_of(b, a, PASS + P * t, P),
+                        out=columns_of((1, jt, g), t),
+                        lhsT=w_codes[1, t // 2][:, a, P * (t % 2) : P * (t % 2 + 1)].bitcast(FP8X4),
+                        lhsT_scale=scale_of(1, a, PASS + P * t, P),
                         rhs=t_codes[g][:, 2 * at : 2 * (at + JT)].bitcast(FP4X4),
                         rhs_scale=scale_of(g, a, JT * jt, JT),
-                        start=(a == 0 if alone else t == 0 and a == 0),
-                        stop=(alone and a == 1),
+                        start=(a == 0 if closed else t == 0 and a == 0),
+                        stop=(closed and a == 1),
                     )
-
-        def neighbour_sum(b, jt, g, slot, alone=True):
-            for u in range(2):
-                table_passes(b, jt, g, u, slot, alone)
 
         def wide_sum(t, g, slot):
             banks[0, t, g] = bank_tile(slot)
@@ -204,7 +199,11 @@ def tile_list_pnet_mix_res_kernel(
                 rounded["c%d" % a] = placed([P, PACK * J], BF16, "c%d_bf" % a, kib)
             dst = rounded["c%d" % a][:, PACK * first_point : PACK * (first_point + points)]
             src = c_raw[a][:, :, first_point : first_point + points]
-            round_to(engine, dst.rearrange("p (x z i) -> p x i z", z=4, i=PACK), src.rearrange("p i (x z) -> p x i z", z=4))
+            round_to(
+                engine,
+                dst.rearrange("p (x z i) -> p x i z", z=4, i=PACK),
+                src.rearrange("p i (x z) -> p x i z", z=4),
+            )
 
         def round_wc(b, a, u, engine, kib=None):
             name = "wc%d%d%d" % (b, a, u)
@@ -250,7 +249,9 @@ def tile_list_pnet_mix_res_kernel(
 
         def larger_of_both(jt, kib=None):
             rounded["h1%d" % jt] = placed([P, PASS], BF16, "h1%d_bf" % jt, kib)
-            nc.vector.tensor_tensor(woven(rounded["h1%d" % jt][:]), in_pairs(banks[1, jt, 1][:]), in_pairs(first[1, jt][:]), ALU.max)
+            nc.vector.tensor_tensor(
+                woven(rounded["h1%d" % jt][:]), in_pairs(banks[1, jt, 1][:]), in_pairs(first[1, jt][:]), ALU.max
+            )
 
         y_bank = {}
 
@@ -286,10 +287,6 @@ def tile_list_pnet_mix_res_kernel(
 
         out_rows = out.rearrange("(n p) j -> p n j", p=P)
 
-        def store(pair, first_block, blocks, result):
-            rows_out = out_rows[:, first_block : first_block + blocks, HALF * pair : HALF * (pair + 1)]
-            nc.sync.dma_start(rows_out, result)
-
         def add_residual_and_store(pair, first_block, blocks):
             result = placed([P, blocks, HALF], F32, "result%d%d" % (pair, first_block))
             at = HALF * (first_block % 2)
@@ -299,7 +296,8 @@ def tile_list_pnet_mix_res_kernel(
                 res_sb[pair][:, first_block : first_block + blocks, :],
                 ALU.add,
             )
-            store(pair, first_block, blocks, result[:])
+            rows_out = out_rows[:, first_block : first_block + blocks, HALF * pair : HALF * (pair + 1)]
+            nc.sync.dma_start(rows_out, result[:])
 
         gather_words(0, 84)
         gather_words(1, 85.5)
@@ -309,7 +307,9 @@ def tile_list_pnet_mix_res_kernel(
         c_raw.append(load_rows("c_raw1", c[PASS : 2 * PASS, :], 76.5))
         wc_raw = {}
         for b, a, kib in ((0, 0, 42), (0, 1, 50), (1, 0, 58), (1, 1, 24)):
-            wc_raw[b, a] = load_rows("wc_raw%d%d" % (b, a), wc[PASS * a : PASS * (a + 1), PASS * b : PASS * (b + 1)], kib)[:]
+            piece = wc[PASS * a : PASS * (a + 1), PASS * b : PASS * (b + 1)]
+            wc_raw[b, a] = load_rows("wc_raw%d%d" % (b, a), piece, kib)[:]
+
         for u in range(2):
             order_w(0, u)
         for t in range(PACK):
@@ -324,40 +324,45 @@ def tile_list_pnet_mix_res_kernel(
         pooled0 = placed([P, PACK, J], F32, "pooled0")
         for t in range(PACK):
             pool(0, t, pooled0[:, t, :])
-        planes.append(placed([P, 2 * N], U8, "planes2", ("w_raw1", 1)))
+
+        planes.append(placed([P, 2 * N], U8, "planes2", ("first01", 0)))
         nc.gpsimd.memset(planes[2][:].bitcast(I32), 0)
         move_rows(planes[2], wd_rows)
         wd_words = placed([P, 6 * N], U8, "wd_words", 73.75)
         nc.sync.dma_start(wd_words[:, 0 : 4 * N].bitcast(I32), wd8_words[0].rearrange("p n i -> p (n i)").bitcast(I32))
         nc.sync.dma_start(wd_words[:, 4 * N : 6 * N].bitcast(I32), wd4_words[0].bitcast(I32))
-        res_rows = res.rearrange("(n p) j -> p n j", p=P)
-        res_sb = []
-        for pair in range(2):
-            res_sb.append(placed([P, N // P, HALF], F32, "res_sb%d" % pair, (77, 39)[pair]))
-            nc.sync.dma_start(res_sb[pair][:], res_rows[:, :, HALF * pair : HALF * (pair + 1)])
+
         for g in range(2):
             for jt in (0, 2):
-                neighbour_sum(1, jt, g, 2 * g + jt // 2)
-        round_c(1, 0, HALF, "vector", ("first01", 0))
+                tile_sum(jt, g, 2 * g + jt // 2)
+        round_c(1, 0, HALF, "scalar", 20)
         round_c(1, HALF, HALF, "scalar")
         copy_first(1, 0, kib=("c_raw1", 4.5))
         copy_first(1, 2, kib=("c_raw1", 6.5))
-        pooled1 = {jt: placed([P, PACK, JT], F32, "pooled1%d" % jt) for jt in (0, 2)}
-        quantise("c1")
-        pool(1, 0, pooled1[0][:])
-        round_wc(0, 0, 0, "vector", ("c1_bf", 0))
-        for g in range(2):
-            neighbour_sum(1, 1, g, (4, 2)[g], False)
-        round_wc(0, 0, 1, "scalar", ("first10", 0))
-        pool(1, 2, pooled1[2][:])
         for u in range(2):
-            quantise("wc00%d" % u, (None, ("wc_raw00", 2))[u])
+            round_wc(0, 0, u, "vector", ("first0%d" % (2 + u), 0))
+        quantise("wc000")
+        quantise("c1", ("wc_raw00", 2))
+        quantise("wc001", ("wc_raw00", 4))
+        res_rows = res.rearrange("(n p) j -> p n j", p=P)
+        res_sb = []
+        for pair in range(2):
+            res_sb.append(placed([P, N // P, HALF], F32, "res_sb%d" % pair, (39, ("c1_bf", 0))[pair]))
+            nc.sync.dma_start(res_sb[pair][:], res_rows[:, :, HALF * pair : HALF * (pair + 1)])
+        for g in range(2):
+            tile_sum(1, g, 4 + g, closed=False)
+        for u in range(2):
             for jt in range(4):
-                own_passes(0, jt, 0, u, slot=(0, 1, 6, 7)[jt])
-        round_wc(0, 1, 0, "vector", ("wc001_bf", 0))
-        round_wc(0, 1, 1, "scalar", ("wc_raw00", 4))
+                own_passes(0, jt, 0, u, slot=(6, 7, 0, 1)[jt])
+
+        round_wc(0, 1, 0, "vector", ("wc000_bf", 0))
+        round_wc(0, 1, 1, "scalar", ("c_raw1", 0.5))
+        pooled1 = {0: placed([P, PACK, JT], F32, "pooled10", ("wc001_bf", 0))}
+        pool(1, 0, pooled1[0][:])
         for u in range(2):
             quantise("wc01%d" % u, (None, ("wc_raw01", 2))[u])
+        pooled1[2] = placed([P, PACK, JT], F32, "pooled12", ("wc011_bf", 0))
+        pool(1, 2, pooled1[2][:])
         for jt in range(4):
             for u in range(2):
                 own_passes(0, jt, 1, u)
@@ -365,20 +370,19 @@ def tile_list_pnet_mix_res_kernel(
         round_wc(1, 0, 1, "scalar", ("wc_raw01", 6))
         summed = [placed([P, 2 * PASS], BF16, "summed0%d" % pair) for pair in range(2)]
         for jt in range(4):
-            add_own(0, jt, pooled0[:, :, JT * jt : JT * (jt + 1)], summed[jt // 2][:, PASS * (jt % 2) : PASS * (jt % 2 + 1)])
+            target = summed[jt // 2][:, PASS * (jt % 2) : PASS * (jt % 2 + 1)]
+            add_own(0, jt, pooled0[:, :, JT * jt : JT * (jt + 1)], target)
+
         for g in range(2):
-            neighbour_sum(1, 3, g, g, False)
-
-        def plain_passes(a, u):
-            for jt in (0, 2):
-                own_passes(1, jt, a, u, slot=(5, 3)[jt // 2])
-
+            tile_sum(3, g, 6 + g, closed=False)
         for u in range(2):
             quantise("wc10%d" % u, (("wc011_codes", 0), ("pooled0", 0))[u])
-            plain_passes(0, u)
+            for jt in (0, 2):
+                own_passes(1, jt, 0, u, slot=2 + jt // 2)
             for jt in (1, 3):
                 for g in range(2):
                     own_passes(1, jt, 0, u, g)
+
         round_wc(1, 1, 0, "vector", ("wc100_bf", 0))
         round_wc(1, 1, 1, "scalar", ("wc_raw10", 2))
         relu("h00", summed[0][:], "vector", ("wc101_bf", 0))
@@ -393,15 +397,16 @@ def tile_list_pnet_mix_res_kernel(
                     own_passes(1, jt, 1, u, g)
         relu("h01", summed[1][:], "scalar", ("wc_raw11", 2))
         quantise("h00", ("wc_raw11", 6))
-        open_second_layer(0, (6, 7))
+        open_second_layer(0, (0, 1))
         late = {jt: placed([P, PASS], BF16, "summed1%d" % jt) for jt in (0, 2)}
         add_own(1, 0, pooled1[0][:], late[0][:])
         quantise("h01", ("pooled10", 0))
         add_own(1, 2, pooled1[2][:], late[2][:])
-        open_second_layer(1, (5, 3))
+        open_second_layer(1, (2, 3))
         for pair in range(2):
             copy_first(1, 2 * pair + 1, ACT.Relu)
             relu("h1%d" % (2 * pair), late[2 * pair][:], "scalar")
+
         larger_of_both(1)
         for jt in range(2):
             quantise("h1%d" % jt)

from contextlib import ExitStack

import concourse.mybir as mybir

K, R, N, T, J = 1024, 1024, 512, 4096, 512
FLOPS = 2 * K * R * 3 * J + 2 * R * N * J

F32 = mybir.dt.float32
BF16 = mybir.dt.bfloat16
I32 = mybir.dt.int32
U32 = mybir.dt.uint32
U16 = mybir.dt.uint16
U8 = mybir.dt.uint8
FP8X4 = mybir.dt.float8_e4m3fn_x4
FP4X4 = mybir.dt.float4_e2m1fn_x4
ALU = mybir.AluOpType
ACT = mybir.ActivationFunctionType

KB = 1024
P = 128
PACK = 4
PASS = P * PACK
HALF = PASS // 2
JT = 128
LIST_GROUP = 16
QUADRANT = 32
ROWS = 4
DENSE = P - 32
WIDTH = {F32: 4, U32: 4, BF16: 2, U8: 1}
FIXED = 92


def tile_list_pnet_mix_res_kernel(
    tc, tab_words, tab_scales, c, w_words, w_scales, wc, wd8_words, wd8_scales,
    wd4_words, wd4_scales, res, offs, out,
):
    nc = tc.nc
    with ExitStack() as ctx:
        lists = ctx.enter_context(tc.tile_pool(name="lists", bufs=1))
        stage = ctx.enter_context(tc.tile_pool(name="stage", bufs=1))
        psum = ctx.enter_context(tc.psum_pool(name="psum", bufs=1))

        where = {}
        free = [FIXED * KB]

        def placed(shape, dtype, name, on=None):
            size = WIDTH[dtype]
            for n in shape[1:]:
                size *= n
            if on is None:
                where[name] = free[0]
                free[0] += -(-size // 64) * 64
            elif isinstance(on, tuple):
                where[name] = where[on[0]] + int(on[1] * KB)
            else:
                where[name] = int(on * KB)
            return stage.tile(shape, dtype, name=name, tag=name, align_bytes=64, offset=where[name])

        def bank_tile(slot):
            return psum.tile([P, PASS], F32, name="bank", tag="bank%d" % slot)

        def move_rows(planes, rows):
            for quad in (0, 2, 1, 3):
                nc.sync.dma_start(
                    planes[QUADRANT * quad : QUADRANT * quad + ROWS, :].bitcast(I32),
                    rows[DENSE + 2 * ROWS * quad : DENSE + 2 * ROWS * (quad + 1), :].bitcast(I32),
                )

        def load_rows(name, rows, kib):
            raw = placed([P, PACK, rows.shape[1]], F32, name, kib)
            nc.sync.dma_start(raw[:], rows.rearrange("(p i) x -> p i x", i=PACK))
            return raw

        def load_dense(target, scales):
            nc.sync.dma_start(target[DENSE:P, :].bitcast(I32), scales.rearrange("a q e -> q a e").bitcast(I32))

        offsets = lists.tile([P, 2 * J // LIST_GROUP], U16, name="offsets")
        nc.sync.dma_start(offsets[:], offs)
        tsc_win = placed([P, T], U8, "tsc_win", 68)
        load_dense(tsc_win, tab_scales)
        wsc_raw = placed([P, R], U8, "wsc_raw", 72)
        load_dense(wsc_raw, w_scales)
        width = (2 * PASS, 2 * PASS, PASS)
        rows = [placed([P, width[s]], U8, "rows%d" % s) for s in range(2)]
        tab = placed([P, T], U32, "tab", 48)
        nc.sync.dma_start(tab[:].bitcast(I32), tab_words[0].rearrange("p e f -> p (e f)").bitcast(I32))
        w_flat = w_words.rearrange("a p r i -> p a (r i)")
        w_raw = {}

        def load_w(b, kib):
            w_raw[b] = placed([P, 2, PASS], U32, "w_raw%d" % b, kib)
            nc.sync.dma_start(w_raw[b][:].bitcast(I32), w_flat[:, :, 4 * PASS * b : 4 * PASS * (b + 1)].bitcast(I32))

        load_w(0, None)
        nc.vector.memset(tsc_win[0:DENSE, :].bitcast(I32), 0)
        nc.vector.memset(wsc_raw[0:DENSE, :].bitcast(I32), 0)
        planes = [placed([P, 2 * width[s]], U8, "planes%d" % s) for s in range(2)]
        for s in range(2):
            nc.vector.memset(planes[s][:].bitcast(I32), 0)
        tsc_got = placed([P, 2 * J], U8, "tsc_got", 20)
        nc.vector.tensor_copy(tsc_got[:], tsc_win[:].indirect(offsets[:]))
        for b in range(2):
            nc.vector.tensor_copy(
                rows[b][:, PASS : 2 * PASS].rearrange("p (t m) -> p t m", t=PACK),
                wsc_raw[:, PASS * b : PASS * (b + 1)].rearrange("p (m t) -> p t m", t=PACK),
            )
        for g in range(2):
            nc.vector.tensor_copy(rows[g][:, 0:J].bitcast(I32), tsc_got[:, J * g : J * (g + 1)].bitcast(I32))
        move_rows(planes[0], rows[0])
        c_raw = [load_rows("c_raw0", c[0:PASS, :], 12.5)]
        move_rows(planes[1], rows[1])
        load_w(1, 20.5)

        def scale_of(s, a, first, count):
            at = width[s] * a + first
            return planes[s][:, at : at + count]

        t_codes = []

        def gather_words(g, kib):
            got = placed([P, J], U32, "t_got%d" % g, kib)
            columns = J // LIST_GROUP
            nc.vector.tensor_copy(got[:], tab[:].indirect(offsets[:, g * columns : (g + 1) * columns]))
            parted = placed([P, 2 * 2 * J], U8, "t_codes%d" % g)
            nc.vector.tensor_copy(
                parted[:].bitcast(U16).rearrange("p (a j) -> p a j", a=2),
                got[:].bitcast(U16).rearrange("p (j a) -> p a j", a=2),
            )
            t_codes.append(parted)

        w_codes = {}

        def order_w(b, u, kib=None):
            w_codes[b, u] = placed([P, 2, HALF], U32, "w_codes%d%d" % (b, u), kib)
            nc.scalar.copy(
                w_codes[b, u][:].rearrange("p a (e m) -> p a m e", e=2),
                w_raw[b][:].rearrange("p a (m u e) -> p u a m e", u=2, e=2)[:, u],
            )

        banks = {}

        def columns_of(key, t):
            return banks[key][:, JT * t : JT * (t + 1)]

        def in_pairs(view):
            return view.rearrange("p (t x z) -> p x t z", t=PACK, z=2)

        def woven(view):
            return view.rearrange("p (x z t) -> p x t z", t=PACK, z=2)

        def tile_sum(jt, g, slot, closed=True):
            banks[1, jt, g] = bank_tile(slot)
            for t in range(PACK):
                for a in range(2):
                    at = J * a + JT * jt
                    nc.tensor.matmul_mx(
                        out=columns_of((1, jt, g), t),
                        lhsT=w_codes[1, t // 2][:, a, P * (t % 2) : P * (t % 2 + 1)].bitcast(FP8X4),
                        lhsT_scale=scale_of(1, a, PASS + P * t, P),
                        rhs=t_codes[g][:, 2 * at : 2 * (at + JT)].bitcast(FP4X4),
                        rhs_scale=scale_of(g, a, JT * jt, JT),
                        start=(a == 0 if closed else t == 0 and a == 0),
                        stop=(closed and a == 1),
                    )

        def wide_sum(t, g, slot):
            banks[0, t, g] = bank_tile(slot)
            for a in range(2):
                nc.tensor.matmul_mx(
                    out=banks[0, t, g][:],
                    lhsT=w_codes[0, t // 2][:, a, P * (t % 2) : P * (t % 2 + 1)].bitcast(FP8X4),
                    lhsT_scale=scale_of(0, a, PASS + P * t, P),
                    rhs=t_codes[g][:, 2 * J * a : 2 * J * (a + 1)].bitcast(FP4X4),
                    rhs_scale=scale_of(g, a, 0, J),
                    start=(a == 0),
                    stop=(a == 1),
                )

        first = {}

        def copy_first(b, k, func=ACT.Copy, kib=None):
            first[b, k] = placed([P, PASS], F32, "first%d%d" % (b, k), kib)
            nc.scalar.activation(first[b, k][:], banks[b, k, 0][:], func)

        def pool(b, k, target):
            nc.vector.tensor_tensor(target, banks[b, k, 1][:], first[b, k][:], ALU.max)

        rounded = {}
        quantised = {}

        def round_to(engine, dst, src):
            if engine == "scalar":
                nc.scalar.activation(dst, src, ACT.Copy)
            else:
                nc.vector.tensor_copy(dst, src)

        def round_c(a, first_point, points, engine, kib=None):
            if first_point == 0:
                rounded["c%d" % a] = placed([P, PACK * J], BF16, "c%d_bf" % a, kib)
            dst = rounded["c%d" % a][:, PACK * first_point : PACK * (first_point + points)]
            src = c_raw[a][:, :, first_point : first_point + points]
            round_to(
                engine,
                dst.rearrange("p (x z i) -> p x i z", z=4, i=PACK),
                src.rearrange("p i (x z) -> p x i z", z=4),
            )

        def round_wc(b, a, u, engine, kib=None):
            name = "wc%d%d%d" % (b, a, u)
            rounded[name] = placed([P, 2 * PASS], BF16, name + "_bf", kib)
            src = wc_raw[b, a].rearrange("p i (m u e) -> p u m i e", u=2, e=2)[:, u]
            round_to(engine, rounded[name][:].rearrange("p (e m i) -> p m i e", e=2, i=PACK), src)

        def quantise(name, kib=None):
            words = rounded[name].shape[1] // PACK
            codes = placed([P, words], U32, name + "_codes", kib)
            plane = placed([P, words], U8, name + "_plane")
            nc.vector.quantize_mx(out=codes[:].bitcast(FP8X4), scales=plane[:], in_=rounded[name][:])
            quantised[name] = (codes, plane)

        def own_passes(b, jt, a, u, g=2, slot=None):
            opens = g == 2 and a == 0 and u == 0
            if opens:
                banks[b, jt, g] = bank_tile(slot)
            w_code, w_plane = quantised["wc%d%d%d" % (b, a, u)]
            c_code, c_plane = quantised["c%d" % a]
            points = slice(JT * jt, JT * (jt + 1))
            for e in range(2):
                nc.tensor.matmul_mx(
                    out=columns_of((b, jt, g), 2 * u + e),
                    lhsT=w_code[:, P * e : P * (e + 1)].bitcast(FP8X4),
                    lhsT_scale=w_plane[:, P * e : P * (e + 1)],
                    rhs=c_code[:, points].bitcast(FP8X4),
                    rhs_scale=c_plane[:, points],
                    start=(opens and e == 0),
                    stop=(a == 1 and u == 1 and e == 1),
                )

        def add_own(b, jt, pooled, target):
            by_pairs = pooled.rearrange("p t (x z) -> p x t z", z=2)
            nc.vector.tensor_tensor(woven(target), in_pairs(banks[b, jt, 2][:]), by_pairs, ALU.add)

        def relu(name, src, engine, kib=None):
            rounded[name] = placed([P, src.shape[1]], BF16, name + "_bf", kib)
            if engine == "scalar":
                nc.scalar.activation(rounded[name][:], src, ACT.Relu)
            else:
                nc.vector.tensor_scalar_max(rounded[name][:], src, 0.0)

        def larger_of_both(jt, kib=None):
            rounded["h1%d" % jt] = placed([P, PASS], BF16, "h1%d_bf" % jt, kib)
            nc.vector.tensor_tensor(
                woven(rounded["h1%d" % jt][:]), in_pairs(banks[1, jt, 1][:]), in_pairs(first[1, jt][:]), ALU.max
            )

        y_bank = {}

        def open_second_layer(pair, slots):
            codes, plane = quantised["h0%d" % pair]
            for nh in range(2):
                y_bank[pair, nh] = bank_tile(slots[nh])
                for x in range(2):
                    n = 2 * nh + x
                    nc.tensor.matmul_mx(
                        out=y_bank[pair, nh][:, HALF * x : HALF * (x + 1)],
                        lhsT=wd_words[:, 4 * P * n : 4 * P * (n + 1)].bitcast(FP8X4),
                        lhsT_scale=scale_of(2, 0, P * n, P),
                        rhs=codes[:].bitcast(FP8X4),
                        rhs_scale=plane[:],
                        start=(x == 0),
                        stop=False,
                    )

        def close_second_layer(jt):
            codes, plane = quantised["h1%d" % jt]
            for n in range(N // P):
                at = HALF * (n % 2) + JT * (jt % 2)
                nc.tensor.matmul_mx(
                    out=y_bank[jt // 2, n // 2][:, at : at + JT],
                    lhsT=wd_words[:, 4 * N + 2 * P * n : 4 * N + 2 * P * (n + 1)].bitcast(FP4X4),
                    lhsT_scale=scale_of(2, 1, P * n, P),
                    rhs=codes[:].bitcast(FP8X4),
                    rhs_scale=plane[:],
                    start=False,
                    stop=(n % 2 == 1 and jt % 2 == 1),
                )

        out_rows = out.rearrange("(n p) j -> p n j", p=P)

        def add_residual_and_store(pair, first_block, blocks):
            result = placed([P, blocks, HALF], F32, "result%d%d" % (pair, first_block))
            at = HALF * (first_block % 2)
            nc.vector.tensor_tensor(
                result[:],
                y_bank[pair, first_block // 2][:, at : at + HALF * blocks].rearrange("p (n j) -> p n j", n=blocks),
                res_sb[pair][:, first_block : first_block + blocks, :],
                ALU.add,
            )
            rows_out = out_rows[:, first_block : first_block + blocks, HALF * pair : HALF * (pair + 1)]
            nc.sync.dma_start(rows_out, result[:])

        gather_words(0, 84)
        gather_words(1, 85.5)
        wd_rows = placed([P, N], U8, "wd_rows", 85)
        for a, scales in enumerate((wd8_scales, wd4_scales)):
            nc.sync.dma_start(wd_rows[DENSE + a : P : 2, :].bitcast(I32), scales[0].bitcast(I32))
        c_raw.append(load_rows("c_raw1", c[PASS : 2 * PASS, :], 76.5))
        wc_raw = {}
        for b, a, kib in ((0, 0, 42), (0, 1, 50), (1, 0, 58), (1, 1, 24)):
            piece = wc[PASS * a : PASS * (a + 1), PASS * b : PASS * (b + 1)]
            wc_raw[b, a] = load_rows("wc_raw%d%d" % (b, a), piece, kib)[:]

        for u in range(2):
            order_w(0, u)
        for t in range(PACK):
            wide_sum(t, 0, t)
            copy_first(0, t)
        for t in range(PACK):
            wide_sum(t, 1, PACK + t)
        round_c(0, 0, J, "vector", 86)
        quantise("c0")
        for u in range(2):
            order_w(1, u, ("c_raw0", 2 * u))
        pooled0 = placed([P, PACK, J], F32, "pooled0")
        for t in range(PACK):
            pool(0, t, pooled0[:, t, :])

        planes.append(placed([P, 2 * N], U8, "planes2", ("first01", 0)))
        nc.gpsimd.memset(planes[2][:].bitcast(I32), 0)
        move_rows(planes[2], wd_rows)
        wd_words = placed([P, 6 * N], U8, "wd_words", 73.75)
        nc.sync.dma_start(wd_words[:, 0 : 4 * N].bitcast(I32), wd8_words[0].rearrange("p n i -> p (n i)").bitcast(I32))
        nc.sync.dma_start(wd_words[:, 4 * N : 6 * N].bitcast(I32), wd4_words[0].bitcast(I32))

        for g in range(2):
            for jt in (0, 2):
                tile_sum(jt, g, 2 * g + jt // 2)
        round_c(1, 0, HALF, "scalar", 20)
        round_c(1, HALF, HALF, "scalar")
        copy_first(1, 0, kib=("c_raw1", 4.5))
        copy_first(1, 2, kib=("c_raw1", 6.5))
        for u in range(2):
            round_wc(0, 0, u, "vector", ("first0%d" % (2 + u), 0))
        quantise("wc000")
        quantise("c1", ("wc_raw00", 2))
        quantise("wc001", ("wc_raw00", 4))
        res_rows = res.rearrange("(n p) j -> p n j", p=P)
        res_sb = []
        for pair in range(2):
            res_sb.append(placed([P, N // P, HALF], F32, "res_sb%d" % pair, (39, ("c1_bf", 0))[pair]))
            nc.sync.dma_start(res_sb[pair][:], res_rows[:, :, HALF * pair : HALF * (pair + 1)])
        for g in range(2):
            tile_sum(1, g, 4 + g, closed=False)
        for u in range(2):
            for jt in range(4):
                own_passes(0, jt, 0, u, slot=(6, 7, 0, 1)[jt])

        round_wc(0, 1, 0, "vector", ("wc000_bf", 0))
        round_wc(0, 1, 1, "scalar", ("c_raw1", 0.5))
        pooled1 = {0: placed([P, PACK, JT], F32, "pooled10", ("wc001_bf", 0))}
        pool(1, 0, pooled1[0][:])
        for u in range(2):
            quantise("wc01%d" % u, (None, ("wc_raw01", 2))[u])
        pooled1[2] = placed([P, PACK, JT], F32, "pooled12", ("wc011_bf", 0))
        pool(1, 2, pooled1[2][:])
        for jt in range(4):
            for u in range(2):
                own_passes(0, jt, 1, u)
        round_wc(1, 0, 0, "scalar", ("wc_raw01", 4))
        round_wc(1, 0, 1, "scalar", ("wc_raw01", 6))
        summed = [placed([P, 2 * PASS], BF16, "summed0%d" % pair) for pair in range(2)]
        for jt in range(4):
            target = summed[jt // 2][:, PASS * (jt % 2) : PASS * (jt % 2 + 1)]
            add_own(0, jt, pooled0[:, :, JT * jt : JT * (jt + 1)], target)

        for g in range(2):
            tile_sum(3, g, 6 + g, closed=False)
        for u in range(2):
            quantise("wc10%d" % u, (("wc011_codes", 0), ("pooled0", 0))[u])
            for jt in (0, 2):
                own_passes(1, jt, 0, u, slot=2 + jt // 2)
            for jt in (1, 3):
                for g in range(2):
                    own_passes(1, jt, 0, u, g)

        round_wc(1, 1, 0, "vector", ("wc100_bf", 0))
        round_wc(1, 1, 1, "scalar", ("wc_raw10", 2))
        relu("h00", summed[0][:], "vector", ("wc101_bf", 0))
        for u in range(2):
            quantise("wc11%d" % u, (None, ("wc_raw11", 4))[u])
        for jt in (0, 2):
            for u in range(2):
                own_passes(1, jt, 1, u)
        for jt in (1, 3):
            for g in range(2):
                for u in range(2):
                    own_passes(1, jt, 1, u, g)
        relu("h01", summed[1][:], "scalar", ("wc_raw11", 2))
        quantise("h00", ("wc_raw11", 6))
        open_second_layer(0, (0, 1))
        late = {jt: placed([P, PASS], BF16, "summed1%d" % jt) for jt in (0, 2)}
        add_own(1, 0, pooled1[0][:], late[0][:])
        quantise("h01", ("pooled10", 0))
        add_own(1, 2, pooled1[2][:], late[2][:])
        open_second_layer(1, (2, 3))
        for pair in range(2):
            copy_first(1, 2 * pair + 1, ACT.Relu)
            relu("h1%d" % (2 * pair), late[2 * pair][:], "scalar")

        larger_of_both(1)
        for jt in range(2):
            quantise("h1%d" % jt)
            close_second_layer(jt)
        larger_of_both(3, ("h10_bf", 0))
        for n in range(2):
            add_residual_and_store(0, n, 1)
        for jt in range(2, 4):
            quantise("h1%d" % jt)
            close_second_layer(jt)
        add_residual_and_store(0, 2, 2)
        add_residual_and_store(1, 0, 2)
        for n in range(2, 4):
            add_residual_and_store(1, n, 1)
